import numpy as np
import ml_dtypes


def mxq(x, axis, fmt="e4m3"):
    dtype, down = {"e4m3": (ml_dtypes.float8_e4m3fn, 7), "e5m2": (ml_dtypes.float8_e5m2, 14)}[fmt]
    v = np.moveaxis(np.asarray(x, np.float32).astype(ml_dtypes.bfloat16).astype(np.float64), axis, -1)
    blocks = v.reshape(v.shape[:-1] + (-1, 32))
    amax = np.abs(blocks).max(-1, keepdims=True)
    byte = np.maximum(np.where(amax > 0, np.frexp(amax)[1] - 1 + 127, 0) - down, 1)
    scale = np.exp2(byte - 127.0)
    codes = (blocks / scale).astype(np.float32).astype(dtype).astype(np.float64)
    return np.moveaxis((codes * scale).reshape(v.shape), -1, axis)


WIDE = False


def mx_kscale(k):
    if not WIDE:
        return np.ones(k)
    levels = np.array([10, -10, 5, -5, 0])
    if k % 512:
        return np.exp2(np.random.permutation(np.resize(levels, k // 32))).repeat(32)
    a = np.empty((k // 512, 16))
    for p in range(k // 512):
        a[p, :8] = np.random.permutation(np.resize(levels, 8))
        for g in range(8):
            far = levels[np.abs(levels - a[p, g]) >= 10]
            a[p, g + 8] = far[np.random.randint(len(far))]
    return np.exp2(a.ravel()).repeat(32)


BF16 = ml_dtypes.bfloat16


def bf(x):
    return np.asarray(x, np.float32).astype(BF16)


def f64(x):
    return np.asarray(x).astype(np.float64)


E2M1 = np.array([0.0, 0.5, 1.0, 1.5, 2.0, 3.0, 4.0, 6.0, -0.0, -0.5, -1.0, -1.5, -2.0, -3.0, -4.0, -6.0])


def pack_weight(w, fmt):
    k, n = w.shape
    w = f64(bf(w)).reshape(k // 32, 32, n)
    amax = np.abs(w).max(1)
    if fmt == "e4m3":
        byte = np.frexp(amax)[1] - 1 + 127 - 7
    else:
        mant, ex = np.frexp(amax / 6.0)
        byte = np.where(mant > 0.5, ex, ex - 1) + 127
    byte = np.clip(np.where(amax > 0, byte, 1), 1, 254)
    scaled = (w * np.exp2(127.0 - byte)[:, None, :]).reshape(k, n).astype(np.float32)
    by_word = np.ascontiguousarray(scaled.reshape(k // 512, 128, 4, n).transpose(0, 1, 3, 2))
    if fmt == "e4m3":
        words = by_word.astype(ml_dtypes.float8_e4m3fn).view(np.uint8)
    else:
        c = by_word.astype(ml_dtypes.float4_e2m1fn).view(np.uint8) & 0xF
        words = c[..., 0::2] | (c[..., 1::2] << 4)
    return np.ascontiguousarray(words), np.ascontiguousarray(byte.astype(np.uint8).reshape(k // 512, 16, n))


def unpack_weight(words, scales, fmt):
    g, p, n, _ = words.shape
    if fmt == "e4m3":
        vals = np.ascontiguousarray(words).view(ml_dtypes.float8_e4m3fn).astype(np.float64)
    else:
        nib = np.empty((g, p, n, 4), np.uint8)
        nib[..., 0::2] = words & 0xF
        nib[..., 1::2] = words >> 4
        vals = E2M1[nib]
    vals = vals * np.repeat(np.exp2(scales.astype(np.float64) - 127.0), 8, axis=1)[..., None]
    return vals.transpose(0, 1, 3, 2).reshape(g * 512, n)
def pack4(w):
    words, scales = pack_weight(w, "e2m1")
    return words.reshape(words.shape[0], 128, -1), scales


def unpack4(words, scales):
    return unpack_weight(words.reshape(words.shape[0], 128, -1, 2), scales, "e2m1")


M, J, C = 1024, 2048, 1024


def setup_inputs():
    s, u, t = mx_kscale(J), mx_kscale(M), mx_kscale(C)
    x = np.random.standard_normal((M, C)) * t
    codes = np.random.standard_normal((M, J)) * s
    patch_gain = (0.5 + np.random.random(M)) * u
    book = np.random.standard_normal((J, C)) / (3 * np.sqrt(J)) / s[:, None] * t
    row = np.random.standard_normal((M, M)) / (3 * np.sqrt(M)) / u[:, None]
    chan = np.random.standard_normal((C, 2 * C)) / np.sqrt(C) / t[:, None]
    book_words, book_scales = pack4(book)
    row_words, row_scales = pack4(row)
    chan_words, chan_scales = pack4(chan)
    return {"x": bf(x), "codes": bf(codes), "patch_gain": bf(patch_gain),
            "book_words": book_words, "book_scales": book_scales,
            "row_words": row_words, "row_scales": row_scales,
            "chan_words": chan_words, "chan_scales": chan_scales}


def reference(x, codes, patch_gain, book_words, book_scales, row_words, row_scales, chan_words, chan_scales):
    y = f64(x) + (mxq(f64(codes), 1, "e4m3") @ unpack4(book_words, book_scales))
    e = y * f64(patch_gain)[:, None]
    z = y + (unpack4(row_words, row_scales).T @ mxq(e, 0, "e4m3"))
    h = mxq(z, 1, "e4m3") @ unpack4(chan_words, chan_scales)
    return h[:, :C] * np.tanh(h[:, C:])

@@ -1,0 +1,330 @@
+from contextlib import ExitStack
+
+import concourse.mybir as mybir
+from concourse.masks import make_identity
+
+FLOPS = 2 * 1024 * 1024 * (2048 + 1024 + 2048)
+
+F32 = mybir.dt.float32
+BF16 = mybir.dt.bfloat16
+U32 = mybir.dt.uint32
+I32 = mybir.dt.int32
+U8 = mybir.dt.uint8
+FP8X4 = mybir.dt.float8_e4m3fn_x4
+FP4X4 = mybir.dt.float4_e2m1fn_x4
+ADD = mybir.AluOpType.add
+MULT = mybir.AluOpType.mult
+ACT = mybir.ActivationFunctionType
+
+P = 128
+ORDER = """
+W0 T0 C00 T1 C01 C10 Q0 R0 C11 A00 Q1 W2 R2 R1 T2 Y00 g C20 A10 R3 C21 A01 W3 Q2 Y10 A11 E00 X4 E10
+A21 Y01 Y11 E01 T3 E11 Y21 T4 C30 R4 C31 A20 R5 C40 Q3 C41 T5 X6 W7 Q4 A30 Y20 C50 A40 C51 Y30 E20
+Q5 T6 E30 Y40 T7 C60 J000 C61 J001 A31 J002 C70 Q6 C71 A50 Y31 E40 Q7 A60 I003 Y50 E21 A70 K00 E50
+Y60 E31 A41 Y70 E60 J010 A51 E70 Y41 I012 J100 A61 J102 I101 Y51 I103 A71 Y61 E41 K10 B00 E51 Y71
+E61 B10 J011 E71 z00 B20 I013 J111 B30 J113 I110 B40 z10 B50 I112 K01 U00 K11 B01 D00 z20 B11 z30
+z40 U10 B60 z50 D10 B21 z01 B31 z11 U01 q00 z60 B41 D01 z21 B51 q01 B61 z31 H02 z41 H00 G00 z51 H03
+z61 H01 G01 F00 U20 U11 q10 U21 D20 F01 H12 D11 q20 H10 D21 q11 H13 G10 q21 H11 G11 F10 H22 H20 F11
+G20 H23 H21 F20 G21 B70 B71 F21 H32 z70 H30 z71 G30 H33 H31 F30 G31 U30 U31 F31 D30 H42 D31 H40 q30
+H43 G40 q31 H41 F40 G41 H52 H50 F41 G50 H53 H51 F50 G51 H62 H60 F51 G60 H63 H61 F60 G61 H72 H70 F61
+G70 H73 H71 F70 G71 F71
+"""
+
+
+def tile_codebook_patch_mixer_t2_kernel(
+    tc, x, codes, patch_gain, book_words, book_scales, row_words, row_scales, chan_words, chan_scales, out
+):
+    nc = tc.nc
+    with ExitStack() as ctx:
+        keep = ctx.enter_context(tc.tile_pool(name="keep", bufs=1))
+        ring = ctx.enter_context(tc.tile_pool(name="ring", bufs=3))
+        psum = ctx.enter_context(tc.psum_pool(name="psum", bufs=8))
+        ctx.enter_context(tc.manual_schedule())
+
+        def kept(name, shape, dt):
+            return keep.tile(shape, dt, name=name, align_bytes=64)
+
+        craw = [kept("craw%d" % m, [P, 2048], BF16) for m in range(8)]
+        qc = [kept("qc%d" % m, [P, 4, P], U32) for m in range(8)]
+        qcs = [kept("qcs%d" % m, [P, 4, P], U8) for m in range(8)]
+        book = [kept("book%d" % h, [P, 4, 1024], U8) for h in range(2)]
+        bs = kept("bs", [P, 4, 1024], U8)
+        xt = [kept("x%d" % m, [P, 1024], BF16) for m in range(8)]
+        y = {(g, h): kept("y%d%d" % (g, h), [P, 4, 512], F32) for g in range(2) for h in range(2)}
+        eq = {(g, h): kept("eq%d%d" % (g, h), [P, 512], U32) for g in range(2) for h in range(2)}
+        eqs = {(g, h): kept("eqs%d%d" % (g, h), [P, 512], U8) for g in range(2) for h in range(2)}
+        rr = kept("rr", [P, 2, 2048], U8)
+        rs = kept("rs", [P, 2, 1024], U8)
+        rp = [kept("rp%d" % g, [P, 2048], U8) for g in range(2)]
+        rps = [kept("rps%d" % g, [P, 1024], U8) for g in range(2)]
+        wt = [kept("wt%d" % g, [P, 4096], U8) for g in range(2)]
+        ws = kept("ws", [P, 2, 2048], U8)
+        zq = {(k, h): kept("zq%d%d" % (k, h), [P, 2, P], U32) for k in range(4) for h in range(2)}
+        zqs = {(k, h): kept("zqs%d%d" % (k, h), [P, 2, P], U8) for k in range(4) for h in range(2)}
+        ident = kept("ident", [P, P], F32)
+        gain_raw = kept("gain_raw", [P, 2, 4], BF16)
+        gain = kept("gain", [P, 8], F32)
+        warm = kept("warm", [P, 1], F32)
+
+        nc.vector.memset(warm[:], 0.0)
+        nc.vector.memset(bs[:].rearrange("p g n -> p (g n)").bitcast(I32), 0)
+        nc.scalar.activation(out=warm[:], in_=warm[:], func=ACT.Tanh)
+        make_identity(nc, ident[:])
+        nc.vector.memset(rs[:].rearrange("p g n -> p (g n)").bitcast(I32), 0)
+        nc.vector.memset(ws[:].rearrange("p g n -> p (g n)").bitcast(I32), 0)
+
+        codes_v = codes.rearrange("(g p t) j -> g t p j", p=P, t=4)
+        x_v = x.rearrange("(g p t) c -> g t p c", p=P, t=4)
+        out_v = out.rearrange("(g p t) c -> g t p c", p=P, t=4)
+
+        def load_codes(m, parts=1):
+            w = 2048 // parts
+            for i in range(parts):
+                nc.sync.dma_start(out=craw[m][:, i * w : (i + 1) * w], in_=codes_v[m // 4, m % 4][:, i * w : (i + 1) * w])
+
+        def load_x(m):
+            nc.sync.dma_start(out=xt[m][:], in_=x_v[m // 4, m % 4])
+
+        def load_scales(tile, src):
+            dst = tile[:].bitcast(I32)
+            for r in range(4):
+                nc.sync.dma_start(
+                    out=dst[r : P : 32],
+                    in_=src.rearrange("g (q r) n -> r q g n", r=4)[r].bitcast(I32),
+                )
+
+        def load_book(h):
+            nc.sync.dma_start(
+                out=book[h][:].bitcast(I32),
+                in_=book_words[:, :, h * 1024 : (h + 1) * 1024].bitcast(I32).rearrange("g p b -> p g b"),
+            )
+
+        nc.scalar.dma_start(out=gain_raw[:], in_=patch_gain.rearrange("(g p t) -> p g t", p=P, t=4))
+        load_codes(0, 2)
+        load_codes(1)
+        load_scales(bs, book_scales)
+        load_book(0)
+        nc.sync.dma_start(out=rr[:].bitcast(I32), in_=row_words.bitcast(I32).rearrange("g p b -> p g b"))
+        load_codes(2)
+        load_book(1)
+        load_x(0)
+        load_codes(3)
+        load_x(1)
+        load_codes(4)
+        load_x(2)
+        load_codes(5)
+        load_scales(rs, row_scales)
+        load_x(3)
+        load_codes(6)
+        load_codes(7)
+        load_x(4)
+        load_x(5)
+        load_x(6)
+        load_x(7)
+        nc.sync.dma_start(out=wt[0][:].bitcast(I32), in_=chan_words[0].bitcast(I32))
+        nc.sync.dma_start(out=wt[1][:].bitcast(I32), in_=chan_words[1].bitcast(I32))
+        load_scales(ws, chan_scales)
+
+        tps = {}
+        cg = {}
+
+        cw = {}
+
+        def w_codes(m, copy):
+            cw[m] = ring.tile([P, 4, 2, P], F32, name="cw", bufs=2)
+            copy(out=cw[m][:], in_=craw[m][:].bitcast(F32).rearrange("p (g q u) -> p g u q", g=4, u=2))
+
+        def t_codes(m):
+            words = craw[m][:].bitcast(F32)
+            for b in range(2):
+                tp = psum.tile([P, 2, 2, P], F32, name="ps")
+                tps[m, b] = tp
+                for i in range(2):
+                    for u in range(2):
+                        w0 = 256 * (2 * b + i)
+                        src = cw[m][:, 2 * b + i, u, :] if m in cw else words[:, w0 + u : w0 + 256 : 2]
+                        nc.tensor.transpose(tp[:, i, u, :], src, ident[:])
+
+        def c_codes(m, b):
+            if b == 0:
+                cg[m] = ring.tile([P, 4, P, 4], BF16, name="cg", align_bytes=64)
+            copy = nc.vector.tensor_copy if (m, b) == (0, 1) else nc.scalar.copy
+            copy(
+                out=cg[m][:].bitcast(F32)[:, 2 * b : 2 * b + 2],
+                in_=tps[m, b][:].rearrange("p i u m -> p i m u"),
+            )
+
+        def q_codes(m):
+            nc.vector.quantize_mx(
+                out=qc[m][:].rearrange("p g m -> p (g m)").bitcast(FP8X4),
+                scales=qcs[m][:].rearrange("p g m -> p (g m)"),
+                in_=cg[m][:].rearrange("p g m t -> p (g m t)"),
+            )
+
+        accs = {}
+
+        def m_book(m, h):
+            acc = psum.tile([P, 512], F32, name="ps")
+            accs[m, h] = acc
+            for g in range(4):
+                nc.tensor.matmul_mx(
+                    out=acc[:],
+                    lhsT=qc[m][:, g, :].bitcast(FP8X4),
+                    lhsT_scale=qcs[m][:, g, :],
+                    rhs=book[h][:, g, :].bitcast(FP4X4),
+                    rhs_scale=bs[:, g, h * 512 : (h + 1) * 512],
+                    start=(g == 0),
+                    stop=(g == 3),
+                )
+
+        def y_add(m, h):
+            nc.vector.tensor_tensor(
+                out=y[m // 4, h][:, m % 4, :], in0=accs[m, h][:], in1=xt[m][:, h * 512 : (h + 1) * 512], op=ADD
+            )
+
+        elin = {}
+        eg = {}
+
+        def e_scale(m, h):
+            g, t = m // 4, m % 4
+            if t == 0:
+                elin[g, h] = ring.tile([P, 4, 512], BF16, name="elin", align_bytes=64)
+                eg[g, h] = ring.tile([P, 512, 4], BF16, name="eg", align_bytes=64)
+            nc.scalar.activation(
+                out=elin[g, h][:, t, :], in_=y[g, h][:, t, :], func=ACT.Copy, scale=gain[:, m : m + 1]
+            )
+
+        def e_inter(g, h, j, copy):
+            cols = slice(j * 128, (j + 1) * 128)
+            copy(
+                out=eg[g, h][:, cols, :].rearrange("p (c i) t -> p c t i", i=4),
+                in_=elin[g, h][:, :, cols].rearrange("p t (c i) -> p c t i", i=4),
+            )
+
+        def q_e(g, h):
+            nc.vector.quantize_mx(
+                out=eq[g, h][:].bitcast(FP8X4), scales=eqs[g, h][:], in_=eg[g, h][:].rearrange("p c t -> p (c t)")
+            )
+
+        def r_words(g, half):
+            sl = slice(half * 1024, (half + 1) * 1024)
+            nc.vector.tensor_copy(
+                out=rp[g][:, sl].rearrange("p (t m b) -> p t m b", t=4, b=2),
+                in_=rr[:, g, sl].rearrange("p (m t b) -> p t m b", t=4, b=2),
+            )
+
+        def r_scales(g):
+            nc.vector.tensor_copy(
+                out=rps[g][:].rearrange("p (G t m) -> p G t m", G=2, t=4),
+                in_=rs[:, g, :].rearrange("p (G m t) -> p G t m", G=2, t=4),
+            )
+
+        zacc = {}
+        zt = {}
+
+        def m_row(mo, h):
+            acc = psum.tile([P, 512], F32, name="ps")
+            zacc[mo, h] = acc
+            for g in range(2):
+                nc.tensor.matmul_mx(
+                    out=acc[:],
+                    lhsT=rp[g][:, mo * 256 : (mo + 1) * 256].bitcast(FP4X4),
+                    lhsT_scale=rps[g][:, mo * P : (mo + 1) * P],
+                    rhs=eq[g, h][:].bitcast(FP8X4),
+                    rhs_scale=eqs[g, h][:],
+                    start=(g == 0),
+                    stop=(g == 1),
+                )
+
+        def z_add(mo, h):
+            zt[mo, h] = keep.tile(
+                [P, 512], BF16, name="z%d%d" % (mo, h), tag="z%d" % mo if h else "craw%d" % mo, align_bytes=64
+            )
+            nc.vector.tensor_tensor(
+                out=zt[mo, h][:].rearrange("p (u q e) -> p u q e", u=2, e=2),
+                in0=zacc[mo, h][:].rearrange("p (q u e) -> p u q e", u=2, e=2),
+                in1=y[mo // 4, h][:, mo % 4, :].rearrange("p (q u e) -> p u q e", u=2, e=2),
+                op=ADD,
+            )
+
+        ztp = {}
+        zg = {}
+
+        def t_z(k, h):
+            tp = psum.tile([P, 2, 2, P], F32, name="ps")
+            ztp[k, h] = tp
+            for i in range(2):
+                words = zt[2 * k + i, h][:].bitcast(F32)
+                for u in range(2):
+                    nc.tensor.transpose(tp[:, i, u, :], words[:, u * P : (u + 1) * P], ident[:])
+
+        def c_z(k, h):
+            zg[k, h] = ring.tile([P, 2, P, 4], BF16, name="zg", align_bytes=64)
+            nc.scalar.copy(out=zg[k, h][:].bitcast(F32), in_=ztp[k, h][:].rearrange("p i u m -> p i m u"))
+
+        def q_z(k, h):
+            nc.vector.quantize_mx(
+                out=zq[k, h][:].rearrange("p i m -> p (i m)").bitcast(FP8X4),
+                scales=zqs[k, h][:].rearrange("p i m -> p (i m)"),
+                in_=zg[k, h][:].rearrange("p i m t -> p (i m t)"),
+            )
+
+        hacc = {}
+
+        def m_chan(mo, n):
+            acc = psum.tile([P, 512], F32, name="ps")
+            hacc[mo, n] = acc
+            for h in range(2):
+                nc.tensor.matmul_mx(
+                    out=acc[:],
+                    lhsT=zq[mo // 2, h][:, mo % 2, :].bitcast(FP8X4),
+                    lhsT_scale=zqs[mo // 2, h][:, mo % 2, :],
+                    rhs=wt[h][:, n * 1024 : (n + 1) * 1024].bitcast(FP4X4),
+                    rhs_scale=ws[:, h, n * 512 : (n + 1) * 512],
+                    start=(h == 0),
+                    stop=(h == 1),
+                )
+
+        th = {}
+
+        def gate(mo, n):
+            th[mo, n] = ring.tile([P, 512], F32, name="th", bufs=4)
+            nc.scalar.activation(out=th[mo, n][:], in_=hacc[mo, n + 2][:], func=ACT.Tanh)
+
+        def finish(mo, n):
+            ot = ring.tile([P, 512], F32, name="ot", bufs=6)
+            parts = 2 if (mo, n) == (7, 1) else 1
+            w = 512 // parts
+            for i in range(parts):
+                sl = slice(i * w, (i + 1) * w)
+                nc.vector.tensor_tensor(out=ot[:, sl], in0=hacc[mo, n][:, sl], in1=th[mo, n][:, sl], op=MULT)
+                nc.sync.dma_start(
+                    out=out_v[mo // 4, mo % 4][:, n * 512 + i * w : n * 512 + (i + 1) * w], in_=ot[:, sl]
+                )
+
+        V, S = nc.vector.tensor_copy, nc.scalar.copy
+        run = {
+            "g": lambda: nc.vector.tensor_copy(out=gain[:], in_=gain_raw[:].rearrange("p g t -> p (g t)")),
+            "T": t_codes,
+            "W": lambda m: w_codes(m, S),
+            "X": lambda m: w_codes(m, V),
+            "C": c_codes,
+            "Q": q_codes,
+            "A": m_book,
+            "Y": y_add,
+            "E": e_scale,
+            "I": lambda g, h, j: e_inter(g, h, j, S),
+            "J": lambda g, h, j: e_inter(g, h, j, V),
+            "K": q_e,
+            "R": lambda i: r_words(i // 2, i % 2) if i < 4 else r_scales(i - 4),
+            "B": m_row,
+            "z": z_add,
+            "U": t_z,
+            "D": c_z,
+            "q": q_z,
+            "H": m_chan,
+            "G": gate,
+            "F": finish,
+        }
+        for token in ORDER.split():
+            run[token[0]](*[int(n) for n in token[1:]])

@@ -9,6 +9,7 @@ F32 = mybir.dt.float32
 BF16 = mybir.dt.bfloat16
 U32 = mybir.dt.uint32
 I32 = mybir.dt.int32
+U16 = mybir.dt.uint16
 U8 = mybir.dt.uint8
 FP8X4 = mybir.dt.float8_e4m3fn_x4
 FP4X4 = mybir.dt.float4_e2m1fn_x4
@@ -17,18 +18,6 @@ MULT = mybir.AluOpType.mult
 ACT = mybir.ActivationFunctionType
 
 P = 128
-ORDER = """
-W0 T0 C00 T1 C01 C10 Q0 R0 C11 A00 Q1 W2 R2 R1 T2 Y00 g C20 A10 R3 C21 A01 W3 Q2 Y10 A11 E00 X4 E10
-A21 Y01 Y11 E01 T3 E11 Y21 T4 C30 R4 C31 A20 R5 C40 Q3 C41 T5 X6 W7 Q4 A30 Y20 C50 A40 C51 Y30 E20
-Q5 T6 E30 Y40 T7 C60 J000 C61 J001 A31 J002 C70 Q6 C71 A50 Y31 E40 Q7 A60 I003 Y50 E21 A70 K00 E50
-Y60 E31 A41 Y70 E60 J010 A51 E70 Y41 I012 J100 A61 J102 I101 Y51 I103 A71 Y61 E41 K10 B00 E51 Y71
-E61 B10 J011 E71 z00 B20 I013 J111 B30 J113 I110 B40 z10 B50 I112 K01 U00 K11 B01 D00 z20 B11 z30
-z40 U10 B60 z50 D10 B21 z01 B31 z11 U01 q00 z60 B41 D01 z21 B51 q01 B61 z31 H02 z41 H00 G00 z51 H03
-z61 H01 G01 F00 U20 U11 q10 U21 D20 F01 H12 D11 q20 H10 D21 q11 H13 G10 q21 H11 G11 F10 H22 H20 F11
-G20 H23 H21 F20 G21 B70 B71 F21 H32 z70 H30 z71 G30 H33 H31 F30 G31 U30 U31 F31 D30 H42 D31 H40 q30
-H43 G40 q31 H41 F40 G41 H52 H50 F41 G50 H53 H51 F50 G51 H62 H60 F51 G60 H63 H61 F60 G61 H72 H70 F61
-G70 H73 H71 F70 G71 F71
-"""
 
 
 def tile_codebook_patch_mixer_t2_kernel(
@@ -37,20 +26,23 @@ def tile_codebook_patch_mixer_t2_kernel(
     nc = tc.nc
     with ExitStack() as ctx:
         keep = ctx.enter_context(tc.tile_pool(name="keep", bufs=1))
-        ring = ctx.enter_context(tc.tile_pool(name="ring", bufs=3))
-        psum = ctx.enter_context(tc.psum_pool(name="psum", bufs=8))
+        ring = ctx.enter_context(tc.tile_pool(name="ring", bufs=2))
+        psum = ctx.enter_context(tc.psum_pool(name="psum", bufs=1))
         ctx.enter_context(tc.manual_schedule())
 
-        def kept(name, shape, dt):
-            return keep.tile(shape, dt, name=name, align_bytes=64)
+        def kept(name, shape, dt, tag=None):
+            return keep.tile(shape, dt, name=name, tag=tag or name, align_bytes=64)
+
+        def bank(name, number, shape):
+            return psum.tile(shape, F32, name=name, tag="bank%d" % number)
 
         craw = [kept("craw%d" % m, [P, 2048], BF16) for m in range(8)]
-        qc = [kept("qc%d" % m, [P, 4, P], U32) for m in range(8)]
-        qcs = [kept("qcs%d" % m, [P, 4, P], U8) for m in range(8)]
+        qc = [kept("qc%d" % m, [P, 4 * P], U32) for m in range(8)]
+        qcs = [kept("qcs%d" % m, [P, 4 * P], U8) for m in range(8)]
         book = [kept("book%d" % h, [P, 4, 1024], U8) for h in range(2)]
-        bs = kept("bs", [P, 4, 1024], U8)
+        bs = [kept("bs%d" % h, [P, 4, 512], U8) for h in range(2)]
         xt = [kept("x%d" % m, [P, 1024], BF16) for m in range(8)]
-        y = {(g, h): kept("y%d%d" % (g, h), [P, 4, 512], F32) for g in range(2) for h in range(2)}
+        y = {(m, h): kept("y%d%d" % (m, h), [P, 512], F32) for m in range(8) for h in range(2)}
         eq = {(g, h): kept("eq%d%d" % (g, h), [P, 512], U32) for g in range(2) for h in range(2)}
         eqs = {(g, h): kept("eqs%d%d" % (g, h), [P, 512], U8) for g in range(2) for h in range(2)}
         rr = kept("rr", [P, 2, 2048], U8)
@@ -59,19 +51,23 @@ def tile_codebook_patch_mixer_t2_kernel(
         rps = [kept("rps%d" % g, [P, 1024], U8) for g in range(2)]
         wt = [kept("wt%d" % g, [P, 4096], U8) for g in range(2)]
         ws = kept("ws", [P, 2, 2048], U8)
-        zq = {(k, h): kept("zq%d%d" % (k, h), [P, 2, P], U32) for k in range(4) for h in range(2)}
-        zqs = {(k, h): kept("zqs%d%d" % (k, h), [P, 2, P], U8) for k in range(4) for h in range(2)}
+        zq = [kept("zq%d" % m, [P, 2 * P], U32) for m in range(8)]
+        zqs = [kept("zqs%d" % m, [P, 2 * P], U8) for m in range(8)]
         ident = kept("ident", [P, P], F32)
         gain_raw = kept("gain_raw", [P, 2, 4], BF16)
         gain = kept("gain", [P, 8], F32)
         warm = kept("warm", [P, 1], F32)
 
+        def clear(plane):
+            nc.vector.memset(plane[:].rearrange("p g n -> p (g n)").bitcast(I32), 0)
+
+        clear(bs[0])
         nc.vector.memset(warm[:], 0.0)
-        nc.vector.memset(bs[:].rearrange("p g n -> p (g n)").bitcast(I32), 0)
         nc.scalar.activation(out=warm[:], in_=warm[:], func=ACT.Tanh)
         make_identity(nc, ident[:])
-        nc.vector.memset(rs[:].rearrange("p g n -> p (g n)").bitcast(I32), 0)
-        nc.vector.memset(ws[:].rearrange("p g n -> p (g n)").bitcast(I32), 0)
+        clear(bs[1])
+        clear(rs)
+        clear(ws)
 
         codes_v = codes.rearrange("(g p t) j -> g t p j", p=P, t=4)
         x_v = x.rearrange("(g p t) c -> g t p c", p=P, t=4)
@@ -85,59 +81,44 @@ def tile_codebook_patch_mixer_t2_kernel(
         def load_x(m):
             nc.sync.dma_start(out=xt[m][:], in_=x_v[m // 4, m % 4])
 
-        def load_scales(tile, src):
-            dst = tile[:].bitcast(I32)
+        def load_scales(plane, src):
+            dst = plane[:].bitcast(I32)
             for r in range(4):
-                nc.sync.dma_start(
-                    out=dst[r : P : 32],
-                    in_=src.rearrange("g (q r) n -> r q g n", r=4)[r].bitcast(I32),
-                )
+                nc.sync.dma_start(out=dst[r:P:32], in_=src.rearrange("g (q r) n -> r q g n", r=4)[r].bitcast(I32))
 
         def load_book(h):
+            load_scales(bs[h], book_scales[:, :, h * 512 : (h + 1) * 512])
             nc.sync.dma_start(
                 out=book[h][:].bitcast(I32),
                 in_=book_words[:, :, h * 1024 : (h + 1) * 1024].bitcast(I32).rearrange("g p b -> p g b"),
             )
 
-        nc.scalar.dma_start(out=gain_raw[:], in_=patch_gain.rearrange("(g p t) -> p g t", p=P, t=4))
-        load_codes(0, 2)
-        load_codes(1)
-        load_scales(bs, book_scales)
-        load_book(0)
-        nc.sync.dma_start(out=rr[:].bitcast(I32), in_=row_words.bitcast(I32).rearrange("g p b -> p g b"))
-        load_codes(2)
-        load_book(1)
-        load_x(0)
-        load_codes(3)
-        load_x(1)
-        load_codes(4)
-        load_x(2)
-        load_codes(5)
-        load_scales(rs, row_scales)
-        load_x(3)
-        load_codes(6)
-        load_codes(7)
-        load_x(4)
-        load_x(5)
-        load_x(6)
-        load_x(7)
-        nc.sync.dma_start(out=wt[0][:].bitcast(I32), in_=chan_words[0].bitcast(I32))
-        nc.sync.dma_start(out=wt[1][:].bitcast(I32), in_=chan_words[1].bitcast(I32))
-        load_scales(ws, chan_scales)
+        def load_row():
+            nc.sync.dma_start(out=rr[:].bitcast(I32), in_=row_words.bitcast(I32).rearrange("g p b -> p g b"))
+            load_scales(rs, row_scales)
 
-        tps = {}
-        cg = {}
+        def load_chan():
+            for h in range(2):
+                nc.sync.dma_start(out=wt[h][:].bitcast(I32), in_=chan_words[h].bitcast(I32))
+            load_scales(ws, chan_scales)
 
-        cw = {}
+        V, S = nc.vector.tensor_copy, nc.scalar.copy
 
-        def w_codes(m, copy):
-            cw[m] = ring.tile([P, 4, 2, P], F32, name="cw", bufs=2)
-            copy(out=cw[m][:], in_=craw[m][:].bitcast(F32).rearrange("p (g q u) -> p g u q", g=4, u=2))
+        cw, tps, cg, accs = {}, {}, {}, {}
+
+        def w_codes(m, copy, parts=1):
+            cw[m] = ring.tile([P, 4, 2, P], F32, name="cw%d" % m, tag="cw", bufs=2)
+            w = 4 // parts
+            for i in range(parts):
+                copy(
+                    out=cw[m][:, i * w : (i + 1) * w],
+                    in_=craw[m][:, i * w * 512 : (i + 1) * w * 512].bitcast(F32).rearrange("p (g q u) -> p g u q", g=w, u=2),
+                )
 
         def t_codes(m):
             words = craw[m][:].bitcast(F32)
             for b in range(2):
-                tp = psum.tile([P, 2, 2, P], F32, name="ps")
+                tp = bank("T%d%d" % (m, b), 2 * (m % 2) + b, [P, 2, 2, P])
                 tps[m, b] = tp
                 for i in range(2):
                     for u in range(2):
@@ -145,60 +126,55 @@ def tile_codebook_patch_mixer_t2_kernel(
                         src = cw[m][:, 2 * b + i, u, :] if m in cw else words[:, w0 + u : w0 + 256 : 2]
                         nc.tensor.transpose(tp[:, i, u, :], src, ident[:])
 
-        def c_codes(m, b):
-            if b == 0:
-                cg[m] = ring.tile([P, 4, P, 4], BF16, name="cg", align_bytes=64)
-            copy = nc.vector.tensor_copy if (m, b) == (0, 1) else nc.scalar.copy
-            copy(
-                out=cg[m][:].bitcast(F32)[:, 2 * b : 2 * b + 2],
-                in_=tps[m, b][:].rearrange("p i u m -> p i m u"),
-            )
+        def c_codes(m, b, copy=S):
+            cg[m, b] = ring.tile([P, 2, P, 4], BF16, name="cg%d%d" % (m, b), tag="cg", bufs=5, align_bytes=64)
+            copy(out=cg[m, b][:].bitcast(F32), in_=tps[m, b][:].rearrange("p i u m -> p i m u"))
 
-        def q_codes(m):
+        def q_codes(m, b):
+            cols = slice(b * 256, (b + 1) * 256)
             nc.vector.quantize_mx(
-                out=qc[m][:].rearrange("p g m -> p (g m)").bitcast(FP8X4),
-                scales=qcs[m][:].rearrange("p g m -> p (g m)"),
-                in_=cg[m][:].rearrange("p g m t -> p (g m t)"),
+                out=qc[m][:, cols].bitcast(FP8X4),
+                scales=qcs[m][:, cols],
+                in_=cg[m, b][:].rearrange("p g m t -> p (g m t)"),
             )
 
-        accs = {}
-
-        def m_book(m, h):
-            acc = psum.tile([P, 512], F32, name="ps")
+        def m_book(m, h, number):
+            acc = bank("A%d%d" % (m, h), number, [P, 512])
             accs[m, h] = acc
             for g in range(4):
                 nc.tensor.matmul_mx(
                     out=acc[:],
-                    lhsT=qc[m][:, g, :].bitcast(FP8X4),
-                    lhsT_scale=qcs[m][:, g, :],
+                    lhsT=qc[m][:, g * P : (g + 1) * P].bitcast(FP8X4),
+                    lhsT_scale=qcs[m][:, g * P : (g + 1) * P],
                     rhs=book[h][:, g, :].bitcast(FP4X4),
-                    rhs_scale=bs[:, g, h * 512 : (h + 1) * 512],
+                    rhs_scale=bs[h][:, g, :],
                     start=(g == 0),
                     stop=(g == 3),
                 )
 
-        def y_add(m, h):
+        def y_add(m, h, c0=0, c1=512):
             nc.vector.tensor_tensor(
-                out=y[m // 4, h][:, m % 4, :], in0=accs[m, h][:], in1=xt[m][:, h * 512 : (h + 1) * 512], op=ADD
+                out=y[m, h][:, c0:c1], in0=accs[m, h][:, c0:c1], in1=xt[m][:, h * 512 + c0 : h * 512 + c1], op=ADD
             )
 
-        elin = {}
-        eg = {}
+        elin, eg = {}, {}
 
-        def e_scale(m, h):
+        def e_scale(m, h, on_vector=False, c0=0, c1=512):
             g, t = m // 4, m % 4
             if t == 0:
-                elin[g, h] = ring.tile([P, 4, 512], BF16, name="elin", align_bytes=64)
-                eg[g, h] = ring.tile([P, 512, 4], BF16, name="eg", align_bytes=64)
-            nc.scalar.activation(
-                out=elin[g, h][:, t, :], in_=y[g, h][:, t, :], func=ACT.Copy, scale=gain[:, m : m + 1]
-            )
+                elin[g, h] = ring.tile([P, 4, 512], BF16, name="elin%d%d" % (g, h), tag="elin", bufs=3, align_bytes=64)
+                eg[g, h] = ring.tile([P, 512, 4], BF16, name="eg%d%d" % (g, h), tag="eg", bufs=3, align_bytes=64)
+            if on_vector:
+                nc.vector.tensor_scalar(
+                    out=elin[g, h][:, t, c0:c1], in0=y[m, h][:, c0:c1], scalar1=gain[:, m : m + 1], scalar2=None, op0=MULT
+                )
+            else:
+                nc.scalar.activation(out=elin[g, h][:, t, c0:c1], in_=y[m, h][:, c0:c1], func=ACT.Copy, scale=gain[:, m : m + 1])
 
-        def e_inter(g, h, j, copy):
-            cols = slice(j * 128, (j + 1) * 128)
+        def e_inter(g, h, c0, c1, copy):
             copy(
-                out=eg[g, h][:, cols, :].rearrange("p (c i) t -> p c t i", i=4),
-                in_=elin[g, h][:, :, cols].rearrange("p t (c i) -> p c t i", i=4),
+                out=eg[g, h][:, c0:c1, :].rearrange("p (c i) t -> p c t i", i=4),
+                in_=elin[g, h][:, :, c0:c1].rearrange("p t (c i) -> p c t i", i=4),
             )
 
         def q_e(g, h):
@@ -206,11 +182,10 @@ def tile_codebook_patch_mixer_t2_kernel(
                 out=eq[g, h][:].bitcast(FP8X4), scales=eqs[g, h][:], in_=eg[g, h][:].rearrange("p c t -> p (c t)")
             )
 
-        def r_words(g, half):
-            sl = slice(half * 1024, (half + 1) * 1024)
+        def r_words(g):
             nc.vector.tensor_copy(
-                out=rp[g][:, sl].rearrange("p (t m b) -> p t m b", t=4, b=2),
-                in_=rr[:, g, sl].rearrange("p (m t b) -> p t m b", t=4, b=2),
+                out=rp[g][:].bitcast(U16).rearrange("p (G t m) -> p G t m", G=2, t=4),
+                in_=rr[:, g, :].bitcast(U16).rearrange("p (G m t) -> p G t m", G=2, t=4),
             )
 
         def r_scales(g):
@@ -219,112 +194,299 @@ def tile_codebook_patch_mixer_t2_kernel(
                 in_=rs[:, g, :].rearrange("p (G m t) -> p G t m", G=2, t=4),
             )
 
-        zacc = {}
-        zt = {}
+        zacc, zt, ztp, zg, hacc, th = {}, {}, {}, {}, {}, {}
 
-        def m_row(mo, h):
-            acc = psum.tile([P, 512], F32, name="ps")
-            zacc[mo, h] = acc
-            for g in range(2):
+        def m_row(m, h, number, groups=(0, 1)):
+            if 0 in groups:
+                zacc[m, h] = bank("B%d%d" % (m, h), number, [P, 512])
+            acc = zacc[m, h]
+            for g in groups:
                 nc.tensor.matmul_mx(
                     out=acc[:],
-                    lhsT=rp[g][:, mo * 256 : (mo + 1) * 256].bitcast(FP4X4),
-                    lhsT_scale=rps[g][:, mo * P : (mo + 1) * P],
+                    lhsT=rp[g][:, m * 256 : (m + 1) * 256].bitcast(FP4X4),
+                    lhsT_scale=rps[g][:, m * P : (m + 1) * P],
                     rhs=eq[g, h][:].bitcast(FP8X4),
                     rhs_scale=eqs[g, h][:],
                     start=(g == 0),
                     stop=(g == 1),
                 )
 
-        def z_add(mo, h):
-            zt[mo, h] = keep.tile(
-                [P, 512], BF16, name="z%d%d" % (mo, h), tag="z%d" % mo if h else "craw%d" % mo, align_bytes=64
-            )
+        def z_add(m, h):
+            if h == 0:
+                zt[m] = kept("z%d" % m, [P, 1024], BF16, tag="craw%d" % m)
             nc.vector.tensor_tensor(
-                out=zt[mo, h][:].rearrange("p (u q e) -> p u q e", u=2, e=2),
-                in0=zacc[mo, h][:].rearrange("p (q u e) -> p u q e", u=2, e=2),
-                in1=y[mo // 4, h][:, mo % 4, :].rearrange("p (q u e) -> p u q e", u=2, e=2),
+                out=zt[m][:, h * 512 : (h + 1) * 512].rearrange("p (u q e) -> p u q e", u=2, e=2),
+                in0=zacc[m, h][:].rearrange("p (q u e) -> p u q e", u=2, e=2),
+                in1=y[m, h][:].rearrange("p (q u e) -> p u q e", u=2, e=2),
                 op=ADD,
             )
 
-        ztp = {}
-        zg = {}
-
-        def t_z(k, h):
-            tp = psum.tile([P, 2, 2, P], F32, name="ps")
-            ztp[k, h] = tp
-            for i in range(2):
-                words = zt[2 * k + i, h][:].bitcast(F32)
+        def t_z(m, number):
+            tp = bank("U%d" % m, number, [P, 2, 2, P])
+            ztp[m] = tp
+            words = zt[m][:].bitcast(F32)
+            for h in range(2):
                 for u in range(2):
-                    nc.tensor.transpose(tp[:, i, u, :], words[:, u * P : (u + 1) * P], ident[:])
+                    nc.tensor.transpose(tp[:, h, u, :], words[:, (2 * h + u) * P : (2 * h + u + 1) * P], ident[:])
 
-        def c_z(k, h):
-            zg[k, h] = ring.tile([P, 2, P, 4], BF16, name="zg", align_bytes=64)
-            nc.scalar.copy(out=zg[k, h][:].bitcast(F32), in_=ztp[k, h][:].rearrange("p i u m -> p i m u"))
+        def c_z(m):
+            zg[m] = ring.tile([P, 2, P, 4], BF16, name="zg%d" % m, tag="cg", bufs=5, align_bytes=64)
+            nc.scalar.copy(out=zg[m][:].bitcast(F32), in_=ztp[m][:].rearrange("p i u m -> p i m u"))
 
-        def q_z(k, h):
+        def q_z(m):
             nc.vector.quantize_mx(
-                out=zq[k, h][:].rearrange("p i m -> p (i m)").bitcast(FP8X4),
-                scales=zqs[k, h][:].rearrange("p i m -> p (i m)"),
-                in_=zg[k, h][:].rearrange("p i m t -> p (i m t)"),
+                out=zq[m][:].bitcast(FP8X4), scales=zqs[m][:], in_=zg[m][:].rearrange("p i m t -> p (i m t)")
             )
 
-        hacc = {}
-
-        def m_chan(mo, n):
-            acc = psum.tile([P, 512], F32, name="ps")
-            hacc[mo, n] = acc
+        def m_chan(m, n, number):
+            acc = bank("H%d%d" % (m, n), number, [P, 512])
+            hacc[m, n] = acc
             for h in range(2):
                 nc.tensor.matmul_mx(
                     out=acc[:],
-                    lhsT=zq[mo // 2, h][:, mo % 2, :].bitcast(FP8X4),
-                    lhsT_scale=zqs[mo // 2, h][:, mo % 2, :],
+                    lhsT=zq[m][:, h * P : (h + 1) * P].bitcast(FP8X4),
+                    lhsT_scale=zqs[m][:, h * P : (h + 1) * P],
                     rhs=wt[h][:, n * 1024 : (n + 1) * 1024].bitcast(FP4X4),
                     rhs_scale=ws[:, h, n * 512 : (n + 1) * 512],
                     start=(h == 0),
                     stop=(h == 1),
                 )
 
-        th = {}
+        def m_chan_piece(m, n, i, number):
+            acc = bank("L%d%d" % (n, i), number, [P, P])
+            hacc[m, n, i] = acc
+            for h in range(2):
+                nc.tensor.matmul_mx(
+                    out=acc[:],
+                    lhsT=zq[m][:, h * P : (h + 1) * P].bitcast(FP8X4),
+                    lhsT_scale=zqs[m][:, h * P : (h + 1) * P],
+                    rhs=wt[h][:, n * 1024 + i * 256 : n * 1024 + (i + 1) * 256].bitcast(FP4X4),
+                    rhs_scale=ws[:, h, n * 512 + i * P : n * 512 + (i + 1) * P],
+                    start=(h == 0),
+                    stop=(h == 1),
+                )
 
-        def gate(mo, n):
-            th[mo, n] = ring.tile([P, 512], F32, name="th", bufs=4)
-            nc.scalar.activation(out=th[mo, n][:], in_=hacc[mo, n + 2][:], func=ACT.Tanh)
+        def gate_piece(m, n, i):
+            th[m, n, i] = ring.tile([P, P], F32, name="tp%d" % i, tag="tp", bufs=4)
+            nc.scalar.activation(out=th[m, n, i][:], in_=hacc[m, n + 2, i][:], func=ACT.Tanh)
 
-        def finish(mo, n):
-            ot = ring.tile([P, 512], F32, name="ot", bufs=6)
-            parts = 2 if (mo, n) == (7, 1) else 1
+        def finish_piece(m, n, i):
+            ot = ring.tile([P, P], F32, name="op%d" % i, tag="op", bufs=4)
+            nc.vector.tensor_tensor(out=ot[:], in0=hacc[m, n, i][:], in1=th[m, n, i][:], op=MULT)
+            nc.sync.dma_start(out=out_v[m // 4, m % 4][:, n * 512 + i * P : n * 512 + (i + 1) * P], in_=ot[:])
+
+        def gate(m, n):
+            th[m, n] = ring.tile([P, 512], F32, name="th%d%d" % (m, n), tag="th", bufs=3)
+            nc.scalar.activation(out=th[m, n][:], in_=hacc[m, n + 2][:], func=ACT.Tanh)
+
+        def finish(m, n, parts=1):
+            ot = ring.tile([P, 512], F32, name="ot%d%d" % (m, n), tag="ot", bufs=5)
             w = 512 // parts
             for i in range(parts):
                 sl = slice(i * w, (i + 1) * w)
-                nc.vector.tensor_tensor(out=ot[:, sl], in0=hacc[mo, n][:, sl], in1=th[mo, n][:, sl], op=MULT)
-                nc.sync.dma_start(
-                    out=out_v[mo // 4, mo % 4][:, n * 512 + i * w : n * 512 + (i + 1) * w], in_=ot[:, sl]
-                )
+                nc.vector.tensor_tensor(out=ot[:, sl], in0=hacc[m, n][:, sl], in1=th[m, n][:, sl], op=MULT)
+                nc.sync.dma_start(out=out_v[m // 4, m % 4][:, n * 512 + i * w : n * 512 + (i + 1) * w], in_=ot[:, sl])
 
-        V, S = nc.vector.tensor_copy, nc.scalar.copy
-        run = {
-            "g": lambda: nc.vector.tensor_copy(out=gain[:], in_=gain_raw[:].rearrange("p g t -> p (g t)")),
-            "T": t_codes,
-            "W": lambda m: w_codes(m, S),
-            "X": lambda m: w_codes(m, V),
-            "C": c_codes,
-            "Q": q_codes,
-            "A": m_book,
-            "Y": y_add,
-            "E": e_scale,
-            "I": lambda g, h, j: e_inter(g, h, j, S),
-            "J": lambda g, h, j: e_inter(g, h, j, V),
-            "K": q_e,
-            "R": lambda i: r_words(i // 2, i % 2) if i < 4 else r_scales(i - 4),
-            "B": m_row,
-            "z": z_add,
-            "U": t_z,
-            "D": c_z,
-            "q": q_z,
-            "H": m_chan,
-            "G": gate,
-            "F": finish,
-        }
-        for token in ORDER.split():
-            run[token[0]](*[int(n) for n in token[1:]])
+
+        load_codes(0, 2)
+        load_book(0)
+        load_codes(1)
+        load_book(1)
+        load_codes(2)
+        load_codes(3)
+        load_x(0)
+        nc.sync.dma_start(out=gain_raw[:], in_=patch_gain.rearrange("(g p t) -> p g t", p=P, t=4))
+        load_x(1)
+        load_row()
+        load_codes(4)
+        load_codes(5)
+        load_x(2)
+        load_x(3)
+        load_codes(6)
+        load_codes(7)
+        for m in range(4, 8):
+            load_x(m)
+        load_chan()
+
+        def turn(m):
+            t_codes(m)
+            c_codes(m, 0)
+            c_codes(m, 1)
+        def quant(m):
+            q_codes(m, 0)
+            q_codes(m, 1)
+        def ye(m, h):
+            y_add(m, h)
+            e_scale(m, h)
+
+        w_codes(0, V, 2)
+        turn(0)
+        quant(0)
+        m_book(0, 0, 4)
+        w_codes(1, V)
+        turn(1)
+        m_book(0, 1, 5)
+        quant(1)
+        m_book(1, 0, 6)
+        w_codes(2, V)
+        w_codes(3, V)
+        turn(2)
+        turn(3)
+        y_add(0, 0)
+        nc.vector.tensor_copy(out=gain[:], in_=gain_raw[:].rearrange("p g t -> p (g t)"))
+        m_book(1, 1, 7)
+        quant(2)
+        y_add(0, 1)
+        quant(3)
+        e_scale(0, 0)
+        e_scale(0, 1)
+        m_book(2, 0, 4)
+        ye(1, 0)
+        m_book(3, 0, 5)
+        ye(1, 1)
+        r_words(0)
+        turn(4)
+        r_words(1)
+        r_scales(0)
+        turn(5)
+        m_book(2, 1, 6)
+        ye(2, 0)
+        quant(4)
+        m_book(3, 1, 7)
+        ye(3, 0)
+        r_scales(1)
+        quant(5)
+        m_book(4, 0, 4)
+        ye(2, 1)
+        ye(3, 1)
+        turn(6)
+        e_inter(0, 0, 0, 512, V)
+        turn(7)
+        ye(4, 0)
+        q_e(0, 0)
+        m_book(5, 0, 5)
+        quant(6)
+        m_book(4, 1, 6)
+        quant(7)
+        e_inter(0, 1, 0, 256, S)
+        ye(5, 0)
+        m_book(6, 0, 7)
+        ye(4, 1)
+        e_inter(0, 1, 256, 512, V)
+        m_book(7, 0, 4)
+        ye(6, 0)
+        m_book(5, 1, 5)
+        ye(7, 0)
+        q_e(0, 1)
+        m_book(6, 1, 6)
+        y_add(5, 1)
+        e_inter(1, 0, 0, 256, V)
+        e_inter(1, 0, 256, 512, S)
+        e_scale(5, 1)
+        m_book(7, 1, 7)
+        ye(6, 1)
+        q_e(1, 0)
+        y_add(7, 1, 0, 256)
+        y_add(7, 1, 256, 512)
+        e_scale(7, 1, False, 0, 256)
+        e_scale(7, 1, False, 256, 512)
+
+        for g in range(2):
+            for m in range(4):
+                m_row(m, 0, m, (g,))
+        e_inter(1, 1, 0, 256, V)
+        e_inter(1, 1, 256, 384, V)
+        e_inter(1, 1, 384, 512, S)
+        z_add(0, 0)
+        q_e(1, 1)
+        m_row(4, 0, 4)
+        m_row(5, 0, 7)
+        for g in range(2):
+            m_row(0, 1, 5, (g,))
+            m_row(1, 1, 6, (g,))
+        z_add(1, 0)
+        z_add(2, 0)
+        z_add(0, 1)
+        z_add(1, 1)
+        m_row(2, 1, 0)
+        m_row(3, 1, 1)
+        t_z(0, 2)
+        t_z(1, 5)
+        c_z(0)
+        c_z(1)
+        z_add(2, 1)
+        z_add(3, 0)
+        q_z(0)
+        m_row(4, 1, 6)
+        m_row(6, 0, 0)
+        def chan(m, b0, b1, b2, b3):
+            m_chan(m, 2, b0)
+            gate(m, 0)
+            m_chan(m, 0, b1)
+            m_chan(m, 3, b2)
+            gate(m, 1)
+            m_chan(m, 1, b3)
+        z_add(3, 1)
+        q_z(1)
+        chan(0, 3, 2, 5, 1)
+        z_add(4, 0)
+        finish(0, 0)
+        z_add(4, 1)
+        finish(0, 1)
+        t_z(2, 3)
+        t_z(3, 4)
+        c_z(2)
+        c_z(3)
+        chan(1, 2, 5, 6, 1)
+        z_add(5, 0)
+        q_z(2)
+        finish(1, 0)
+        q_z(3)
+        z_add(6, 0)
+        finish(1, 1)
+        m_row(5, 1, 3)
+        m_row(6, 1, 4)
+        chan(2, 2, 7, 6, 0)
+        z_add(5, 1)
+        finish(2, 0)
+        z_add(6, 1)
+        finish(2, 1)
+        t_z(4, 5)
+        t_z(5, 1)
+        c_z(4)
+        c_z(5)
+        m_row(7, 0, 3)
+        m_row(7, 1, 2)
+        chan(3, 4, 7, 6, 0)
+        q_z(4)
+        q_z(5)
+        z_add(7, 0)
+        finish(3, 0)
+        z_add(7, 1)
+        finish(3, 1)
+        chan(4, 5, 1, 3, 4)
+        finish(4, 0)
+        finish(4, 1)
+        t_z(6, 2)
+        t_z(7, 7)
+        c_z(6)
+        c_z(7)
+        chan(5, 6, 0, 5, 1)
+        q_z(6)
+        finish(5, 0)
+        q_z(7)
+        finish(5, 1)
+        chan(6, 3, 4, 2, 7)
+        finish(6, 0)
+        finish(6, 1)
+        m_chan(7, 2, 6)
+        gate(7, 0)
+        m_chan(7, 0, 0)
+        finish(7, 0)
+        for i in range(5):
+            if i < 4:
+                m_chan_piece(7, 3, i, (5, 3, 2, 6)[i])
+                gate_piece(7, 1, i)
+            if i > 0:
+                m_chan_piece(7, 1, i - 1, (1, 4, 7, 5)[i - 1])
+                finish_piece(7, 1, i - 1)

@@ -18,6 +18,7 @@ MULT = mybir.AluOpType.mult
 ACT = mybir.ActivationFunctionType
 
 P = 128
+R_PARTS = ((0, 4), (4, 6), (6, 8))
 
 
 def tile_codebook_patch_mixer_t2_kernel(
@@ -41,14 +42,18 @@ def tile_codebook_patch_mixer_t2_kernel(
         qcs = [kept("qcs%d" % m, [P, 4 * P], U8) for m in range(8)]
         book = [kept("book%d" % h, [P, 4, 1024], U8) for h in range(2)]
         bs = [kept("bs%d" % h, [P, 4, 512], U8) for h in range(2)]
-        xt = [kept("x%d" % m, [P, 1024], BF16) for m in range(8)]
+        xt = {(m, h): kept("x%d%d" % (m, h), [P, 512], BF16) for m in range(8) for h in range(2)}
         y = {(m, h): kept("y%d%d" % (m, h), [P, 512], F32) for m in range(8) for h in range(2)}
         eq = {(g, h): kept("eq%d%d" % (g, h), [P, 512], U32) for g in range(2) for h in range(2)}
         eqs = {(g, h): kept("eqs%d%d" % (g, h), [P, 512], U8) for g in range(2) for h in range(2)}
         rr = kept("rr", [P, 2, 2048], U8)
         rs = kept("rs", [P, 2, 1024], U8)
-        rp = [kept("rp%d" % g, [P, 2048], U8) for g in range(2)]
-        rps = [kept("rps%d" % g, [P, 1024], U8) for g in range(2)]
+        rp, rps, rcol = {}, {}, {}
+        for m0, m1 in R_PARTS:
+            rp[m0] = kept("rp%d" % m0, [P, 2 * (m1 - m0) * 256], U8)
+            rps[m0] = kept("rps%d" % m0, [P, 2 * (m1 - m0) * P], U8)
+            for m in range(m0, m1):
+                rcol[m] = (m0, [(g * (m1 - m0) + m - m0) * P for g in range(2)])
         wt = [kept("wt%d" % g, [P, 4096], U8) for g in range(2)]
         ws = kept("ws", [P, 2, 2048], U8)
         zq = [kept("zq%d" % m, [P, 2 * P], U32) for m in range(8)]
@@ -78,8 +83,8 @@ def tile_codebook_patch_mixer_t2_kernel(
             for i in range(parts):
                 nc.sync.dma_start(out=craw[m][:, i * w : (i + 1) * w], in_=codes_v[m // 4, m % 4][:, i * w : (i + 1) * w])
 
-        def load_x(m):
-            nc.sync.dma_start(out=xt[m][:], in_=x_v[m // 4, m % 4])
+        def load_x(m, h):
+            nc.sync.dma_start(out=xt[m, h][:], in_=x_v[m // 4, m % 4][:, h * 512 : (h + 1) * 512])
 
         def load_scales(plane, src):
             dst = plane[:].bitcast(I32)
@@ -152,9 +157,31 @@ def tile_codebook_patch_mixer_t2_kernel(
                     stop=(g == 3),
                 )
 
+        def m_book_half(m, h, j, number):
+            acc = bank("a%d%d" % (m, j), number, [P, 256])
+            accs[m, h, j] = acc
+            for i in range(2):
+                c0 = j * 256 + i * P
+                for g in range(4):
+                    nc.tensor.matmul_mx(
+                        out=acc[:, i * P : (i + 1) * P],
+                        lhsT=qc[m][:, g * P : (g + 1) * P].bitcast(FP8X4),
+                        lhsT_scale=qcs[m][:, g * P : (g + 1) * P],
+                        rhs=book[h][:, g, 2 * c0 : 2 * (c0 + P)].bitcast(FP4X4),
+                        rhs_scale=bs[h][:, g, c0 : c0 + P],
+                        start=(g == 0),
+                        stop=(g == 3),
+                    )
+
+        def y_add_half(m, h, j):
+            c0, c1 = j * 256, (j + 1) * 256
+            nc.vector.tensor_tensor(
+                out=y[m, h][:, c0:c1], in0=accs[m, h, j][:], in1=xt[m, h][:, c0:c1], op=ADD
+            )
+
         def y_add(m, h, c0=0, c1=512):
             nc.vector.tensor_tensor(
-                out=y[m, h][:, c0:c1], in0=accs[m, h][:, c0:c1], in1=xt[m][:, h * 512 + c0 : h * 512 + c1], op=ADD
+                out=y[m, h][:, c0:c1], in0=accs[m, h][:, c0:c1], in1=xt[m, h][:, c0:c1], op=ADD
             )
 
         elin, eg = {}, {}
@@ -177,21 +204,25 @@ def tile_codebook_patch_mixer_t2_kernel(
                 in_=elin[g, h][:, :, c0:c1].rearrange("p t (c i) -> p c t i", i=4),
             )
 
-        def q_e(g, h):
+        def q_e(g, h, c0=0, c1=512):
             nc.vector.quantize_mx(
-                out=eq[g, h][:].bitcast(FP8X4), scales=eqs[g, h][:], in_=eg[g, h][:].rearrange("p c t -> p (c t)")
+                out=eq[g, h][:, c0:c1].bitcast(FP8X4),
+                scales=eqs[g, h][:, c0:c1],
+                in_=eg[g, h][:, c0:c1, :].rearrange("p c t -> p (c t)"),
             )
 
-        def r_words(g):
+        def r_words(m0, m1):
+            G, t0, t1 = m0 // 4, m0 % 4, (m1 - 1) % 4 + 1
             nc.vector.tensor_copy(
-                out=rp[g][:].bitcast(U16).rearrange("p (G t m) -> p G t m", G=2, t=4),
-                in_=rr[:, g, :].bitcast(U16).rearrange("p (G m t) -> p G t m", G=2, t=4),
+                out=rp[m0][:].bitcast(U16).rearrange("p (g t m) -> p g t m", g=2, m=P),
+                in_=rr[:].bitcast(U16).rearrange("p g (G m t) -> p G g t m", G=2, t=4)[:, G, :, t0:t1],
             )
 
-        def r_scales(g):
+        def r_scales(m0, m1):
+            G, t0, t1 = m0 // 4, m0 % 4, (m1 - 1) % 4 + 1
             nc.vector.tensor_copy(
-                out=rps[g][:].rearrange("p (G t m) -> p G t m", G=2, t=4),
-                in_=rs[:, g, :].rearrange("p (G m t) -> p G t m", G=2, t=4),
+                out=rps[m0][:].rearrange("p (g t m) -> p g t m", g=2, m=P),
+                in_=rs[:].rearrange("p g (G m t) -> p G g t m", G=2, t=4)[:, G, :, t0:t1],
             )
 
         zacc, zt, ztp, zg, hacc, th = {}, {}, {}, {}, {}, {}
@@ -203,8 +234,8 @@ def tile_codebook_patch_mixer_t2_kernel(
             for g in groups:
                 nc.tensor.matmul_mx(
                     out=acc[:],
-                    lhsT=rp[g][:, m * 256 : (m + 1) * 256].bitcast(FP4X4),
-                    lhsT_scale=rps[g][:, m * P : (m + 1) * P],
+                    lhsT=rp[rcol[m][0]][:, 2 * rcol[m][1][g] : 2 * (rcol[m][1][g] + P)].bitcast(FP4X4),
+                    lhsT_scale=rps[rcol[m][0]][:, rcol[m][1][g] : rcol[m][1][g] + P],
                     rhs=eq[g, h][:].bitcast(FP8X4),
                     rhs_scale=eqs[g, h][:],
                     start=(g == 0),
@@ -289,23 +320,18 @@ def tile_codebook_patch_mixer_t2_kernel(
 
 
         load_codes(0, 2)
-        load_book(0)
         load_codes(1)
-        load_book(1)
-        load_codes(2)
-        load_codes(3)
-        load_x(0)
+        load_book(0)
+        load_x(0, 0)
         nc.sync.dma_start(out=gain_raw[:], in_=patch_gain.rearrange("(g p t) -> p g t", p=P, t=4))
-        load_x(1)
+        for m in range(2, 8):
+            load_codes(m)
+            load_x(m - 1, 0)
         load_row()
-        load_codes(4)
-        load_codes(5)
-        load_x(2)
-        load_x(3)
-        load_codes(6)
-        load_codes(7)
-        for m in range(4, 8):
-            load_x(m)
+        load_book(1)
+        load_x(7, 0)
+        for m in range(8):
+            load_x(m, 1)
         load_chan()
 
         def turn(m):
@@ -321,104 +347,92 @@ def tile_codebook_patch_mixer_t2_kernel(
 
         w_codes(0, V, 2)
         turn(0)
-        quant(0)
-        m_book(0, 0, 4)
         w_codes(1, V)
+        quant(0)
         turn(1)
-        m_book(0, 1, 5)
         quant(1)
-        m_book(1, 0, 6)
-        w_codes(2, V)
-        w_codes(3, V)
-        turn(2)
-        turn(3)
-        y_add(0, 0)
         nc.vector.tensor_copy(out=gain[:], in_=gain_raw[:].rearrange("p g t -> p (g t)"))
-        m_book(1, 1, 7)
+        m_book(0, 0, 4)
+        turn(2)
+        ye(0, 0)
+        m_book(1, 0, 5)
+        w_codes(3, V)
         quant(2)
-        y_add(0, 1)
-        quant(3)
-        e_scale(0, 0)
-        e_scale(0, 1)
-        m_book(2, 0, 4)
-        ye(1, 0)
-        m_book(3, 0, 5)
-        ye(1, 1)
-        r_words(0)
-        turn(4)
-        r_words(1)
-        r_scales(0)
-        turn(5)
-        m_book(2, 1, 6)
-        ye(2, 0)
-        quant(4)
-        m_book(3, 1, 7)
-        ye(3, 0)
-        r_scales(1)
-        quant(5)
-        m_book(4, 0, 4)
-        ye(2, 1)
-        ye(3, 1)
-        turn(6)
-        e_inter(0, 0, 0, 512, V)
-        turn(7)
-        ye(4, 0)
-        q_e(0, 0)
-        m_book(5, 0, 5)
-        quant(6)
-        m_book(4, 1, 6)
-        quant(7)
-        e_inter(0, 1, 0, 256, S)
-        ye(5, 0)
-        m_book(6, 0, 7)
-        ye(4, 1)
-        e_inter(0, 1, 256, 512, V)
-        m_book(7, 0, 4)
-        ye(6, 0)
-        m_book(5, 1, 5)
+        for m in range(2, 7):
+            turn(m + 1)
+            ye(m - 1, 0)
+            m_book(m, 0, 4 + m % 4)
+            if m + 2 <= 6:
+                w_codes(m + 2, V)
+            if m == 5:
+                r_words(0, 4)
+            if m == 6:
+                r_scales(0, 4)
+            quant(m + 1)
+        m_book(0, 1, 0)
+        y_add(6, 0)
+        e_inter(0, 0, 0, 256, V)
+        e_inter(0, 0, 256, 512, S)
+        e_scale(6, 0)
+        m_book(7, 0, 7)
+        ye(0, 1)
+        r_words(4, 6)
+        m_book(1, 1, 1)
         ye(7, 0)
-        q_e(0, 1)
-        m_book(6, 1, 6)
-        y_add(5, 1)
+        q_e(0, 0)
+        m_book(2, 1, 2)
+        y_add(1, 1)
         e_inter(1, 0, 0, 256, V)
         e_inter(1, 0, 256, 512, S)
-        e_scale(5, 1)
-        m_book(7, 1, 7)
-        ye(6, 1)
+        e_scale(1, 1)
+        m_book(3, 1, 3)
+        ye(2, 1)
+        m_book(4, 1, 4)
+        ye(3, 1)
         q_e(1, 0)
-        y_add(7, 1, 0, 256)
-        y_add(7, 1, 256, 512)
+        r_scales(4, 6)
+        m_book(5, 1, 5)
+        y_add(4, 1)
+        e_inter(0, 1, 0, 256, V)
+        e_inter(0, 1, 256, 512, S)
+        e_scale(4, 1)
+        m_book(6, 1, 6)
+        ye(5, 1)
+        m_book_half(7, 1, 0, 7)
+        m_book_half(7, 1, 1, 4)
+        ye(6, 1)
+        y_add_half(7, 1, 0)
+        y_add_half(7, 1, 1)
+        q_e(0, 1)
         e_scale(7, 1, False, 0, 256)
         e_scale(7, 1, False, 256, 512)
 
-        for g in range(2):
-            for m in range(4):
-                m_row(m, 0, m, (g,))
+        for m in range(4):
+            m_row(m, 0, m)
         e_inter(1, 1, 0, 256, V)
         e_inter(1, 1, 256, 384, V)
         e_inter(1, 1, 384, 512, S)
+        q_e(1, 1, 0, 256)
+        q_e(1, 1, 256, 512)
         z_add(0, 0)
-        q_e(1, 1)
-        m_row(4, 0, 4)
-        m_row(5, 0, 7)
+        m_row(4, 0, 7)
         for g in range(2):
             m_row(0, 1, 5, (g,))
             m_row(1, 1, 6, (g,))
         z_add(1, 0)
-        z_add(2, 0)
         z_add(0, 1)
         z_add(1, 1)
-        m_row(2, 1, 0)
-        m_row(3, 1, 1)
-        t_z(0, 2)
+        m_row(2, 1, 4)
+        m_row(3, 1, 0)
+        t_z(0, 1)
         t_z(1, 5)
         c_z(0)
         c_z(1)
+        z_add(2, 0)
         z_add(2, 1)
-        z_add(3, 0)
         q_z(0)
         m_row(4, 1, 6)
-        m_row(6, 0, 0)
+        m_row(5, 0, 2)
         def chan(m, b0, b1, b2, b3):
             m_chan(m, 2, b0)
             gate(m, 0)
@@ -426,67 +440,71 @@ def tile_codebook_patch_mixer_t2_kernel(
             m_chan(m, 3, b2)
             gate(m, 1)
             m_chan(m, 1, b3)
-        z_add(3, 1)
+        z_add(3, 0)
         q_z(1)
-        chan(0, 3, 2, 5, 1)
+        z_add(3, 1)
+        chan(0, 1, 4, 5, 3)
         z_add(4, 0)
         finish(0, 0)
-        z_add(4, 1)
         finish(0, 1)
-        t_z(2, 3)
-        t_z(3, 4)
+        t_z(2, 0)
+        t_z(3, 1)
         c_z(2)
         c_z(3)
-        chan(1, 2, 5, 6, 1)
-        z_add(5, 0)
+        chan(1, 7, 4, 5, 3)
+        z_add(4, 1)
         q_z(2)
         finish(1, 0)
         q_z(3)
-        z_add(6, 0)
         finish(1, 1)
-        m_row(5, 1, 3)
-        m_row(6, 1, 4)
-        chan(2, 2, 7, 6, 0)
+        m_row(5, 1, 0)
+        chan(2, 1, 6, 7, 4)
+        z_add(5, 0)
         z_add(5, 1)
         finish(2, 0)
-        z_add(6, 1)
+        r_words(6, 8)
         finish(2, 1)
+        r_scales(6, 8)
         t_z(4, 5)
-        t_z(5, 1)
+        t_z(5, 3)
         c_z(4)
         c_z(5)
-        m_row(7, 0, 3)
-        m_row(7, 1, 2)
-        chan(3, 4, 7, 6, 0)
+        chan(3, 2, 0, 1, 6)
         q_z(4)
-        q_z(5)
-        z_add(7, 0)
         finish(3, 0)
-        z_add(7, 1)
+        q_z(5)
         finish(3, 1)
-        chan(4, 5, 1, 3, 4)
+        m_row(6, 0, 7)
+        m_row(6, 1, 4)
+        m_row(7, 0, 5)
+        m_row(7, 1, 3)
+        chan(4, 2, 0, 1, 6)
+        z_add(6, 0)
+        z_add(6, 1)
+        z_add(7, 0)
+        z_add(7, 1)
         finish(4, 0)
         finish(4, 1)
-        t_z(6, 2)
-        t_z(7, 7)
+        t_z(6, 7)
+        t_z(7, 4)
         c_z(6)
         c_z(7)
-        chan(5, 6, 0, 5, 1)
+        chan(5, 5, 3, 2, 0)
         q_z(6)
         finish(5, 0)
         q_z(7)
         finish(5, 1)
-        chan(6, 3, 4, 2, 7)
+        chan(6, 1, 6, 7, 4)
         finish(6, 0)
         finish(6, 1)
-        m_chan(7, 2, 6)
+        m_chan(7, 2, 5)
         gate(7, 0)
-        m_chan(7, 0, 0)
+        m_chan(7, 0, 3)
         finish(7, 0)
         for i in range(5):
             if i < 4:
-                m_chan_piece(7, 3, i, (5, 3, 2, 6)[i])
+                m_chan_piece(7, 3, i, (2, 1, 7, 5)[i])
                 gate_piece(7, 1, i)
             if i > 0:
-                m_chan_piece(7, 1, i - 1, (1, 4, 7, 5)[i - 1])
+                m_chan_piece(7, 1, i - 1, (0, 6, 4, 2)[i - 1])
                 finish_piece(7, 1, i - 1)

@@ -132,7 +132,10 @@ def tile_codebook_patch_mixer_t2_kernel(
                         nc.tensor.transpose(tp[:, i, u, :], src, ident[:])
 
         def c_codes(m, b, copy=S):
-            cg[m, b] = ring.tile([P, 2, P, 4], BF16, name="cg%d%d" % (m, b), tag="cg", bufs=5, align_bytes=64)
+            if (m, b) == (7, 1):
+                cg[m, b] = keep.tile([P, 2, P, 4], BF16, name="cg71", tag="eg", align_bytes=64)
+            else:
+                cg[m, b] = ring.tile([P, 2, P, 4], BF16, name="cg%d%d" % (m, b), tag="cg", bufs=5, align_bytes=64)
             copy(out=cg[m, b][:].bitcast(F32), in_=tps[m, b][:].rearrange("p i u m -> p i m u"))
 
         def q_codes(m, b):
@@ -190,7 +193,6 @@ def tile_codebook_patch_mixer_t2_kernel(
             g, t = m // 4, m % 4
             if t == 0:
                 elin[g, h] = ring.tile([P, 4, 512], BF16, name="elin%d%d" % (g, h), tag="elin", bufs=3, align_bytes=64)
-                eg[g, h] = ring.tile([P, 512, 4], BF16, name="eg%d%d" % (g, h), tag="eg", bufs=3, align_bytes=64)
             if on_vector:
                 nc.vector.tensor_scalar(
                     out=elin[g, h][:, t, c0:c1], in0=y[m, h][:, c0:c1], scalar1=gain[:, m : m + 1], scalar2=None, op0=MULT
@@ -198,17 +200,34 @@ def tile_codebook_patch_mixer_t2_kernel(
             else:
                 nc.scalar.activation(out=elin[g, h][:, t, c0:c1], in_=y[m, h][:, c0:c1], func=ACT.Copy, scale=gain[:, m : m + 1])
 
-        def e_inter(g, h, c0, c1, copy):
+        def new_eg(g, h, c0, c1, tag):
+            eg[g, h, c0] = keep.tile([P, c1 - c0, 4], BF16, name="eg%d%d%d" % (g, h, c0), tag=tag, align_bytes=64)
+
+        def e_inter_pool(g, h, c0, c1):
+            new_eg(g, h, c0, c1, "eg")
+            nc.gpsimd.tensor_scalar(
+                out=eg[g, h, c0][:],
+                in0=elin[g, h][:, :, c0:c1].rearrange("p t c -> p c t"),
+                scalar1=1.0,
+                scalar2=1.0,
+                op0=MULT,
+                op1=MULT,
+            )
+
+        def e_inter(g, h, c0, c1, copy, base=None):
+            if base is None:
+                new_eg(g, h, c0, max(c1, c0 + 256), "eg%d%d" % (g, c0))
+                base = c0
             copy(
-                out=eg[g, h][:, c0:c1, :].rearrange("p (c i) t -> p c t i", i=4),
+                out=eg[g, h, base][:, c0 - base : c1 - base, :].rearrange("p (c i) t -> p c t i", i=4),
                 in_=elin[g, h][:, :, c0:c1].rearrange("p t (c i) -> p c t i", i=4),
             )
 
-        def q_e(g, h, c0=0, c1=512):
+        def q_e(g, h, c0, c1):
             nc.vector.quantize_mx(
                 out=eq[g, h][:, c0:c1].bitcast(FP8X4),
                 scales=eqs[g, h][:, c0:c1],
-                in_=eg[g, h][:, c0:c1, :].rearrange("p c t -> p (c t)"),
+                in_=eg[g, h, c0][:].rearrange("p c t -> p (c t)"),
             )
 
         def r_words(m0, m1):
@@ -371,29 +390,31 @@ def tile_codebook_patch_mixer_t2_kernel(
             quant(m + 1)
         m_book(0, 1, 0)
         y_add(6, 0)
-        e_inter(0, 0, 0, 256, V)
+        e_inter_pool(0, 0, 0, 256)
         e_inter(0, 0, 256, 512, S)
         e_scale(6, 0)
         m_book(7, 0, 7)
         ye(0, 1)
-        r_words(4, 6)
         m_book(1, 1, 1)
         ye(7, 0)
-        q_e(0, 0)
+        r_words(4, 6)
+        q_e(0, 0, 256, 512)
+        q_e(0, 0, 0, 256)
         m_book(2, 1, 2)
         y_add(1, 1)
-        e_inter(1, 0, 0, 256, V)
+        e_inter_pool(1, 0, 0, 256)
         e_inter(1, 0, 256, 512, S)
         e_scale(1, 1)
         m_book(3, 1, 3)
         ye(2, 1)
         m_book(4, 1, 4)
         ye(3, 1)
-        q_e(1, 0)
         r_scales(4, 6)
+        q_e(1, 0, 256, 512)
+        q_e(1, 0, 0, 256)
         m_book(5, 1, 5)
         y_add(4, 1)
-        e_inter(0, 1, 0, 256, V)
+        e_inter_pool(0, 1, 0, 256)
         e_inter(0, 1, 256, 512, S)
         e_scale(4, 1)
         m_book(6, 1, 6)
@@ -403,7 +424,8 @@ def tile_codebook_patch_mixer_t2_kernel(
         ye(6, 1)
         y_add_half(7, 1, 0)
         y_add_half(7, 1, 1)
-        q_e(0, 1)
+        q_e(0, 1, 256, 512)
+        q_e(0, 1, 0, 256)
         e_scale(7, 1, False, 0, 256)
         e_scale(7, 1, False, 256, 512)
 
@@ -411,7 +433,7 @@ def tile_codebook_patch_mixer_t2_kernel(
             m_row(m, 0, m)
         e_inter(1, 1, 0, 256, V)
         e_inter(1, 1, 256, 384, V)
-        e_inter(1, 1, 384, 512, S)
+        e_inter(1, 1, 384, 512, S, 256)
         q_e(1, 1, 0, 256)
         q_e(1, 1, 256, 512)
         z_add(0, 0)

@@ -46,8 +46,8 @@ def tile_codebook_patch_mixer_t2_kernel(
         y = {(m, h): kept("y%d%d" % (m, h), [P, 512], F32) for m in range(8) for h in range(2)}
         eq = {(g, h): kept("eq%d%d" % (g, h), [P, 512], U32) for g in range(2) for h in range(2)}
         eqs = {(g, h): kept("eqs%d%d" % (g, h), [P, 512], U8) for g in range(2) for h in range(2)}
-        rr = kept("rr", [P, 2, 2048], U8)
-        rs = kept("rs", [P, 2, 1024], U8)
+        rr = [kept("rr%d" % G, [P, 2, 1024], U8) for G in range(2)]
+        rs = [kept("rs%d" % G, [P, 2, 512], U8) for G in range(2)]
         rp, rps, rcol = {}, {}, {}
         for m0, m1 in R_PARTS:
             rp[m0] = kept("rp%d" % m0, [P, 2 * (m1 - m0) * 256], U8)
@@ -71,7 +71,8 @@ def tile_codebook_patch_mixer_t2_kernel(
         nc.scalar.activation(out=warm[:], in_=warm[:], func=ACT.Tanh)
         make_identity(nc, ident[:])
         clear(bs[1])
-        clear(rs)
+        clear(rs[0])
+        clear(rs[1])
         clear(ws)
 
         codes_v = codes.rearrange("(g p t) j -> g t p j", p=P, t=4)
@@ -98,9 +99,14 @@ def tile_codebook_patch_mixer_t2_kernel(
                 in_=book_words[:, :, h * 1024 : (h + 1) * 1024].bitcast(I32).rearrange("g p b -> p g b"),
             )
 
-        def load_row():
-            nc.sync.dma_start(out=rr[:].bitcast(I32), in_=row_words.bitcast(I32).rearrange("g p b -> p g b"))
-            load_scales(rs, row_scales)
+        def load_row_scales(G):
+            load_scales(rs[G], row_scales[:, :, G * 512 : (G + 1) * 512])
+
+        def load_row_words(G):
+            nc.sync.dma_start(
+                out=rr[G][:].bitcast(I32),
+                in_=row_words[:, :, G * 1024 : (G + 1) * 1024].bitcast(I32).rearrange("g p b -> p g b"),
+            )
 
         def load_chan():
             for h in range(2):
@@ -234,14 +240,14 @@ def tile_codebook_patch_mixer_t2_kernel(
             G, t0, t1 = m0 // 4, m0 % 4, (m1 - 1) % 4 + 1
             nc.vector.tensor_copy(
                 out=rp[m0][:].bitcast(U16).rearrange("p (g t m) -> p g t m", g=2, m=P),
-                in_=rr[:].bitcast(U16).rearrange("p g (G m t) -> p G g t m", G=2, t=4)[:, G, :, t0:t1],
+                in_=rr[G][:].bitcast(U16).rearrange("p g (m t) -> p g t m", t=4)[:, :, t0:t1],
             )
 
         def r_scales(m0, m1):
             G, t0, t1 = m0 // 4, m0 % 4, (m1 - 1) % 4 + 1
             nc.vector.tensor_copy(
                 out=rps[m0][:].rearrange("p (g t m) -> p g t m", g=2, m=P),
-                in_=rs[:].rearrange("p g (G m t) -> p G g t m", G=2, t=4)[:, G, :, t0:t1],
+                in_=rs[G][:].rearrange("p g (m t) -> p g t m", t=4)[:, :, t0:t1],
             )
 
         zacc, zt, ztp, zg, hacc, th = {}, {}, {}, {}, {}, {}
@@ -341,15 +347,21 @@ def tile_codebook_patch_mixer_t2_kernel(
         load_codes(0, 2)
         load_codes(1)
         load_book(0)
-        load_x(0, 0)
-        nc.sync.dma_start(out=gain_raw[:], in_=patch_gain.rearrange("(g p t) -> p g t", p=P, t=4))
         for m in range(2, 8):
             load_codes(m)
-            load_x(m - 1, 0)
-        load_row()
+            load_x(m - 2, 0)
+            if m == 2:
+                nc.sync.dma_start(out=gain_raw[:], in_=patch_gain.rearrange("(g p t) -> p g t", p=P, t=4))
+        load_row_words(0)
+        load_row_scales(0)
         load_book(1)
+        load_x(6, 0)
         load_x(7, 0)
-        for m in range(8):
+        load_x(0, 1)
+        load_x(1, 1)
+        load_row_words(1)
+        load_row_scales(1)
+        for m in range(2, 8):
             load_x(m, 1)
         load_chan()
 
@@ -370,10 +382,11 @@ def tile_codebook_patch_mixer_t2_kernel(
         quant(0)
         turn(1)
         quant(1)
-        nc.vector.tensor_copy(out=gain[:], in_=gain_raw[:].rearrange("p g t -> p (g t)"))
         m_book(0, 0, 4)
         turn(2)
-        ye(0, 0)
+        y_add(0, 0)
+        nc.vector.tensor_copy(out=gain[:], in_=gain_raw[:].rearrange("p g t -> p (g t)"))
+        e_scale(0, 0)
         m_book(1, 0, 5)
         w_codes(3, V)
         quant(2)

@@ -61,14 +61,11 @@ def tile_codebook_patch_mixer_t2_kernel(
         ident = kept("ident", [P, P], F32)
         gain_raw = kept("gain_raw", [P, 2, 4], BF16)
         gain = kept("gain", [P, 8], F32)
-        warm = kept("warm", [P, 1], F32)
 
         def clear(plane):
             nc.vector.memset(plane[:].rearrange("p g n -> p (g n)").bitcast(I32), 0)
 
         clear(bs[0])
-        nc.vector.memset(warm[:], 0.0)
-        nc.scalar.activation(out=warm[:], in_=warm[:], func=ACT.Tanh)
         make_identity(nc, ident[:])
         clear(bs[1])
         clear(rs[0])

@@ -18,7 +18,11 @@ MULT = mybir.AluOpType.mult
 ACT = mybir.ActivationFunctionType
 
 P = 128
-R_PARTS = ((0, 4), (4, 6), (6, 8))
+TILES = 8
+HALF = 512
+SHARE = 256
+ROW_PARTS = ((0, 4), (4, 6), (6, 8))
+UNSORTED = (2, 7)
 
 
 def tile_codebook_patch_mixer_t2_kernel(
@@ -31,512 +35,456 @@ def tile_codebook_patch_mixer_t2_kernel(
         psum = ctx.enter_context(tc.psum_pool(name="psum", bufs=1))
         ctx.enter_context(tc.manual_schedule())
 
-        def kept(name, shape, dt, tag=None):
-            return keep.tile(shape, dt, name=name, tag=tag or name, align_bytes=64)
+        def kept(name, shape, dtype, tag=None):
+            return keep.tile(shape, dtype, name=name, tag=tag or name, align_bytes=64)
 
-        def bank(name, number, shape):
-            return psum.tile(shape, F32, name=name, tag="bank%d" % number)
+        free_banks = list(range(8))
+        bank_of = {}
 
-        craw = [kept("craw%d" % m, [P, 2048], BF16) for m in range(8)]
-        qc = [kept("qc%d" % m, [P, 4 * P], U32) for m in range(8)]
-        qcs = [kept("qcs%d" % m, [P, 4 * P], U8) for m in range(8)]
-        book = [kept("book%d" % h, [P, 4, 1024], U8) for h in range(2)]
-        bs = [kept("bs%d" % h, [P, 4, 512], U8) for h in range(2)]
-        xt = {(m, h): kept("x%d%d" % (m, h), [P, 512], BF16) for m in range(8) for h in range(2)}
-        y = {(m, h): kept("y%d%d" % (m, h), [P, 512], F32) for m in range(8) for h in range(2)}
-        eq = {(g, h): kept("eq%d%d" % (g, h), [P, 512], U32) for g in range(2) for h in range(2)}
-        eqs = {(g, h): kept("eqs%d%d" % (g, h), [P, 512], U8) for g in range(2) for h in range(2)}
-        rr = [kept("rr%d" % G, [P, 2, 1024], U8) for G in range(2)]
-        rs = [kept("rs%d" % G, [P, 2, 512], U8) for G in range(2)]
-        rp, rps, rcol = {}, {}, {}
-        for m0, m1 in R_PARTS:
-            rp[m0] = kept("rp%d" % m0, [P, 2 * (m1 - m0) * 256], U8)
-            rps[m0] = kept("rps%d" % m0, [P, 2 * (m1 - m0) * P], U8)
-            for m in range(m0, m1):
-                rcol[m] = (m0, [(g * (m1 - m0) + m - m0) * P for g in range(2)])
-        wt = [kept("wt%d" % g, [P, 4096], U8) for g in range(2)]
-        ws = kept("ws", [P, 2, 2048], U8)
-        zq = [kept("zq%d" % m, [P, 2 * P], U32) for m in range(8)]
-        zqs = [kept("zqs%d" % m, [P, 2 * P], U8) for m in range(8)]
+        def take_bank(name, shape):
+            bank_of[name] = free_banks[0]
+            free_banks.remove(bank_of[name])
+            return psum.tile(shape, F32, name=name, tag="bank%d" % bank_of[name])
+
+        def give_bank(name):
+            free_banks.append(bank_of[name])
+
+        halves = [(m, h) for m in range(TILES) for h in range(2)]
+        groups = [(g, h) for g in range(2) for h in range(2)]
+        codes_raw = [kept("codes_raw%d" % m, [P, 2048], BF16) for m in range(TILES)]
+        codes_q = [kept("codes_q%d" % m, [P, 4 * P], U32) for m in range(TILES)]
+        codes_s = [kept("codes_s%d" % m, [P, 4 * P], U8) for m in range(TILES)]
+        book_w = [kept("book_w%d" % h, [P, 4, 2 * HALF], U8) for h in range(2)]
+        book_s = [kept("book_s%d" % h, [P, 4, HALF], U8) for h in range(2)]
+        x_sb = {(m, h): kept("x%d%d" % (m, h), [P, HALF], BF16) for m, h in halves}
+        y_sb = {(m, h): kept("y%d%d" % (m, h), [P, HALF], F32) for m, h in halves}
+        e_q = {(g, h): kept("e_q%d%d" % (g, h), [P, HALF], U32) for g, h in groups}
+        e_s = {(g, h): kept("e_s%d%d" % (g, h), [P, HALF], U8) for g, h in groups}
+        row_w_raw = [kept("row_w_raw%d" % g, [P, 2, 2 * HALF], U8) for g in range(2)]
+        row_s_raw = [kept("row_s_raw%d" % g, [P, 2, HALF], U8) for g in range(2)]
+        row_w, row_s, row_at = {}, {}, {}
+        for part in ROW_PARTS:
+            width = part[1] - part[0]
+            row_w[part] = kept("row_w%d" % part[0], [P, 2 * width * 2 * P], U8)
+            row_s[part] = kept("row_s%d" % part[0], [P, 2 * width * P], U8)
+            for m in range(*part):
+                row_at[m] = (part, [(g * width + m - part[0]) * P for g in range(2)])
+        chan_w = [kept("chan_w%d" % h, [P, 4096], U8) for h in range(2)]
+        chan_s = kept("chan_s", [P, 2, 2048], U8)
+        z_q = [kept("z_q%d" % m, [P, 2 * P], U32) for m in range(TILES)]
+        z_s = [kept("z_s%d" % m, [P, 2 * P], U8) for m in range(TILES)]
         ident = kept("ident", [P, P], F32)
         gain_raw = kept("gain_raw", [P, 2, 4], BF16)
-        gain = kept("gain", [P, 8], F32)
+        gain = kept("gain", [P, TILES], F32)
 
         def clear(plane):
             nc.vector.memset(plane[:].rearrange("p g n -> p (g n)").bitcast(I32), 0)
 
-        clear(bs[0])
+        clear(book_s[0])
         make_identity(nc, ident[:])
-        clear(bs[1])
-        clear(rs[0])
-        clear(rs[1])
-        clear(ws)
+        clear(book_s[1])
+        clear(row_s_raw[0])
+        clear(row_s_raw[1])
+        clear(chan_s)
 
         codes_v = codes.rearrange("(g p t) j -> g t p j", p=P, t=4)
         x_v = x.rearrange("(g p t) c -> g t p c", p=P, t=4)
         out_v = out.rearrange("(g p t) c -> g t p c", p=P, t=4)
 
         def load_codes(m, parts=1):
-            w = 2048 // parts
+            width = 2048 // parts
             for i in range(parts):
-                nc.sync.dma_start(out=craw[m][:, i * w : (i + 1) * w], in_=codes_v[m // 4, m % 4][:, i * w : (i + 1) * w])
+                cols = slice(i * width, (i + 1) * width)
+                nc.sync.dma_start(out=codes_raw[m][:, cols], in_=codes_v[m // 4, m % 4][:, cols])
 
         def load_x(m, h):
-            nc.sync.dma_start(out=xt[m, h][:], in_=x_v[m // 4, m % 4][:, h * 512 : (h + 1) * 512])
+            nc.sync.dma_start(out=x_sb[m, h][:], in_=x_v[m // 4, m % 4][:, h * HALF : (h + 1) * HALF])
 
-        def load_scales(plane, src):
-            dst = plane[:].bitcast(I32)
+        def load_words(tile, words):
+            nc.sync.dma_start(out=tile[:].bitcast(I32), in_=words.bitcast(I32).rearrange("g p b -> p g b"))
+
+        def load_scales(plane, scales):
+            rows = plane[:].bitcast(I32)
             for r in range(4):
-                nc.sync.dma_start(out=dst[r:P:32], in_=src.rearrange("g (q r) n -> r q g n", r=4)[r].bitcast(I32))
+                nc.sync.dma_start(out=rows[r:P:32], in_=scales.rearrange("g (q r) n -> r q g n", r=4)[r].bitcast(I32))
 
-        def load_book(h):
-            load_scales(bs[h], book_scales[:, :, h * 512 : (h + 1) * 512])
-            nc.sync.dma_start(
-                out=book[h][:].bitcast(I32),
-                in_=book_words[:, :, h * 1024 : (h + 1) * 1024].bitcast(I32).rearrange("g p b -> p g b"),
-            )
+        def word_cols(h):
+            return slice(h * 2 * HALF, (h + 1) * 2 * HALF)
 
-        def load_row_scales(G):
-            load_scales(rs[G], row_scales[:, :, G * 512 : (G + 1) * 512])
+        def scale_cols(h):
+            return slice(h * HALF, (h + 1) * HALF)
 
-        def load_row_words(G):
-            nc.sync.dma_start(
-                out=rr[G][:].bitcast(I32),
-                in_=row_words[:, :, G * 1024 : (G + 1) * 1024].bitcast(I32).rearrange("g p b -> p g b"),
-            )
+        sorted_words, turned, grouped, sums = {}, {}, {}, {}
 
-        def load_chan():
-            for h in range(2):
-                nc.sync.dma_start(out=wt[h][:].bitcast(I32), in_=chan_words[h].bitcast(I32))
-            load_scales(ws, chan_scales)
-
-        V, S = nc.vector.tensor_copy, nc.scalar.copy
-
-        cw, tps, cg, accs = {}, {}, {}, {}
-
-        def w_codes(m, copy, parts=1):
-            cw[m] = ring.tile([P, 4, 2, P], F32, name="cw%d" % m, tag="cw", bufs=2)
-            w = 4 // parts
+        def sort_codes(m, parts=1):
+            sorted_words[m] = ring.tile([P, 4, 2, P], F32, name="sorted%d" % m, tag="sorted", bufs=2)
+            width = 4 // parts
             for i in range(parts):
-                copy(
-                    out=cw[m][:, i * w : (i + 1) * w],
-                    in_=craw[m][:, i * w * 512 : (i + 1) * w * 512].bitcast(F32).rearrange("p (g q u) -> p g u q", g=w, u=2),
+                raw = codes_raw[m][:, i * width * 512 : (i + 1) * width * 512].bitcast(F32)
+                nc.vector.tensor_copy(
+                    out=sorted_words[m][:, i * width : (i + 1) * width],
+                    in_=raw.rearrange("p (g q u) -> p g u q", g=width, u=2),
                 )
 
-        def t_codes(m):
-            words = craw[m][:].bitcast(F32)
+        def turn_codes(m):
+            words = codes_raw[m][:].bitcast(F32)
             for b in range(2):
-                tp = bank("T%d%d" % (m, b), 2 * (m % 2) + b, [P, 2, 2, P])
-                tps[m, b] = tp
+                turned[b] = take_bank("turn%d%d" % (m, b), [P, 2, 2, P])
                 for i in range(2):
+                    g = 2 * b + i
                     for u in range(2):
-                        w0 = 256 * (2 * b + i)
-                        src = cw[m][:, 2 * b + i, u, :] if m in cw else words[:, w0 + u : w0 + 256 : 2]
-                        nc.tensor.transpose(tp[:, i, u, :], src, ident[:])
+                        if m in UNSORTED:
+                            source = words[:, 256 * g + u : 256 * (g + 1) : 2]
+                        else:
+                            source = sorted_words[m][:, g, u, :]
+                        nc.tensor.transpose(turned[b][:, i, u, :], source, ident[:])
+            for b in range(2):
+                if (m, b) == (TILES - 1, 1):
+                    grouped[m, b] = kept("grouped_last", [P, 2, P, 4], BF16, tag="pool_out")
+                else:
+                    grouped[m, b] = ring.tile(
+                        [P, 2, P, 4], BF16, name="grouped%d%d" % (m, b), tag="grouped", bufs=5, align_bytes=64
+                    )
+                nc.scalar.copy(out=grouped[m, b][:].bitcast(F32), in_=turned[b][:].rearrange("p i u m -> p i m u"))
+                give_bank("turn%d%d" % (m, b))
 
-        def c_codes(m, b, copy=S):
-            if (m, b) == (7, 1):
-                cg[m, b] = keep.tile([P, 2, P, 4], BF16, name="cg71", tag="eg", align_bytes=64)
-            else:
-                cg[m, b] = ring.tile([P, 2, P, 4], BF16, name="cg%d%d" % (m, b), tag="cg", bufs=5, align_bytes=64)
-            copy(out=cg[m, b][:].bitcast(F32), in_=tps[m, b][:].rearrange("p i u m -> p i m u"))
+        def quantize_codes(m):
+            for b in range(2):
+                cols = slice(b * 2 * P, (b + 1) * 2 * P)
+                nc.vector.quantize_mx(
+                    out=codes_q[m][:, cols].bitcast(FP8X4),
+                    scales=codes_s[m][:, cols],
+                    in_=grouped[m, b][:].rearrange("p g m t -> p (g m t)"),
+                )
 
-        def q_codes(m, b):
-            cols = slice(b * 256, (b + 1) * 256)
-            nc.vector.quantize_mx(
-                out=qc[m][:, cols].bitcast(FP8X4),
-                scales=qcs[m][:, cols],
-                in_=cg[m, b][:].rearrange("p g m t -> p (g m t)"),
-            )
-
-        def m_book(m, h, number):
-            acc = bank("A%d%d" % (m, h), number, [P, 512])
-            accs[m, h] = acc
+        def book_passes(acc, m, h, c0, width):
             for g in range(4):
                 nc.tensor.matmul_mx(
-                    out=acc[:],
-                    lhsT=qc[m][:, g * P : (g + 1) * P].bitcast(FP8X4),
-                    lhsT_scale=qcs[m][:, g * P : (g + 1) * P],
-                    rhs=book[h][:, g, :].bitcast(FP4X4),
-                    rhs_scale=bs[h][:, g, :],
+                    out=acc,
+                    lhsT=codes_q[m][:, g * P : (g + 1) * P].bitcast(FP8X4),
+                    lhsT_scale=codes_s[m][:, g * P : (g + 1) * P],
+                    rhs=book_w[h][:, g, 2 * c0 : 2 * (c0 + width)].bitcast(FP4X4),
+                    rhs_scale=book_s[h][:, g, c0 : c0 + width],
                     start=(g == 0),
                     stop=(g == 3),
                 )
 
-        def m_book_half(m, h, j, number):
-            acc = bank("a%d%d" % (m, j), number, [P, 256])
-            accs[m, h, j] = acc
-            for i in range(2):
-                c0 = j * 256 + i * P
-                for g in range(4):
-                    nc.tensor.matmul_mx(
-                        out=acc[:, i * P : (i + 1) * P],
-                        lhsT=qc[m][:, g * P : (g + 1) * P].bitcast(FP8X4),
-                        lhsT_scale=qcs[m][:, g * P : (g + 1) * P],
-                        rhs=book[h][:, g, 2 * c0 : 2 * (c0 + P)].bitcast(FP4X4),
-                        rhs_scale=bs[h][:, g, c0 : c0 + P],
-                        start=(g == 0),
-                        stop=(g == 3),
-                    )
+        def book_product(m, h):
+            sums[m, h, 0] = take_bank("book%d%d0" % (m, h), [P, HALF])
+            book_passes(sums[m, h, 0][:], m, h, 0, HALF)
 
-        def y_add_half(m, h, j):
-            c0, c1 = j * 256, (j + 1) * 256
-            nc.vector.tensor_tensor(
-                out=y[m, h][:, c0:c1], in0=accs[m, h, j][:], in1=xt[m, h][:, c0:c1], op=ADD
-            )
+        def book_product_share(m, h, c0):
+            sums[m, h, c0] = take_bank("book%d%d%d" % (m, h, c0), [P, SHARE])
+            for i in range(0, SHARE, P):
+                book_passes(sums[m, h, c0][:, i : i + P], m, h, c0 + i, P)
 
-        def y_add(m, h, c0=0, c1=512):
-            nc.vector.tensor_tensor(
-                out=y[m, h][:, c0:c1], in0=accs[m, h][:, c0:c1], in1=xt[m, h][:, c0:c1], op=ADD
-            )
+        def add_x(m, h, c0=0, c1=HALF):
+            nc.vector.tensor_tensor(out=y_sb[m, h][:, c0:c1], in0=sums[m, h, c0][:], in1=x_sb[m, h][:, c0:c1], op=ADD)
+            give_bank("book%d%d%d" % (m, h, c0))
 
-        elin, eg = {}, {}
+        e_rows, e_words = {}, {}
 
-        def e_scale(m, h, on_vector=False, c0=0, c1=512):
+        def scale_y(m, h, c0=0, c1=HALF):
             g, t = m // 4, m % 4
             if t == 0:
-                elin[g, h] = ring.tile([P, 4, 512], BF16, name="elin%d%d" % (g, h), tag="elin", bufs=3, align_bytes=64)
-            if on_vector:
-                nc.vector.tensor_scalar(
-                    out=elin[g, h][:, t, c0:c1], in0=y[m, h][:, c0:c1], scalar1=gain[:, m : m + 1], scalar2=None, op0=MULT
-                )
-            else:
-                nc.scalar.activation(out=elin[g, h][:, t, c0:c1], in_=y[m, h][:, c0:c1], func=ACT.Copy, scale=gain[:, m : m + 1])
+                e_rows[g, h] = ring.tile([P, 4, HALF], BF16, name="e_rows%d%d" % (g, h), tag="e_rows", bufs=3, align_bytes=64)
+            nc.scalar.activation(
+                out=e_rows[g, h][:, t, c0:c1], in_=y_sb[m, h][:, c0:c1], func=ACT.Copy, scale=gain[:, m : m + 1]
+            )
 
-        def new_eg(g, h, c0, c1, tag):
-            eg[g, h, c0] = keep.tile([P, c1 - c0, 4], BF16, name="eg%d%d%d" % (g, h, c0), tag=tag, align_bytes=64)
+        def finish_y(m, h):
+            add_x(m, h)
+            scale_y(m, h)
 
-        def e_inter_pool(g, h, c0, c1):
-            new_eg(g, h, c0, c1, "eg")
+        def new_e_words(g, h, share, tag):
+            e_words[g, h, share] = kept("e_words%d%d%d" % (g, h, share), [P, SHARE, 4], BF16, tag=tag)
+
+        def interleave(copy, g, h, c0, c1):
+            share, first = c0 // SHARE, c0 % SHARE
+            copy(
+                out=e_words[g, h, share][:, first : first + c1 - c0, :].rearrange("p (c i) t -> p c t i", i=4),
+                in_=e_rows[g, h][:, :, c0:c1].rearrange("p t (c i) -> p c t i", i=4),
+            )
+
+        def interleave_shared(g, h):
+            new_e_words(g, h, 0, "pool_out")
             nc.gpsimd.tensor_scalar(
-                out=eg[g, h, c0][:],
-                in0=elin[g, h][:, :, c0:c1].rearrange("p t c -> p c t"),
+                out=e_words[g, h, 0][:],
+                in0=e_rows[g, h][:, :, 0:SHARE].rearrange("p t c -> p c t"),
                 scalar1=1.0,
                 scalar2=1.0,
                 op0=MULT,
                 op1=MULT,
             )
+            new_e_words(g, h, 1, "e_words%d1" % g)
+            interleave(nc.scalar.copy, g, h, SHARE, HALF)
 
-        def e_inter(g, h, c0, c1, copy, base=None):
-            if base is None:
-                new_eg(g, h, c0, max(c1, c0 + 256), "eg%d%d" % (g, c0))
-                base = c0
-            copy(
-                out=eg[g, h, base][:, c0 - base : c1 - base, :].rearrange("p (c i) t -> p c t i", i=4),
-                in_=elin[g, h][:, :, c0:c1].rearrange("p t (c i) -> p c t i", i=4),
-            )
-
-        def q_e(g, h, c0, c1):
-            nc.vector.quantize_mx(
-                out=eq[g, h][:, c0:c1].bitcast(FP8X4),
-                scales=eqs[g, h][:, c0:c1],
-                in_=eg[g, h, c0][:].rearrange("p c t -> p (c t)"),
-            )
-
-        def r_words(m0, m1):
-            G, t0, t1 = m0 // 4, m0 % 4, (m1 - 1) % 4 + 1
-            nc.vector.tensor_copy(
-                out=rp[m0][:].bitcast(U16).rearrange("p (g t m) -> p g t m", g=2, m=P),
-                in_=rr[G][:].bitcast(U16).rearrange("p g (m t) -> p g t m", t=4)[:, :, t0:t1],
-            )
-
-        def r_scales(m0, m1):
-            G, t0, t1 = m0 // 4, m0 % 4, (m1 - 1) % 4 + 1
-            nc.vector.tensor_copy(
-                out=rps[m0][:].rearrange("p (g t m) -> p g t m", g=2, m=P),
-                in_=rs[G][:].rearrange("p g (m t) -> p g t m", t=4)[:, :, t0:t1],
-            )
-
-        zacc, zt, ztp, zg, hacc, th = {}, {}, {}, {}, {}, {}
-
-        def m_row(m, h, number, groups=(0, 1)):
-            if 0 in groups:
-                zacc[m, h] = bank("B%d%d" % (m, h), number, [P, 512])
-            acc = zacc[m, h]
-            for g in groups:
-                nc.tensor.matmul_mx(
-                    out=acc[:],
-                    lhsT=rp[rcol[m][0]][:, 2 * rcol[m][1][g] : 2 * (rcol[m][1][g] + P)].bitcast(FP4X4),
-                    lhsT_scale=rps[rcol[m][0]][:, rcol[m][1][g] : rcol[m][1][g] + P],
-                    rhs=eq[g, h][:].bitcast(FP8X4),
-                    rhs_scale=eqs[g, h][:],
-                    start=(g == 0),
-                    stop=(g == 1),
+        def quantize_e(g, h, shares):
+            for share in shares:
+                cols = slice(share * SHARE, (share + 1) * SHARE)
+                nc.vector.quantize_mx(
+                    out=e_q[g, h][:, cols].bitcast(FP8X4),
+                    scales=e_s[g, h][:, cols],
+                    in_=e_words[g, h, share][:].rearrange("p c t -> p (c t)"),
                 )
 
-        def z_add(m, h):
+        def deal_row_words(part):
+            t0, t1 = part[0] % 4, (part[1] - 1) % 4 + 1
+            nc.vector.tensor_copy(
+                out=row_w[part][:].bitcast(U16).rearrange("p (g t m) -> p g t m", g=2, m=P),
+                in_=row_w_raw[part[0] // 4][:].bitcast(U16).rearrange("p g (m t) -> p g t m", t=4)[:, :, t0:t1],
+            )
+
+        def deal_row_scales(part):
+            t0, t1 = part[0] % 4, (part[1] - 1) % 4 + 1
+            nc.vector.tensor_copy(
+                out=row_s[part][:].rearrange("p (g t m) -> p g t m", g=2, m=P),
+                in_=row_s_raw[part[0] // 4][:].rearrange("p g (m t) -> p g t m", t=4)[:, :, t0:t1],
+            )
+
+        mixed, z_sb, z_turned, z_grouped = {}, {}, {}, {}
+
+        def row_pass(m, h, g):
+            if g == 0:
+                mixed[m, h] = take_bank("row%d%d" % (m, h), [P, HALF])
+            part, at = row_at[m]
+            nc.tensor.matmul_mx(
+                out=mixed[m, h][:],
+                lhsT=row_w[part][:, 2 * at[g] : 2 * (at[g] + P)].bitcast(FP4X4),
+                lhsT_scale=row_s[part][:, at[g] : at[g] + P],
+                rhs=e_q[g, h][:].bitcast(FP8X4),
+                rhs_scale=e_s[g, h][:],
+                start=(g == 0),
+                stop=(g == 1),
+            )
+
+        def row_product(m, h):
+            for g in range(2):
+                row_pass(m, h, g)
+
+        def add_y(m, h):
             if h == 0:
-                zt[m] = kept("z%d" % m, [P, 1024], BF16, tag="craw%d" % m)
+                z_sb[m] = kept("z%d" % m, [P, 2 * HALF], BF16, tag="codes_raw%d" % m)
             nc.vector.tensor_tensor(
-                out=zt[m][:, h * 512 : (h + 1) * 512].rearrange("p (u q e) -> p u q e", u=2, e=2),
-                in0=zacc[m, h][:].rearrange("p (q u e) -> p u q e", u=2, e=2),
-                in1=y[m, h][:].rearrange("p (q u e) -> p u q e", u=2, e=2),
+                out=z_sb[m][:, h * HALF : (h + 1) * HALF].rearrange("p (u q e) -> p u q e", u=2, e=2),
+                in0=mixed[m, h][:].rearrange("p (q u e) -> p u q e", u=2, e=2),
+                in1=y_sb[m, h][:].rearrange("p (q u e) -> p u q e", u=2, e=2),
                 op=ADD,
             )
+            give_bank("row%d%d" % (m, h))
 
-        def t_z(m, number):
-            tp = bank("U%d" % m, number, [P, 2, 2, P])
-            ztp[m] = tp
-            words = zt[m][:].bitcast(F32)
+        def turn_z(m):
+            z_turned[m] = take_bank("turn_z%d" % m, [P, 2, 2, P])
+            words = z_sb[m][:].bitcast(F32)
             for h in range(2):
                 for u in range(2):
-                    nc.tensor.transpose(tp[:, h, u, :], words[:, (2 * h + u) * P : (2 * h + u + 1) * P], ident[:])
+                    run = slice((2 * h + u) * P, (2 * h + u + 1) * P)
+                    nc.tensor.transpose(z_turned[m][:, h, u, :], words[:, run], ident[:])
 
-        def c_z(m):
-            zg[m] = ring.tile([P, 2, P, 4], BF16, name="zg%d" % m, tag="cg", bufs=5, align_bytes=64)
-            nc.scalar.copy(out=zg[m][:].bitcast(F32), in_=ztp[m][:].rearrange("p i u m -> p i m u"))
-
-        def q_z(m):
-            nc.vector.quantize_mx(
-                out=zq[m][:].bitcast(FP8X4), scales=zqs[m][:], in_=zg[m][:].rearrange("p i m t -> p (i m t)")
-            )
-
-        def m_chan(m, n, number):
-            acc = bank("H%d%d" % (m, n), number, [P, 512])
-            hacc[m, n] = acc
-            for h in range(2):
-                nc.tensor.matmul_mx(
-                    out=acc[:],
-                    lhsT=zq[m][:, h * P : (h + 1) * P].bitcast(FP8X4),
-                    lhsT_scale=zqs[m][:, h * P : (h + 1) * P],
-                    rhs=wt[h][:, n * 1024 : (n + 1) * 1024].bitcast(FP4X4),
-                    rhs_scale=ws[:, h, n * 512 : (n + 1) * 512],
-                    start=(h == 0),
-                    stop=(h == 1),
-                )
-
-        def m_chan_piece(m, n, i, number):
-            acc = bank("L%d%d" % (n, i), number, [P, P])
-            hacc[m, n, i] = acc
-            for h in range(2):
-                nc.tensor.matmul_mx(
-                    out=acc[:],
-                    lhsT=zq[m][:, h * P : (h + 1) * P].bitcast(FP8X4),
-                    lhsT_scale=zqs[m][:, h * P : (h + 1) * P],
-                    rhs=wt[h][:, n * 1024 + i * 256 : n * 1024 + (i + 1) * 256].bitcast(FP4X4),
-                    rhs_scale=ws[:, h, n * 512 + i * P : n * 512 + (i + 1) * P],
-                    start=(h == 0),
-                    stop=(h == 1),
-                )
-
-        def gate_piece(m, n, i):
-            th[m, n, i] = ring.tile([P, P], F32, name="tp%d" % i, tag="tp", bufs=4)
-            nc.scalar.activation(out=th[m, n, i][:], in_=hacc[m, n + 2, i][:], func=ACT.Tanh)
-
-        def finish_piece(m, n, i):
-            ot = ring.tile([P, P], F32, name="op%d" % i, tag="op", bufs=4)
-            nc.vector.tensor_tensor(out=ot[:], in0=hacc[m, n, i][:], in1=th[m, n, i][:], op=MULT)
-            nc.sync.dma_start(out=out_v[m // 4, m % 4][:, n * 512 + i * P : n * 512 + (i + 1) * P], in_=ot[:])
-
-        def gate(m, n):
-            th[m, n] = ring.tile([P, 512], F32, name="th%d%d" % (m, n), tag="th", bufs=3)
-            nc.scalar.activation(out=th[m, n][:], in_=hacc[m, n + 2][:], func=ACT.Tanh)
-
-        def finish(m, n, parts=1):
-            ot = ring.tile([P, 512], F32, name="ot%d%d" % (m, n), tag="ot", bufs=5)
-            w = 512 // parts
+        def group_z(m, parts=1):
+            z_grouped[m] = ring.tile([P, 2, P, 4], BF16, name="z_grouped%d" % m, tag="grouped", bufs=5, align_bytes=64)
             for i in range(parts):
-                sl = slice(i * w, (i + 1) * w)
-                nc.vector.tensor_tensor(out=ot[:, sl], in0=hacc[m, n][:, sl], in1=th[m, n][:, sl], op=MULT)
-                nc.sync.dma_start(out=out_v[m // 4, m % 4][:, n * 512 + i * w : n * 512 + (i + 1) * w], in_=ot[:, sl])
+                passes = slice(2 * i // parts, 2 * (i + 1) // parts)
+                nc.scalar.copy(
+                    out=z_grouped[m][:, passes].bitcast(F32), in_=z_turned[m][:, passes].rearrange("p h u m -> p h m u")
+                )
+            give_bank("turn_z%d" % m)
 
+        def quantize_z(m, parts=1):
+            for i in range(parts):
+                passes = slice(2 * i // parts, 2 * (i + 1) // parts)
+                cols = slice(passes.start * P, passes.stop * P)
+                nc.vector.quantize_mx(
+                    out=z_q[m][:, cols].bitcast(FP8X4),
+                    scales=z_s[m][:, cols],
+                    in_=z_grouped[m][:, passes].rearrange("p h m t -> p (h m t)"),
+                )
 
-        load_codes(0, 2)
+        h_sums, gates = {}, {}
+
+        def chan_product(m, c0, width):
+            h_sums[m, c0] = take_bank("chan%d_%d" % (m, c0), [P, width])
+            group = HALF if width == HALF else P
+            for i in range(0, width, group):
+                for h in range(2):
+                    nc.tensor.matmul_mx(
+                        out=h_sums[m, c0][:, i : i + group],
+                        lhsT=z_q[m][:, h * P : (h + 1) * P].bitcast(FP8X4),
+                        lhsT_scale=z_s[m][:, h * P : (h + 1) * P],
+                        rhs=chan_w[h][:, 2 * (c0 + i) : 2 * (c0 + i + group)].bitcast(FP4X4),
+                        rhs_scale=chan_s[:, h, c0 + i : c0 + i + group],
+                        start=(h == 0),
+                        stop=(h == 1),
+                    )
+
+        def gate_product(m, c0, width):
+            chan_product(m, 2 * HALF + c0, width)
+            gates[m, c0] = ring.tile(
+                [P, width], F32, name="gate%d_%d" % (m, c0), tag="gate%d" % width, bufs=3 if width == HALF else 4
+            )
+            nc.scalar.activation(out=gates[m, c0][:], in_=h_sums[m, 2 * HALF + c0][:], func=ACT.Tanh)
+            give_bank("chan%d_%d" % (m, 2 * HALF + c0))
+
+        def store_product(m, c0, width):
+            result = ring.tile(
+                [P, width], F32, name="result%d_%d" % (m, c0), tag="result%d" % width, bufs=5 if width == HALF else 4
+            )
+            nc.vector.tensor_tensor(out=result[:], in0=h_sums[m, c0][:], in1=gates[m, c0][:], op=MULT)
+            give_bank("chan%d_%d" % (m, c0))
+            nc.sync.dma_start(out=out_v[m // 4, m % 4][:, c0 : c0 + width], in_=result[:])
+
+        def out_half(m, n):
+            gate_product(m, n * HALF, HALF)
+            chan_product(m, n * HALF, HALF)
+            store_product(m, n * HALF, HALF)
+
+        load_codes(0, parts=2)
         load_codes(1)
-        load_book(0)
-        for m in range(2, 8):
+        load_scales(book_s[0], book_scales[:, :, scale_cols(0)])
+        load_words(book_w[0], book_words[:, :, word_cols(0)])
+        for m in range(2, TILES):
             load_codes(m)
             load_x(m - 2, 0)
             if m == 2:
                 nc.sync.dma_start(out=gain_raw[:], in_=patch_gain.rearrange("(g p t) -> p g t", p=P, t=4))
-        load_row_words(0)
-        load_row_scales(0)
-        load_book(1)
+        load_words(row_w_raw[0], row_words[:, :, word_cols(0)])
+        load_scales(row_s_raw[0], row_scales[:, :, scale_cols(0)])
+        load_words(book_w[1], book_words[:, :, word_cols(1)])
+        load_scales(book_s[1], book_scales[:, :, scale_cols(1)])
         load_x(6, 0)
         load_x(7, 0)
         load_x(0, 1)
+        load_words(row_w_raw[1], row_words[:, :, word_cols(1)])
         load_x(1, 1)
-        load_row_words(1)
-        load_row_scales(1)
-        for m in range(2, 8):
+        load_scales(row_s_raw[1], row_scales[:, :, scale_cols(1)])
+        for m in range(2, TILES):
             load_x(m, 1)
-        load_chan()
+        for h in range(2):
+            nc.sync.dma_start(out=chan_w[h][:].bitcast(I32), in_=chan_words[h].bitcast(I32))
+        load_scales(chan_s, chan_scales)
 
-        def turn(m):
-            t_codes(m)
-            c_codes(m, 0)
-            c_codes(m, 1)
-        def quant(m):
-            q_codes(m, 0)
-            q_codes(m, 1)
-        def ye(m, h):
-            y_add(m, h)
-            e_scale(m, h)
+        sort_codes(0, parts=2)
+        turn_codes(0)
+        sort_codes(1)
+        quantize_codes(0)
+        turn_codes(1)
+        quantize_codes(1)
 
-        w_codes(0, V, 2)
-        turn(0)
-        w_codes(1, V)
-        quant(0)
-        turn(1)
-        quant(1)
-        m_book(0, 0, 4)
-        turn(2)
-        y_add(0, 0)
+        book_product(0, 0)
+        turn_codes(2)
+        add_x(0, 0)
         nc.vector.tensor_copy(out=gain[:], in_=gain_raw[:].rearrange("p g t -> p (g t)"))
-        e_scale(0, 0)
-        m_book(1, 0, 5)
-        w_codes(3, V)
-        quant(2)
-        for m in range(2, 7):
-            turn(m + 1)
-            ye(m - 1, 0)
-            m_book(m, 0, 4 + m % 4)
-            if m + 2 <= 6:
-                w_codes(m + 2, V)
-            if m == 5:
-                r_words(0, 4)
-            if m == 6:
-                r_scales(0, 4)
-            quant(m + 1)
-        m_book(0, 1, 0)
-        y_add(6, 0)
-        e_inter_pool(0, 0, 0, 256)
-        e_inter(0, 0, 256, 512, S)
-        e_scale(6, 0)
-        m_book(7, 0, 7)
-        ye(0, 1)
-        m_book(1, 1, 1)
-        ye(7, 0)
-        r_words(4, 6)
-        q_e(0, 0, 256, 512)
-        q_e(0, 0, 0, 256)
-        m_book(2, 1, 2)
-        y_add(1, 1)
-        e_inter_pool(1, 0, 0, 256)
-        e_inter(1, 0, 256, 512, S)
-        e_scale(1, 1)
-        m_book(3, 1, 3)
-        ye(2, 1)
-        m_book(4, 1, 4)
-        ye(3, 1)
-        r_scales(4, 6)
-        q_e(1, 0, 256, 512)
-        q_e(1, 0, 0, 256)
-        m_book(5, 1, 5)
-        y_add(4, 1)
-        e_inter_pool(0, 1, 0, 256)
-        e_inter(0, 1, 256, 512, S)
-        e_scale(4, 1)
-        m_book(6, 1, 6)
-        ye(5, 1)
-        m_book_half(7, 1, 0, 7)
-        m_book_half(7, 1, 1, 4)
-        ye(6, 1)
-        y_add_half(7, 1, 0)
-        y_add_half(7, 1, 1)
-        q_e(0, 1, 256, 512)
-        q_e(0, 1, 0, 256)
-        e_scale(7, 1, False, 0, 256)
-        e_scale(7, 1, False, 256, 512)
+        scale_y(0, 0)
+        book_product(1, 0)
+        sort_codes(3)
+        quantize_codes(2)
+        for m in range(2, TILES - 1):
+            turn_codes(m + 1)
+            finish_y(m - 1, 0)
+            book_product(m, 0)
+            if m + 2 < TILES - 1:
+                sort_codes(m + 2)
+            elif m + 2 == TILES - 1:
+                deal_row_words(ROW_PARTS[0])
+            else:
+                deal_row_scales(ROW_PARTS[0])
+            quantize_codes(m + 1)
 
-        for m in range(4):
-            m_row(m, 0, m)
-        e_inter(1, 1, 0, 256, V)
-        e_inter(1, 1, 256, 384, V)
-        e_inter(1, 1, 384, 512, S, 256)
-        q_e(1, 1, 0, 256)
-        q_e(1, 1, 256, 512)
-        z_add(0, 0)
-        m_row(4, 0, 7)
+        book_product(0, 1)
+        add_x(6, 0)
+        interleave_shared(0, 0)
+        scale_y(6, 0)
+        book_product(7, 0)
+        finish_y(0, 1)
+        book_product(1, 1)
+        finish_y(7, 0)
+        deal_row_words(ROW_PARTS[1])
+        quantize_e(0, 0, (1, 0))
+        book_product(2, 1)
+        add_x(1, 1)
+        interleave_shared(1, 0)
+        scale_y(1, 1)
+        for m in (3, 4):
+            book_product(m, 1)
+            finish_y(m - 1, 1)
+        deal_row_scales(ROW_PARTS[1])
+        quantize_e(1, 0, (1, 0))
+        book_product(5, 1)
+        add_x(4, 1)
+        interleave_shared(0, 1)
+        scale_y(4, 1)
+        book_product(6, 1)
+        finish_y(5, 1)
+
+        for c0 in (0, SHARE):
+            book_product_share(7, 1, c0)
+        finish_y(6, 1)
+        for c0 in (0, SHARE):
+            add_x(7, 1, c0, c0 + SHARE)
+        quantize_e(0, 1, (1, 0))
+        for c0 in (0, SHARE):
+            scale_y(7, 1, c0, c0 + SHARE)
+
+        for m in range(5):
+            row_product(m, 0)
+        for share in range(2):
+            new_e_words(1, 1, share, "e_words1%d" % share)
+        interleave(nc.vector.tensor_copy, 1, 1, 0, SHARE)
+        interleave(nc.vector.tensor_copy, 1, 1, SHARE, SHARE + P)
+        interleave(nc.scalar.copy, 1, 1, SHARE + P, HALF)
+        quantize_e(1, 1, (0, 1))
         for g in range(2):
-            m_row(0, 1, 5, (g,))
-            m_row(1, 1, 6, (g,))
-        z_add(1, 0)
-        z_add(0, 1)
-        z_add(1, 1)
-        m_row(2, 1, 4)
-        m_row(3, 1, 0)
-        t_z(0, 1)
-        t_z(1, 5)
-        c_z(0)
-        c_z(1)
-        z_add(2, 0)
-        z_add(2, 1)
-        q_z(0)
-        m_row(4, 1, 6)
-        m_row(5, 0, 2)
-        def chan(m, b0, b1, b2, b3):
-            m_chan(m, 2, b0)
-            gate(m, 0)
-            m_chan(m, 0, b1)
-            m_chan(m, 3, b2)
-            gate(m, 1)
-            m_chan(m, 1, b3)
-        z_add(3, 0)
-        q_z(1)
-        z_add(3, 1)
-        chan(0, 1, 4, 5, 3)
-        z_add(4, 0)
-        finish(0, 0)
-        finish(0, 1)
-        t_z(2, 0)
-        t_z(3, 1)
-        c_z(2)
-        c_z(3)
-        chan(1, 7, 4, 5, 3)
-        z_add(4, 1)
-        q_z(2)
-        finish(1, 0)
-        q_z(3)
-        finish(1, 1)
-        m_row(5, 1, 0)
-        chan(2, 1, 6, 7, 4)
-        z_add(5, 0)
-        z_add(5, 1)
-        finish(2, 0)
-        r_words(6, 8)
-        finish(2, 1)
-        r_scales(6, 8)
-        t_z(4, 5)
-        t_z(5, 3)
-        c_z(4)
-        c_z(5)
-        chan(3, 2, 0, 1, 6)
-        q_z(4)
-        finish(3, 0)
-        q_z(5)
-        finish(3, 1)
-        m_row(6, 0, 7)
-        m_row(6, 1, 4)
-        m_row(7, 0, 5)
-        m_row(7, 1, 3)
-        chan(4, 2, 0, 1, 6)
-        z_add(6, 0)
-        z_add(6, 1)
-        z_add(7, 0)
-        z_add(7, 1)
-        finish(4, 0)
-        finish(4, 1)
-        t_z(6, 7)
-        t_z(7, 4)
-        c_z(6)
-        c_z(7)
-        chan(5, 5, 3, 2, 0)
-        q_z(6)
-        finish(5, 0)
-        q_z(7)
-        finish(5, 1)
-        chan(6, 1, 6, 7, 4)
-        finish(6, 0)
-        finish(6, 1)
-        m_chan(7, 2, 5)
-        gate(7, 0)
-        m_chan(7, 0, 3)
-        finish(7, 0)
-        for i in range(5):
-            if i < 4:
-                m_chan_piece(7, 3, i, (2, 1, 7, 5)[i])
-                gate_piece(7, 1, i)
-            if i > 0:
-                m_chan_piece(7, 1, i - 1, (0, 6, 4, 2)[i - 1])
-                finish_piece(7, 1, i - 1)
+            for m in range(2):
+                row_pass(m, 1, g)
+        for h in range(2):
+            for m in range(2):
+                add_y(m, h)
+        for m in range(2, 4):
+            row_product(m, 1)
+
+        turn_z(0)
+        turn_z(1)
+        add_y(2, 0)
+        group_z(0, parts=2)
+        add_y(2, 1)
+        group_z(1)
+        quantize_z(0, parts=2)
+        row_product(4, 1)
+        row_product(5, 0)
+        add_y(3, 0)
+        quantize_z(1)
+        add_y(3, 1)
+        add_y(4, 0)
+        out_half(0, 0)
+        out_half(0, 1)
+
+        rows_left = {2: [(5, 1)], 4: [(6, 0), (6, 1), (7, 0), (7, 1)], 6: []}
+        sums_left = {2: [(5, 0), (5, 1)], 4: rows_left[4], 6: []}
+        for m in range(2, TILES, 2):
+            turn_z(m)
+            turn_z(m + 1)
+            group_z(m)
+            group_z(m + 1)
+            if m == 2:
+                add_y(4, 1)
+            for n in range(2):
+                quantize_z(m + n)
+                out_half(m - 1, n)
+            for tile_half in rows_left[m]:
+                row_product(*tile_half)
+            for tile_half in sums_left[m]:
+                add_y(*tile_half)
+            out_half(m, 0)
+            if m == 2:
+                deal_row_words(ROW_PARTS[2])
+            out_half(m, 1)
+            if m == 2:
+                deal_row_scales(ROW_PARTS[2])
+
+        last = TILES - 1
+        gate_product(last, 0, SHARE)
+        for c0 in range(0, 2 * HALF, SHARE):
+            if c0 + SHARE < 2 * HALF:
+                gate_product(last, c0 + SHARE, SHARE)
+            chan_product(last, c0, SHARE)
+            store_product(last, c0, SHARE)

@@ -83,9 +83,26 @@ def tile_codebook_patch_mixer_t2_kernel(
         clear(book_s[0])
         make_identity(nc, ident[:])
         clear(book_s[1])
+        nc.vector.memset(codes_q[TILES - 1][:, 0:P], 0)
+        nc.vector.memset(codes_s[TILES - 1][:, 0:P].bitcast(I32), 0)
+        nc.vector.memset(book_w[1][:, 0, :].bitcast(I32), 0)
         clear(row_s_raw[0])
         clear(row_s_raw[1])
         clear(chan_s)
+
+        def warm_up(name, passes):
+            acc = take_bank(name, [P, HALF])
+            for i in range(passes):
+                nc.tensor.matmul_mx(
+                    out=acc[:],
+                    lhsT=codes_q[TILES - 1][:, 0:P].bitcast(FP8X4),
+                    lhsT_scale=codes_s[TILES - 1][:, 0:P],
+                    rhs=book_w[1][:, 0, :].bitcast(FP4X4),
+                    rhs_scale=book_s[1][:, 0, :],
+                    start=True,
+                    stop=True,
+                )
+            give_bank(name)
 
         codes_v = codes.rearrange("(g p t) j -> g t p j", p=P, t=4)
         x_v = x.rearrange("(g p t) c -> g t p c", p=P, t=4)
@@ -347,6 +364,16 @@ def tile_codebook_patch_mixer_t2_kernel(
             load_x(m - 2, 0)
             if m == 2:
                 nc.sync.dma_start(out=gain_raw[:], in_=patch_gain.rearrange("(g p t) -> p g t", p=P, t=4))
+
+        warm_up("warm0", 3)
+        sort_codes(0, parts=2)
+        turn_codes(0)
+        warm_up("warm1", 2)
+        sort_codes(1)
+        quantize_codes(0)
+        turn_codes(1)
+        warm_up("warm2", 1)
+
         load_words(row_w_raw[0], row_words[:, :, word_cols(0)])
         load_scales(row_s_raw[0], row_scales[:, :, scale_cols(0)])
         load_words(book_w[1], book_words[:, :, word_cols(1)])
@@ -363,11 +390,6 @@ def tile_codebook_patch_mixer_t2_kernel(
             nc.sync.dma_start(out=chan_w[h][:].bitcast(I32), in_=chan_words[h].bitcast(I32))
         load_scales(chan_s, chan_scales)
 
-        sort_codes(0, parts=2)
-        turn_codes(0)
-        sort_codes(1)
-        quantize_codes(0)
-        turn_codes(1)
         quantize_codes(1)
 
         book_product(0, 0)

@@ -23,6 +23,7 @@ HALF = 512
 SHARE = 256
 ROW_PARTS = ((0, 4), (4, 6), (6, 8))
 UNSORTED = (2, 7)
+ON_TENSOR = 2
 
 
 def tile_codebook_patch_mixer_t2_kernel(
@@ -134,7 +135,7 @@ def tile_codebook_patch_mixer_t2_kernel(
         sorted_words, turned, grouped, sums = {}, {}, {}, {}
 
         def sort_codes(m, parts=1):
-            sorted_words[m] = ring.tile([P, 4, 2, P], F32, name="sorted%d" % m, tag="sorted", bufs=2)
+            sorted_words[m] = ring.tile([P, 4, 2, P], F32, name="sorted%d" % m, tag="sorted", bufs=2, align_bytes=64)
             width = 4 // parts
             for i in range(parts):
                 raw = codes_raw[m][:, i * width * 512 : (i + 1) * width * 512].bitcast(F32)
@@ -282,13 +283,42 @@ def tile_codebook_patch_mixer_t2_kernel(
         def add_y(m, h):
             if h == 0:
                 z_sb[m] = kept("z%d" % m, [P, 2 * HALF], BF16, tag="codes_raw%d" % m)
+            if m < ON_TENSOR:
+                target = z_sb[m][:, h * HALF : (h + 1) * HALF].rearrange("p (u q j e) -> p u q j e", u=2, q=4, e=2)
+            else:
+                target = z_sb[m][:].rearrange("p (q h u j e) -> p h u q j e", q=4, h=2, u=2, e=2)[:, h]
             nc.vector.tensor_tensor(
-                out=z_sb[m][:, h * HALF : (h + 1) * HALF].rearrange("p (u q e) -> p u q e", u=2, e=2),
-                in0=mixed[m, h][:].rearrange("p (q u e) -> p u q e", u=2, e=2),
-                in1=y_sb[m, h][:].rearrange("p (q u e) -> p u q e", u=2, e=2),
+                out=target,
+                in0=mixed[m, h][:].rearrange("p (q j u e) -> p u q j e", q=4, u=2, e=2),
+                in1=y_sb[m, h][:].rearrange("p (q j u e) -> p u q j e", q=4, u=2, e=2),
                 op=ADD,
             )
             give_bank("row%d%d" % (m, h))
+
+        z_back, z_blocks = {}, {}
+
+        def parking(m):
+            return out[HALF + 64 * (m - ON_TENSOR) : HALF + 64 * (m - ON_TENSOR + 1), :].bitcast(BF16)
+
+        def park_z(m):
+            room = parking(m).rearrange("a (b w) -> (a b) w", w=2 * P).rearrange("(q p) w -> p q w", q=4)
+            nc.sync.dma_start(out=room, in_=z_sb[m][:].rearrange("p (q w) -> p q w", q=4))
+
+        def fetch_z(m):
+            z_back[m] = ring.tile([P, 2 * HALF], BF16, name="z_back%d" % m, tag="e_rows", bufs=3, align_bytes=64)
+            nc.sync.dma_start(out=z_back[m][:], in_=parking(m).rearrange("a (b w) -> (a b) w", w=2 * HALF))
+
+        def turn_z_blocks(m):
+            z_blocks[m] = ring.tile([P, HALF], F32, name="z_blocks%d" % m, tag="sorted", bufs=2, align_bytes=64)
+            nc.vector.transpose(out=z_blocks[m][:], in_=z_back[m][:].bitcast(F32))
+
+        def group_z_blocks(m):
+            z_grouped[m] = ring.tile([P, 2, P, 4], BF16, name="z_grouped%d" % m, tag="grouped", bufs=5, align_bytes=64)
+            blocks = z_blocks[m][:].rearrange("p (a b h u i) -> p h a i b u", a=2, b=2, h=2, u=2)
+            for h in range(2):
+                nc.scalar.copy(
+                    out=z_grouped[m][:, h].bitcast(F32).rearrange("p (i a b) u -> p a i b u", a=2, b=2), in_=blocks[:, h]
+                )
 
         def turn_z(m):
             z_turned[m] = take_bank("turn_z%d" % m, [P, 2, 2, P])
@@ -426,29 +456,35 @@ def tile_codebook_patch_mixer_t2_kernel(
         add_x(1, 1)
         interleave_shared(1, 0)
         scale_y(1, 1)
-        for m in (3, 4):
-            book_product(m, 1)
-            finish_y(m - 1, 1)
+        book_product(3, 1)
+        finish_y(2, 1)
+        deal_row_words(ROW_PARTS[2])
+        book_product(4, 1)
+        finish_y(3, 1)
         deal_row_scales(ROW_PARTS[1])
         quantize_e(1, 0, (1, 0))
         book_product(5, 1)
         add_x(4, 1)
         interleave_shared(0, 1)
         scale_y(4, 1)
-        book_product(6, 1)
+        row_product(2, 0)
         finish_y(5, 1)
-
-        for c0 in (0, SHARE):
-            book_product_share(7, 1, c0)
+        book_product(6, 1)
+        add_y(2, 0)
+        deal_row_scales(ROW_PARTS[2])
+        row_product(0, 0)
         finish_y(6, 1)
         for c0 in (0, SHARE):
-            add_x(7, 1, c0, c0 + SHARE)
+            book_product_share(7, 1, c0)
         quantize_e(0, 1, (1, 0))
+        add_y(0, 0)
+        for c0 in (0, SHARE):
+            add_x(7, 1, c0, c0 + SHARE)
         for c0 in (0, SHARE):
             scale_y(7, 1, c0, c0 + SHARE)
-
-        for m in range(5):
+        for m in (1, 3, 4, 5):
             row_product(m, 0)
+        add_y(1, 0)
         for share in range(2):
             new_e_words(1, 1, share, "e_words1%d" % share)
         interleave(nc.vector.tensor_copy, 1, 1, 0, SHARE)
@@ -456,52 +492,54 @@ def tile_codebook_patch_mixer_t2_kernel(
         interleave(nc.scalar.copy, 1, 1, SHARE + P, HALF)
         quantize_e(1, 1, (0, 1))
         for g in range(2):
-            for m in range(2):
+            for m in (0, 2, 1):
                 row_pass(m, 1, g)
-        for h in range(2):
-            for m in range(2):
-                add_y(m, h)
-        for m in range(2, 4):
-            row_product(m, 1)
-
+        add_y(3, 0)
+        add_y(0, 1)
+        add_y(2, 1)
+        park_z(2)
+        add_y(1, 1)
+        row_product(3, 1)
+        row_product(4, 1)
         turn_z(0)
         turn_z(1)
-        add_y(2, 0)
+        add_y(3, 1)
+        park_z(3)
         group_z(0, parts=2)
-        add_y(2, 1)
         group_z(1)
         quantize_z(0, parts=2)
-        row_product(4, 1)
-        row_product(5, 0)
-        add_y(3, 0)
-        quantize_z(1)
-        add_y(3, 1)
+        row_product(5, 1)
         add_y(4, 0)
-        out_half(0, 0)
-        out_half(0, 1)
-
-        rows_left = {2: [(5, 1)], 4: [(6, 0), (6, 1), (7, 0), (7, 1)], 6: []}
-        sums_left = {2: [(5, 0), (5, 1)], 4: rows_left[4], 6: []}
-        for m in range(2, TILES, 2):
-            turn_z(m)
-            turn_z(m + 1)
-            group_z(m)
-            group_z(m + 1)
-            if m == 2:
-                add_y(4, 1)
-            for n in range(2):
-                quantize_z(m + n)
-                out_half(m - 1, n)
-            for tile_half in rows_left[m]:
-                row_product(*tile_half)
-            for tile_half in sums_left[m]:
-                add_y(*tile_half)
-            out_half(m, 0)
-            if m == 2:
-                deal_row_words(ROW_PARTS[2])
+        fetch_z(2)
+        add_y(4, 1)
+        park_z(4)
+        quantize_z(1)
+        fetch_z(3)
+        add_y(5, 0)
+        add_y(5, 1)
+        park_z(5)
+        for m in range(TILES - 1):
+            gate_product(m, 0, HALF)
+            chan_product(m, 0, HALF)
+            if m > 1:
+                quantize_z(m + 1)
+            if 2 <= m < TILES - 2:
+                turn_z_blocks(m + 2)
+            if m + 4 < TILES:
+                fetch_z(m + 4)
+            store_product(m, 0, HALF)
+            if m == 1:
+                quantize_z(2)
             out_half(m, 1)
-            if m == 2:
-                deal_row_scales(ROW_PARTS[2])
+            if m < 2:
+                row_product(m + 6, 0)
+                row_product(m + 6, 1)
+                turn_z_blocks(m + 2)
+                add_y(m + 6, 0)
+                add_y(m + 6, 1)
+                park_z(m + 6)
+            if m + 2 < TILES:
+                group_z_blocks(m + 2)
 
         last = TILES - 1
         gate_product(last, 0, SHARE)

@@ -21,9 +21,9 @@ P = 128
 TILES = 8
 HALF = 512
 SHARE = 256
-ROW_PARTS = ((0, 4), (4, 6), (6, 8))
+ROW_PARTS = ((0, 4), (4, 8))
 UNSORTED = (2, 7)
-ON_TENSOR = 2
+ON_TENSOR = 4
 
 
 def tile_codebook_patch_mixer_t2_kernel(
@@ -367,7 +367,7 @@ def tile_codebook_patch_mixer_t2_kernel(
         def gate_product(m, c0, width):
             chan_product(m, 2 * HALF + c0, width)
             gates[m, c0] = ring.tile(
-                [P, width], F32, name="gate%d_%d" % (m, c0), tag="gate%d" % width, bufs=3 if width == HALF else 4
+                [P, width], F32, name="gate%d_%d" % (m, c0), tag="gate%d" % width, bufs=5 if width == HALF else 4
             )
             nc.scalar.activation(out=gates[m, c0][:], in_=h_sums[m, 2 * HALF + c0][:], func=ACT.Tanh)
             give_bank("chan%d_%d" % (m, 2 * HALF + c0))
@@ -456,35 +456,29 @@ def tile_codebook_patch_mixer_t2_kernel(
         add_x(1, 1)
         interleave_shared(1, 0)
         scale_y(1, 1)
-        book_product(3, 1)
-        finish_y(2, 1)
-        deal_row_words(ROW_PARTS[2])
-        book_product(4, 1)
-        finish_y(3, 1)
+        for m in (3, 4):
+            book_product(m, 1)
+            finish_y(m - 1, 1)
         deal_row_scales(ROW_PARTS[1])
         quantize_e(1, 0, (1, 0))
         book_product(5, 1)
         add_x(4, 1)
         interleave_shared(0, 1)
         scale_y(4, 1)
-        row_product(2, 0)
-        finish_y(5, 1)
         book_product(6, 1)
-        add_y(2, 0)
-        deal_row_scales(ROW_PARTS[2])
-        row_product(0, 0)
-        finish_y(6, 1)
+        finish_y(5, 1)
+
         for c0 in (0, SHARE):
             book_product_share(7, 1, c0)
-        quantize_e(0, 1, (1, 0))
-        add_y(0, 0)
+        finish_y(6, 1)
         for c0 in (0, SHARE):
             add_x(7, 1, c0, c0 + SHARE)
+        quantize_e(0, 1, (1, 0))
         for c0 in (0, SHARE):
             scale_y(7, 1, c0, c0 + SHARE)
-        for m in (1, 3, 4, 5):
+
+        for m in range(5):
             row_product(m, 0)
-        add_y(1, 0)
         for share in range(2):
             new_e_words(1, 1, share, "e_words1%d" % share)
         interleave(nc.vector.tensor_copy, 1, 1, 0, SHARE)
@@ -492,52 +486,67 @@ def tile_codebook_patch_mixer_t2_kernel(
         interleave(nc.scalar.copy, 1, 1, SHARE + P, HALF)
         quantize_e(1, 1, (0, 1))
         for g in range(2):
-            for m in (0, 2, 1):
+            for m in range(2):
                 row_pass(m, 1, g)
-        add_y(3, 0)
-        add_y(0, 1)
-        add_y(2, 1)
-        park_z(2)
-        add_y(1, 1)
-        row_product(3, 1)
-        row_product(4, 1)
+        for h in range(2):
+            for m in range(2):
+                add_y(m, h)
+        for m in range(2, 4):
+            row_product(m, 1)
+
         turn_z(0)
         turn_z(1)
-        add_y(3, 1)
-        park_z(3)
+        add_y(2, 0)
         group_z(0, parts=2)
+        add_y(2, 1)
         group_z(1)
         quantize_z(0, parts=2)
-        row_product(5, 1)
+        row_product(4, 1)
+        row_product(5, 0)
+        add_y(3, 0)
+        quantize_z(1)
+        add_y(3, 1)
         add_y(4, 0)
-        fetch_z(2)
         add_y(4, 1)
         park_z(4)
-        quantize_z(1)
-        fetch_z(3)
+        out_half(0, 0)
+        out_half(0, 1)
+        row_product(5, 1)
+        turn_z(2)
+        turn_z(3)
+        group_z(2)
+        group_z(3)
+        quantize_z(2)
         add_y(5, 0)
         add_y(5, 1)
         park_z(5)
-        for m in range(TILES - 1):
+        fetch_z(4)
+        gate_product(1, 0, HALF)
+        chan_product(1, 0, HALF)
+        quantize_z(3)
+        store_product(1, 0, HALF)
+        gate_product(1, HALF, HALF)
+        chan_product(1, HALF, HALF)
+        for m in (6, 7):
+            for h in range(2):
+                row_product(m, h)
+                add_y(m, h)
+            park_z(m)
+            if m == 6:
+                store_product(1, HALF, HALF)
+                fetch_z(5)
+        fetch_z(6)
+        for m in range(2, TILES - 1):
             gate_product(m, 0, HALF)
             chan_product(m, 0, HALF)
-            if m > 1:
+            if m > 2:
                 quantize_z(m + 1)
-            if 2 <= m < TILES - 2:
+            if m + 2 < TILES:
                 turn_z_blocks(m + 2)
-            if m + 4 < TILES:
-                fetch_z(m + 4)
             store_product(m, 0, HALF)
-            if m == 1:
-                quantize_z(2)
             out_half(m, 1)
-            if m < 2:
-                row_product(m + 6, 0)
-                row_product(m + 6, 1)
-                turn_z_blocks(m + 2)
-                add_y(m + 6, 0)
-                add_y(m + 6, 1)
-                park_z(m + 6)
+            if m == 2:
+                fetch_z(7)
             if m + 2 < TILES:
                 group_z_blocks(m + 2)
 

@@ -374,7 +374,7 @@ def tile_codebook_patch_mixer_t2_kernel(
 
         def store_product(m, c0, width):
             result = ring.tile(
-                [P, width], F32, name="result%d_%d" % (m, c0), tag="result%d" % width, bufs=5 if width == HALF else 4
+                [P, width], F32, name="result%d_%d" % (m, c0), tag="result%d" % width, bufs=7 if width == HALF else 4
             )
             nc.vector.tensor_tensor(out=result[:], in0=h_sums[m, c0][:], in1=gates[m, c0][:], op=MULT)
             give_bank("chan%d_%d" % (m, c0))
@@ -503,52 +503,50 @@ def tile_codebook_patch_mixer_t2_kernel(
         quantize_z(0, parts=2)
         row_product(4, 1)
         row_product(5, 0)
-        add_y(3, 0)
-        quantize_z(1)
-        add_y(3, 1)
         add_y(4, 0)
         add_y(4, 1)
         park_z(4)
-        out_half(0, 0)
-        out_half(0, 1)
+        quantize_z(1)
+        add_y(3, 0)
+        add_y(3, 1)
+        gate_product(0, 0, HALF)
+        chan_product(0, 0, HALF)
+        gate_product(0, HALF, HALF)
+        chan_product(0, HALF, HALF)
         row_product(5, 1)
         turn_z(2)
         turn_z(3)
         group_z(2)
         group_z(3)
-        quantize_z(2)
         add_y(5, 0)
         add_y(5, 1)
         park_z(5)
-        fetch_z(4)
-        gate_product(1, 0, HALF)
-        chan_product(1, 0, HALF)
-        quantize_z(3)
-        store_product(1, 0, HALF)
-        gate_product(1, HALF, HALF)
-        chan_product(1, HALF, HALF)
-        for m in (6, 7):
+        for n in range(2):
+            store_product(0, n * HALF, HALF)
             for h in range(2):
-                row_product(m, h)
-                add_y(m, h)
-            park_z(m)
-            if m == 6:
-                store_product(1, HALF, HALF)
-                fetch_z(5)
-        fetch_z(6)
+                row_product(6 + n, h)
+                add_y(6 + n, h)
+            fetch_z(4 + n)
+            park_z(6 + n)
+            gate_product(1, n * HALF, HALF)
+            chan_product(1, n * HALF, HALF)
+            quantize_z(2 + n)
+        store_product(1, 0, HALF)
         for m in range(2, TILES - 1):
             gate_product(m, 0, HALF)
             chan_product(m, 0, HALF)
-            if m > 2:
-                quantize_z(m + 1)
             if m + 2 < TILES:
                 turn_z_blocks(m + 2)
-            store_product(m, 0, HALF)
-            out_half(m, 1)
-            if m == 2:
-                fetch_z(7)
-            if m + 2 < TILES:
                 group_z_blocks(m + 2)
+            if m + 4 < TILES:
+                fetch_z(m + 4)
+            store_product(m - 1, HALF, HALF)
+            store_product(m, 0, HALF)
+            if m + 2 < TILES:
+                quantize_z(m + 2)
+            gate_product(m, HALF, HALF)
+            chan_product(m, HALF, HALF)
+        store_product(TILES - 2, HALF, HALF)
 
         last = TILES - 1
         gate_product(last, 0, SHARE)

@@ -297,16 +297,13 @@ def tile_codebook_patch_mixer_t2_kernel(
 
         z_back, z_blocks = {}, {}
 
-        def parking(m):
-            return out[HALF + 64 * (m - ON_TENSOR) : HALF + 64 * (m - ON_TENSOR + 1), :].bitcast(BF16)
-
         def park_z(m):
-            room = parking(m).rearrange("a (b w) -> (a b) w", w=2 * P).rearrange("(q p) w -> p q w", q=4)
-            nc.sync.dma_start(out=room, in_=z_sb[m][:].rearrange("p (q w) -> p q w", q=4))
-
-        def fetch_z(m):
-            z_back[m] = ring.tile([P, 2 * HALF], BF16, name="z_back%d" % m, tag="e_rows", bufs=3, align_bytes=64)
-            nc.sync.dma_start(out=z_back[m][:], in_=parking(m).rearrange("a (b w) -> (a b) w", w=2 * HALF))
+            z_back[m] = kept("z_back%d" % m, [P, 2 * HALF], BF16, tag="codes_q%d" % m)
+            for q in range(4):
+                nc.sync.dma_start(
+                    out=z_back[m][32 * q : 32 * (q + 1), :].rearrange("i (a w) -> i a w", a=4),
+                    in_=z_sb[m][:, q * SHARE : (q + 1) * SHARE],
+                )
 
         def turn_z_blocks(m):
             z_blocks[m] = ring.tile([P, HALF], F32, name="z_blocks%d" % m, tag="sorted", bufs=2, align_bytes=64)
@@ -395,7 +392,7 @@ def tile_codebook_patch_mixer_t2_kernel(
             if m == 2:
                 nc.sync.dma_start(out=gain_raw[:], in_=patch_gain.rearrange("(g p t) -> p g t", p=P, t=4))
 
-        warm_up("warm0", 3)
+        warm_up("warm0", 4)
         sort_codes(0, parts=2)
         turn_codes(0)
         warm_up("warm1", 2)
@@ -523,29 +520,31 @@ def tile_codebook_patch_mixer_t2_kernel(
         park_z(5)
         for n in range(2):
             store_product(0, n * HALF, HALF)
+        for n in range(2):
             for h in range(2):
                 row_product(6 + n, h)
                 add_y(6 + n, h)
-            fetch_z(4 + n)
             park_z(6 + n)
             gate_product(1, n * HALF, HALF)
             chan_product(1, n * HALF, HALF)
             quantize_z(2 + n)
+            if n == 0:
+                turn_z_blocks(4)
+                group_z_blocks(4)
         store_product(1, 0, HALF)
         for m in range(2, TILES - 1):
             gate_product(m, 0, HALF)
             chan_product(m, 0, HALF)
             if m + 2 < TILES:
-                turn_z_blocks(m + 2)
-                group_z_blocks(m + 2)
-            if m + 4 < TILES:
-                fetch_z(m + 4)
+                quantize_z(m + 2)
+            if m + 3 < TILES:
+                turn_z_blocks(m + 3)
             store_product(m - 1, HALF, HALF)
             store_product(m, 0, HALF)
-            if m + 2 < TILES:
-                quantize_z(m + 2)
             gate_product(m, HALF, HALF)
             chan_product(m, HALF, HALF)
+            if m + 3 < TILES:
+                group_z_blocks(m + 3)
         store_product(TILES - 2, HALF, HALF)
 
         last = TILES - 1

@@ -23,6 +23,7 @@ HALF = 512
 SHARE = 256
 ROW_PARTS = ((0, 4), (4, 8))
 UNSORTED = (2, 7)
+SORTED_PASSES = 3
 ON_TENSOR = 4
 
 
@@ -144,6 +145,14 @@ def tile_codebook_patch_mixer_t2_kernel(
                     in_=raw.rearrange("p (g q u) -> p g u q", g=width, u=2),
                 )
 
+        def sort_codes_but_last(m):
+            sorted_words[m] = ring.tile([P, 4, 2, P], F32, name="sorted%d" % m, tag="sorted", bufs=2, align_bytes=64)
+            raw = codes_raw[m][:, 0 : SORTED_PASSES * 512].bitcast(F32)
+            nc.vector.tensor_copy(
+                out=sorted_words[m][:, 0:SORTED_PASSES].rearrange("p g u q -> p u g q"),
+                in_=raw.rearrange("p (g q u) -> p u g q", g=SORTED_PASSES, u=2),
+            )
+
         def turn_codes(m):
             words = codes_raw[m][:].bitcast(F32)
             for b in range(2):
@@ -151,7 +160,7 @@ def tile_codebook_patch_mixer_t2_kernel(
                 for i in range(2):
                     g = 2 * b + i
                     for u in range(2):
-                        if m in UNSORTED:
+                        if m in UNSORTED or (m > 2 and g >= SORTED_PASSES):
                             source = words[:, 256 * g + u : 256 * (g + 1) : 2]
                         else:
                             source = sorted_words[m][:, g, u, :]
@@ -425,14 +434,14 @@ def tile_codebook_patch_mixer_t2_kernel(
         nc.vector.tensor_copy(out=gain[:], in_=gain_raw[:].rearrange("p g t -> p (g t)"))
         scale_y(0, 0)
         book_product(1, 0)
-        sort_codes(3)
+        sort_codes_but_last(3)
         quantize_codes(2)
         for m in range(2, TILES - 1):
             turn_codes(m + 1)
             finish_y(m - 1, 0)
             book_product(m, 0)
             if m + 2 < TILES - 1:
-                sort_codes(m + 2)
+                sort_codes_but_last(m + 2)
             elif m + 2 == TILES - 1:
                 deal_row_words(ROW_PARTS[0])
             else:

@@ -24,7 +24,7 @@ SHARE = 256
 ROW_PARTS = ((0, 4), (4, 8))
 UNSORTED = (2, 7)
 SORTED_PASSES = 3
-ON_TENSOR = 4
+ON_TENSOR = 2
 
 
 def tile_codebook_patch_mixer_t2_kernel(
@@ -386,6 +386,17 @@ def tile_codebook_patch_mixer_t2_kernel(
             give_bank("chan%d_%d" % (m, c0))
             nc.sync.dma_start(out=out_v[m // 4, m % 4][:, c0 : c0 + width], in_=result[:])
 
+        def store_product_pool(m, c0):
+            values = ring.tile([P, HALF], F32, name="values%d_%d" % (m, c0), tag="values", bufs=2)
+            nc.scalar.copy(out=values[:], in_=h_sums[m, c0][:])
+            give_bank("chan%d_%d" % (m, c0))
+            result = ring.tile([P, HALF], F32, name="result%d_%d" % (m, c0), tag="result%d" % HALF, bufs=7)
+            nc.gpsimd.tensor_tensor(out=result[:], in0=values[:], in1=gates[m, c0][:], op=MULT)
+            return result
+
+        def store(m, c0, result):
+            nc.sync.dma_start(out=out_v[m // 4, m % 4][:, c0 : c0 + HALF], in_=result[:])
+
         def out_half(m, n):
             gate_product(m, n * HALF, HALF)
             chan_product(m, n * HALF, HALF)
@@ -506,54 +517,50 @@ def tile_codebook_patch_mixer_t2_kernel(
         group_z(0, parts=2)
         add_y(2, 1)
         group_z(1)
+        park_z(2)
         quantize_z(0, parts=2)
         row_product(4, 1)
         row_product(5, 0)
+        add_y(3, 0)
+        add_y(3, 1)
+        park_z(3)
+        quantize_z(1)
         add_y(4, 0)
         add_y(4, 1)
         park_z(4)
-        quantize_z(1)
-        add_y(3, 0)
-        add_y(3, 1)
-        gate_product(0, 0, HALF)
-        chan_product(0, 0, HALF)
-        gate_product(0, HALF, HALF)
-        chan_product(0, HALF, HALF)
+        early = {}
+        for n in range(2):
+            gate_product(0, n * HALF, HALF)
+            chan_product(0, n * HALF, HALF)
+            early[n] = store_product_pool(0, n * HALF)
         row_product(5, 1)
-        turn_z(2)
-        turn_z(3)
-        group_z(2)
-        group_z(3)
         add_y(5, 0)
         add_y(5, 1)
         park_z(5)
         for n in range(2):
-            store_product(0, n * HALF, HALF)
-        for n in range(2):
+            turn_z_blocks(2 + n)
             for h in range(2):
                 row_product(6 + n, h)
                 add_y(6 + n, h)
             park_z(6 + n)
+            store(0, n * HALF, early[n])
+            group_z_blocks(2 + n)
             gate_product(1, n * HALF, HALF)
             chan_product(1, n * HALF, HALF)
             quantize_z(2 + n)
-            if n == 0:
-                turn_z_blocks(4)
-                group_z_blocks(4)
         store_product(1, 0, HALF)
         for m in range(2, TILES - 1):
             gate_product(m, 0, HALF)
             chan_product(m, 0, HALF)
             if m + 2 < TILES:
-                quantize_z(m + 2)
-            if m + 3 < TILES:
-                turn_z_blocks(m + 3)
+                turn_z_blocks(m + 2)
+                group_z_blocks(m + 2)
             store_product(m - 1, HALF, HALF)
             store_product(m, 0, HALF)
+            if m + 2 < TILES:
+                quantize_z(m + 2)
             gate_product(m, HALF, HALF)
             chan_product(m, HALF, HALF)
-            if m + 3 < TILES:
-                group_z_blocks(m + 3)
         store_product(TILES - 2, HALF, HALF)
 
         last = TILES - 1

@@ -547,20 +547,28 @@ def tile_codebook_patch_mixer_t2_kernel(
             group_z_blocks(2 + n)
             gate_product(1, n * HALF, HALF)
             chan_product(1, n * HALF, HALF)
+            early[2 + n] = store_product_pool(1, n * HALF)
             quantize_z(2 + n)
-        store_product(1, 0, HALF)
+        turn_z_blocks(4)
+        store(1, 0, early[2])
         for m in range(2, TILES - 1):
             gate_product(m, 0, HALF)
             chan_product(m, 0, HALF)
-            if m + 2 < TILES:
-                turn_z_blocks(m + 2)
-                group_z_blocks(m + 2)
-            store_product(m - 1, HALF, HALF)
-            store_product(m, 0, HALF)
+            if m == 2:
+                group_z_blocks(4)
+                turn_z_blocks(5)
+                store(1, HALF, early[3])
+            else:
+                store_product(m - 1, HALF, HALF)
             if m + 2 < TILES:
                 quantize_z(m + 2)
+            if m > 2 and m + 3 < TILES:
+                turn_z_blocks(m + 3)
+            store_product(m, 0, HALF)
             gate_product(m, HALF, HALF)
             chan_product(m, HALF, HALF)
+            if m + 3 < TILES:
+                group_z_blocks(m + 3)
         store_product(TILES - 2, HALF, HALF)
 
         last = TILES - 1

@@ -22,7 +22,7 @@ TILES = 8
 HALF = 512
 SHARE = 256
 ROW_PARTS = ((0, 4), (4, 8))
-UNSORTED = (2, 7)
+UNSORTED = (2,)
 SORTED_PASSES = 3
 ON_TENSOR = 2
 
@@ -63,12 +63,13 @@ def tile_codebook_patch_mixer_t2_kernel(
         e_q = {(g, h): kept("e_q%d%d" % (g, h), [P, HALF], U32) for g, h in groups}
         e_s = {(g, h): kept("e_s%d%d" % (g, h), [P, HALF], U8) for g, h in groups}
         row_w_raw = [kept("row_w_raw%d" % g, [P, 2, 2 * HALF], U8) for g in range(2)]
-        row_s_raw = [kept("row_s_raw%d" % g, [P, 2, HALF], U8) for g in range(2)]
-        row_w, row_s, row_at = {}, {}, {}
+        row_s_raw = kept("row_s_raw", [P, 2 * HALF], U8)
+        row_s_dealt = kept("row_s_dealt", [P, 2 * HALF], U8)
+        row_s = kept("row_s", [P, 2, 2 * HALF], U8)
+        row_w, row_at = {}, {}
         for part in ROW_PARTS:
             width = part[1] - part[0]
             row_w[part] = kept("row_w%d" % part[0], [P, 2 * width * 2 * P], U8)
-            row_s[part] = kept("row_s%d" % part[0], [P, 2 * width * P], U8)
             for m in range(*part):
                 row_at[m] = (part, [(g * width + m - part[0]) * P for g in range(2)])
         chan_w = [kept("chan_w%d" % h, [P, 4096], U8) for h in range(2)]
@@ -88,9 +89,7 @@ def tile_codebook_patch_mixer_t2_kernel(
         nc.vector.memset(codes_q[TILES - 1][:, 0:P], 0)
         nc.vector.memset(codes_s[TILES - 1][:, 0:P].bitcast(I32), 0)
         nc.vector.memset(book_w[1][:, 0, :].bitcast(I32), 0)
-        clear(row_s_raw[0])
-        clear(row_s_raw[1])
-        clear(chan_s)
+        nc.vector.memset(row_s_raw[:].bitcast(I32), 0)
 
         def warm_up(name, passes):
             acc = take_bank(name, [P, HALF])
@@ -160,7 +159,7 @@ def tile_codebook_patch_mixer_t2_kernel(
                 for i in range(2):
                     g = 2 * b + i
                     for u in range(2):
-                        if m in UNSORTED or (m > 2 and g >= SORTED_PASSES):
+                        if m in UNSORTED or (2 < m < TILES - 1 and g >= SORTED_PASSES):
                             source = words[:, 256 * g + u : 256 * (g + 1) : 2]
                         else:
                             source = sorted_words[m][:, g, u, :]
@@ -256,18 +255,26 @@ def tile_codebook_patch_mixer_t2_kernel(
                 )
 
         def deal_row_words(part):
-            t0, t1 = part[0] % 4, (part[1] - 1) % 4 + 1
             nc.vector.tensor_copy(
-                out=row_w[part][:].bitcast(U16).rearrange("p (g t m) -> p g t m", g=2, m=P),
-                in_=row_w_raw[part[0] // 4][:].bitcast(U16).rearrange("p g (m t) -> p g t m", t=4)[:, :, t0:t1],
+                out=row_w[part][:].bitcast(U16).rearrange("p (g t c m) -> p g c t m", g=2, t=4, m=8),
+                in_=row_w_raw[part[0] // 4][:].bitcast(U16).rearrange("p g (c m t) -> p g c t m", m=8, t=4),
             )
 
-        def deal_row_scales(part):
-            t0, t1 = part[0] % 4, (part[1] - 1) % 4 + 1
+        def load_row_scales():
+            rows = row_s_raw[:].bitcast(I32)
+            for r in range(4):
+                source = row_scales.rearrange("g (q r) n -> r q g n", r=4)[r].bitcast(I32)
+                nc.sync.dma_start(out=rows[8 * r : 8 * (r + 1)], in_=source)
+
+        def deal_row_scales():
             nc.vector.tensor_copy(
-                out=row_s[part][:].rearrange("p (g t m) -> p g t m", g=2, m=P),
-                in_=row_s_raw[part[0] // 4][:].rearrange("p g (m t) -> p g t m", t=4)[:, :, t0:t1],
+                out=row_s_dealt[:].rearrange("p (a t m) -> p a t m", a=2, t=4),
+                in_=row_s_raw[:].rearrange("p (a m t) -> p a t m", a=2, t=4),
             )
+
+        def place_row_scales():
+            for r in range(4):
+                nc.sync.dma_start(out=row_s[:].bitcast(I32)[r:P:32], in_=row_s_dealt[:].bitcast(I32)[8 * r : 8 * (r + 1)])
 
         mixed, z_sb, z_turned, z_grouped = {}, {}, {}, {}
 
@@ -278,7 +285,7 @@ def tile_codebook_patch_mixer_t2_kernel(
             nc.tensor.matmul_mx(
                 out=mixed[m, h][:],
                 lhsT=row_w[part][:, 2 * at[g] : 2 * (at[g] + P)].bitcast(FP4X4),
-                lhsT_scale=row_s[part][:, at[g] : at[g] + P],
+                lhsT_scale=row_s[:, g, m * P : (m + 1) * P],
                 rhs=e_q[g, h][:].bitcast(FP8X4),
                 rhs_scale=e_s[g, h][:],
                 start=(g == 0),
@@ -418,24 +425,22 @@ def tile_codebook_patch_mixer_t2_kernel(
         warm_up("warm1", 2)
         sort_codes(1)
         quantize_codes(0)
+        clear(row_s)
+        clear(chan_s)
         turn_codes(1)
         warm_up("warm2", 1)
 
-        load_words(row_w_raw[0], row_words[:, :, word_cols(0)])
-        load_scales(row_s_raw[0], row_scales[:, :, scale_cols(0)])
+        load_row_scales()
         load_words(book_w[1], book_words[:, :, word_cols(1)])
         load_scales(book_s[1], book_scales[:, :, scale_cols(1)])
         load_x(6, 0)
-        load_x(7, 0)
         load_x(0, 1)
-        load_words(row_w_raw[1], row_words[:, :, word_cols(1)])
+        load_words(row_w_raw[0], row_words[:, :, word_cols(0)])
+        load_x(7, 0)
         load_x(1, 1)
-        load_scales(row_s_raw[1], row_scales[:, :, scale_cols(1)])
+        load_words(row_w_raw[1], row_words[:, :, word_cols(1)])
         for m in range(2, TILES):
             load_x(m, 1)
-        for h in range(2):
-            nc.sync.dma_start(out=chan_w[h][:].bitcast(I32), in_=chan_words[h].bitcast(I32))
-        load_scales(chan_s, chan_scales)
 
         quantize_codes(1)
 
@@ -454,10 +459,14 @@ def tile_codebook_patch_mixer_t2_kernel(
             if m + 2 < TILES - 1:
                 sort_codes_but_last(m + 2)
             elif m + 2 == TILES - 1:
-                deal_row_words(ROW_PARTS[0])
+                sort_codes(m + 2)
             else:
-                deal_row_scales(ROW_PARTS[0])
+                deal_row_scales()
             quantize_codes(m + 1)
+        place_row_scales()
+        for h in range(2):
+            nc.sync.dma_start(out=chan_w[h][:].bitcast(I32), in_=chan_words[h].bitcast(I32))
+        load_scales(chan_s, chan_scales)
 
         book_product(0, 1)
         add_x(6, 0)
@@ -467,7 +476,7 @@ def tile_codebook_patch_mixer_t2_kernel(
         finish_y(0, 1)
         book_product(1, 1)
         finish_y(7, 0)
-        deal_row_words(ROW_PARTS[1])
+        deal_row_words(ROW_PARTS[0])
         quantize_e(0, 0, (1, 0))
         book_product(2, 1)
         add_x(1, 1)
@@ -476,7 +485,7 @@ def tile_codebook_patch_mixer_t2_kernel(
         for m in (3, 4):
             book_product(m, 1)
             finish_y(m - 1, 1)
-        deal_row_scales(ROW_PARTS[1])
+        deal_row_words(ROW_PARTS[1])
         quantize_e(1, 0, (1, 0))
         book_product(5, 1)
         add_x(4, 1)

@@ -21,10 +21,11 @@ P = 128
 TILES = 8
 HALF = 512
 SHARE = 256
-ROW_PARTS = ((0, 4), (4, 8))
-UNSORTED = (2,)
+PART = 256
+UNSORTED_TILE = 2
 SORTED_PASSES = 3
 ON_TENSOR = 2
+EARLY_ROWS = 5
 
 
 def tile_codebook_patch_mixer_t2_kernel(
@@ -66,12 +67,7 @@ def tile_codebook_patch_mixer_t2_kernel(
         row_s_raw = kept("row_s_raw", [P, 2 * HALF], U8)
         row_s_dealt = kept("row_s_dealt", [P, 2 * HALF], U8)
         row_s = kept("row_s", [P, 2, 2 * HALF], U8)
-        row_w, row_at = {}, {}
-        for part in ROW_PARTS:
-            width = part[1] - part[0]
-            row_w[part] = kept("row_w%d" % part[0], [P, 2 * width * 2 * P], U8)
-            for m in range(*part):
-                row_at[m] = (part, [(g * width + m - part[0]) * P for g in range(2)])
+        row_w = [kept("row_w%d" % (4 * g), [P, 4 * HALF], U8) for g in range(2)]
         chan_w = [kept("chan_w%d" % h, [P, 4096], U8) for h in range(2)]
         chan_s = kept("chan_s", [P, 2, 2048], U8)
         z_q = [kept("z_q%d" % m, [P, 2 * P], U32) for m in range(TILES)]
@@ -141,15 +137,15 @@ def tile_codebook_patch_mixer_t2_kernel(
                 raw = codes_raw[m][:, i * width * 512 : (i + 1) * width * 512].bitcast(F32)
                 nc.vector.tensor_copy(
                     out=sorted_words[m][:, i * width : (i + 1) * width],
-                    in_=raw.rearrange("p (g q u) -> p g u q", g=width, u=2),
+                    in_=raw.rearrange("p (g w u) -> p g u w", g=width, u=2),
                 )
 
-        def sort_codes_but_last(m):
+        def sort_first_passes(m):
             sorted_words[m] = ring.tile([P, 4, 2, P], F32, name="sorted%d" % m, tag="sorted", bufs=2, align_bytes=64)
             raw = codes_raw[m][:, 0 : SORTED_PASSES * 512].bitcast(F32)
             nc.vector.tensor_copy(
-                out=sorted_words[m][:, 0:SORTED_PASSES].rearrange("p g u q -> p u g q"),
-                in_=raw.rearrange("p (g q u) -> p u g q", g=SORTED_PASSES, u=2),
+                out=sorted_words[m][:, 0:SORTED_PASSES].rearrange("p g u w -> p u g w"),
+                in_=raw.rearrange("p (g w u) -> p u g w", g=SORTED_PASSES, u=2),
             )
 
         def turn_codes(m):
@@ -159,7 +155,7 @@ def tile_codebook_patch_mixer_t2_kernel(
                 for i in range(2):
                     g = 2 * b + i
                     for u in range(2):
-                        if m in UNSORTED or (2 < m < TILES - 1 and g >= SORTED_PASSES):
+                        if m == UNSORTED_TILE or (UNSORTED_TILE < m < TILES - 1 and g >= SORTED_PASSES):
                             source = words[:, 256 * g + u : 256 * (g + 1) : 2]
                         else:
                             source = sorted_words[m][:, g, u, :]
@@ -171,7 +167,7 @@ def tile_codebook_patch_mixer_t2_kernel(
                     grouped[m, b] = ring.tile(
                         [P, 2, P, 4], BF16, name="grouped%d%d" % (m, b), tag="grouped", bufs=5, align_bytes=64
                     )
-                nc.scalar.copy(out=grouped[m, b][:].bitcast(F32), in_=turned[b][:].rearrange("p i u m -> p i m u"))
+                nc.scalar.copy(out=grouped[m, b][:].bitcast(F32), in_=turned[b][:].rearrange("p i u n -> p i n u"))
                 give_bank("turn%d%d" % (m, b))
 
         def quantize_codes(m):
@@ -180,7 +176,7 @@ def tile_codebook_patch_mixer_t2_kernel(
                 nc.vector.quantize_mx(
                     out=codes_q[m][:, cols].bitcast(FP8X4),
                     scales=codes_s[m][:, cols],
-                    in_=grouped[m, b][:].rearrange("p g m t -> p (g m t)"),
+                    in_=grouped[m, b][:].rearrange("p g n t -> p (g n t)"),
                 )
 
         def book_passes(acc, m, h, c0, width):
@@ -213,7 +209,9 @@ def tile_codebook_patch_mixer_t2_kernel(
         def scale_y(m, h, c0=0, c1=HALF):
             g, t = m // 4, m % 4
             if t == 0:
-                e_rows[g, h] = ring.tile([P, 4, HALF], BF16, name="e_rows%d%d" % (g, h), tag="e_rows", bufs=3, align_bytes=64)
+                e_rows[g, h] = ring.tile(
+                    [P, 4, HALF], BF16, name="e_rows%d%d" % (g, h), tag="e_rows", bufs=3, align_bytes=64
+                )
             nc.scalar.activation(
                 out=e_rows[g, h][:, t, c0:c1], in_=y_sb[m, h][:, c0:c1], func=ACT.Copy, scale=gain[:, m : m + 1]
             )
@@ -254,10 +252,10 @@ def tile_codebook_patch_mixer_t2_kernel(
                     in_=e_words[g, h, share][:].rearrange("p c t -> p (c t)"),
                 )
 
-        def deal_row_words(part):
+        def deal_row_words(group):
             nc.vector.tensor_copy(
-                out=row_w[part][:].bitcast(U16).rearrange("p (g t c m) -> p g c t m", g=2, t=4, m=8),
-                in_=row_w_raw[part[0] // 4][:].bitcast(U16).rearrange("p g (c m t) -> p g c t m", m=8, t=4),
+                out=row_w[group][:].bitcast(U16).rearrange("p (g t c n) -> p g c t n", g=2, t=4, n=8),
+                in_=row_w_raw[group][:].bitcast(U16).rearrange("p g (c n t) -> p g c t n", n=8, t=4),
             )
 
         def load_row_scales():
@@ -268,23 +266,24 @@ def tile_codebook_patch_mixer_t2_kernel(
 
         def deal_row_scales():
             nc.vector.tensor_copy(
-                out=row_s_dealt[:].rearrange("p (a t m) -> p a t m", a=2, t=4),
-                in_=row_s_raw[:].rearrange("p (a m t) -> p a t m", a=2, t=4),
+                out=row_s_dealt[:].rearrange("p (a t n) -> p a t n", a=2, t=4),
+                in_=row_s_raw[:].rearrange("p (a n t) -> p a t n", a=2, t=4),
             )
 
         def place_row_scales():
+            dealt = row_s_dealt[:].bitcast(I32)
             for r in range(4):
-                nc.sync.dma_start(out=row_s[:].bitcast(I32)[r:P:32], in_=row_s_dealt[:].bitcast(I32)[8 * r : 8 * (r + 1)])
+                nc.sync.dma_start(out=row_s[:].bitcast(I32)[r:P:32], in_=dealt[8 * r : 8 * (r + 1)])
 
         mixed, z_sb, z_turned, z_grouped = {}, {}, {}, {}
 
         def row_pass(m, h, g):
             if g == 0:
                 mixed[m, h] = take_bank("row%d%d" % (m, h), [P, HALF])
-            part, at = row_at[m]
+            first = (4 * g + m % 4) * P
             nc.tensor.matmul_mx(
                 out=mixed[m, h][:],
-                lhsT=row_w[part][:, 2 * at[g] : 2 * (at[g] + P)].bitcast(FP4X4),
+                lhsT=row_w[m // 4][:, 2 * first : 2 * (first + P)].bitcast(FP4X4),
                 lhsT_scale=row_s[:, g, m * P : (m + 1) * P],
                 rhs=e_q[g, h][:].bitcast(FP8X4),
                 rhs_scale=e_s[g, h][:],
@@ -300,38 +299,37 @@ def tile_codebook_patch_mixer_t2_kernel(
             if h == 0:
                 z_sb[m] = kept("z%d" % m, [P, 2 * HALF], BF16, tag="codes_raw%d" % m)
             if m < ON_TENSOR:
-                target = z_sb[m][:, h * HALF : (h + 1) * HALF].rearrange("p (u q j e) -> p u q j e", u=2, q=4, e=2)
+                target = z_sb[m][:, h * HALF : (h + 1) * HALF].rearrange("p (u d j s) -> p u d j s", u=2, d=4, s=2)
             else:
-                target = z_sb[m][:].rearrange("p (q h u j e) -> p h u q j e", q=4, h=2, u=2, e=2)[:, h]
+                target = z_sb[m][:].rearrange("p (d h u j s) -> p h u d j s", d=4, h=2, u=2, s=2)[:, h]
             nc.vector.tensor_tensor(
                 out=target,
-                in0=mixed[m, h][:].rearrange("p (q j u e) -> p u q j e", q=4, u=2, e=2),
-                in1=y_sb[m, h][:].rearrange("p (q j u e) -> p u q j e", q=4, u=2, e=2),
+                in0=mixed[m, h][:].rearrange("p (d j u s) -> p u d j s", d=4, u=2, s=2),
+                in1=y_sb[m, h][:].rearrange("p (d j u s) -> p u d j s", d=4, u=2, s=2),
                 op=ADD,
             )
             give_bank("row%d%d" % (m, h))
 
-        z_back, z_blocks = {}, {}
+        z_moved, z_blocks = {}, {}
 
-        def park_z(m):
-            z_back[m] = kept("z_back%d" % m, [P, 2 * HALF], BF16, tag="codes_q%d" % m)
-            for q in range(4):
+        def move_z(m):
+            z_moved[m] = kept("z_moved%d" % m, [P, 2 * HALF], BF16, tag="codes_q%d" % m)
+            for d in range(4):
                 nc.sync.dma_start(
-                    out=z_back[m][32 * q : 32 * (q + 1), :].rearrange("i (a w) -> i a w", a=4),
-                    in_=z_sb[m][:, q * SHARE : (q + 1) * SHARE],
+                    out=z_moved[m][32 * d : 32 * (d + 1), :].rearrange("i (a w) -> i a w", a=4),
+                    in_=z_sb[m][:, d * PART : (d + 1) * PART],
                 )
 
         def turn_z_blocks(m):
             z_blocks[m] = ring.tile([P, HALF], F32, name="z_blocks%d" % m, tag="sorted", bufs=2, align_bytes=64)
-            nc.vector.transpose(out=z_blocks[m][:], in_=z_back[m][:].bitcast(F32))
+            nc.vector.transpose(out=z_blocks[m][:], in_=z_moved[m][:].bitcast(F32))
 
         def group_z_blocks(m):
             z_grouped[m] = ring.tile([P, 2, P, 4], BF16, name="z_grouped%d" % m, tag="grouped", bufs=5, align_bytes=64)
             blocks = z_blocks[m][:].rearrange("p (a b h u i) -> p h a i b u", a=2, b=2, h=2, u=2)
             for h in range(2):
-                nc.scalar.copy(
-                    out=z_grouped[m][:, h].bitcast(F32).rearrange("p (i a b) u -> p a i b u", a=2, b=2), in_=blocks[:, h]
-                )
+                words = z_grouped[m][:, h].bitcast(F32).rearrange("p (i a b) u -> p a i b u", a=2, b=2)
+                nc.scalar.copy(out=words, in_=blocks[:, h])
 
         def turn_z(m):
             z_turned[m] = take_bank("turn_z%d" % m, [P, 2, 2, P])
@@ -346,7 +344,7 @@ def tile_codebook_patch_mixer_t2_kernel(
             for i in range(parts):
                 passes = slice(2 * i // parts, 2 * (i + 1) // parts)
                 nc.scalar.copy(
-                    out=z_grouped[m][:, passes].bitcast(F32), in_=z_turned[m][:, passes].rearrange("p h u m -> p h m u")
+                    out=z_grouped[m][:, passes].bitcast(F32), in_=z_turned[m][:, passes].rearrange("p h u n -> p h n u")
                 )
             give_bank("turn_z%d" % m)
 
@@ -357,7 +355,7 @@ def tile_codebook_patch_mixer_t2_kernel(
                 nc.vector.quantize_mx(
                     out=z_q[m][:, cols].bitcast(FP8X4),
                     scales=z_s[m][:, cols],
-                    in_=z_grouped[m][:, passes].rearrange("p h m t -> p (h m t)"),
+                    in_=z_grouped[m][:, passes].rearrange("p h n t -> p (h n t)"),
                 )
 
         h_sums, gates = {}, {}
@@ -385,29 +383,35 @@ def tile_codebook_patch_mixer_t2_kernel(
             nc.scalar.activation(out=gates[m, c0][:], in_=h_sums[m, 2 * HALF + c0][:], func=ACT.Tanh)
             give_bank("chan%d_%d" % (m, 2 * HALF + c0))
 
-        def store_product(m, c0, width):
-            result = ring.tile(
+        def new_result(m, c0, width):
+            return ring.tile(
                 [P, width], F32, name="result%d_%d" % (m, c0), tag="result%d" % width, bufs=7 if width == HALF else 4
             )
-            nc.vector.tensor_tensor(out=result[:], in0=h_sums[m, c0][:], in1=gates[m, c0][:], op=MULT)
-            give_bank("chan%d_%d" % (m, c0))
+
+        def store(m, c0, width, result):
             nc.sync.dma_start(out=out_v[m // 4, m % 4][:, c0 : c0 + width], in_=result[:])
 
-        def store_product_pool(m, c0):
+        def store_product(m, c0, width):
+            result = new_result(m, c0, width)
+            nc.vector.tensor_tensor(out=result[:], in0=h_sums[m, c0][:], in1=gates[m, c0][:], op=MULT)
+            give_bank("chan%d_%d" % (m, c0))
+            store(m, c0, width, result)
+
+        pool_results = {}
+
+        def pool_product(m, c0):
             values = ring.tile([P, HALF], F32, name="values%d_%d" % (m, c0), tag="values", bufs=2)
             nc.scalar.copy(out=values[:], in_=h_sums[m, c0][:])
             give_bank("chan%d_%d" % (m, c0))
-            result = ring.tile([P, HALF], F32, name="result%d_%d" % (m, c0), tag="result%d" % HALF, bufs=7)
-            nc.gpsimd.tensor_tensor(out=result[:], in0=values[:], in1=gates[m, c0][:], op=MULT)
-            return result
+            pool_results[m, c0] = new_result(m, c0, HALF)
+            nc.gpsimd.tensor_tensor(out=pool_results[m, c0][:], in0=values[:], in1=gates[m, c0][:], op=MULT)
 
-        def store(m, c0, result):
-            nc.sync.dma_start(out=out_v[m // 4, m % 4][:, c0 : c0 + HALF], in_=result[:])
+        def store_pool_result(m, c0):
+            store(m, c0, HALF, pool_results[m, c0])
 
-        def out_half(m, n):
+        def half_products(m, n):
             gate_product(m, n * HALF, HALF)
             chan_product(m, n * HALF, HALF)
-            store_product(m, n * HALF, HALF)
 
         load_codes(0, parts=2)
         load_codes(1)
@@ -419,7 +423,7 @@ def tile_codebook_patch_mixer_t2_kernel(
             if m == 2:
                 nc.sync.dma_start(out=gain_raw[:], in_=patch_gain.rearrange("(g p t) -> p g t", p=P, t=4))
 
-        warm_up("warm0", 4)
+        warm_up("warm0", 3)
         sort_codes(0, parts=2)
         turn_codes(0)
         warm_up("warm1", 2)
@@ -450,14 +454,14 @@ def tile_codebook_patch_mixer_t2_kernel(
         nc.vector.tensor_copy(out=gain[:], in_=gain_raw[:].rearrange("p g t -> p (g t)"))
         scale_y(0, 0)
         book_product(1, 0)
-        sort_codes_but_last(3)
+        sort_first_passes(3)
         quantize_codes(2)
         for m in range(2, TILES - 1):
             turn_codes(m + 1)
             finish_y(m - 1, 0)
             book_product(m, 0)
             if m + 2 < TILES - 1:
-                sort_codes_but_last(m + 2)
+                sort_first_passes(m + 2)
             elif m + 2 == TILES - 1:
                 sort_codes(m + 2)
             else:
@@ -476,7 +480,7 @@ def tile_codebook_patch_mixer_t2_kernel(
         finish_y(0, 1)
         book_product(1, 1)
         finish_y(7, 0)
-        deal_row_words(ROW_PARTS[0])
+        deal_row_words(0)
         quantize_e(0, 0, (1, 0))
         book_product(2, 1)
         add_x(1, 1)
@@ -485,7 +489,7 @@ def tile_codebook_patch_mixer_t2_kernel(
         for m in (3, 4):
             book_product(m, 1)
             finish_y(m - 1, 1)
-        deal_row_words(ROW_PARTS[1])
+        deal_row_words(1)
         quantize_e(1, 0, (1, 0))
         book_product(5, 1)
         add_x(4, 1)
@@ -503,7 +507,7 @@ def tile_codebook_patch_mixer_t2_kernel(
         for c0 in (0, SHARE):
             scale_y(7, 1, c0, c0 + SHARE)
 
-        for m in range(5):
+        for m in range(EARLY_ROWS):
             row_product(m, 0)
         for share in range(2):
             new_e_words(1, 1, share, "e_words1%d" % share)
@@ -526,56 +530,56 @@ def tile_codebook_patch_mixer_t2_kernel(
         group_z(0, parts=2)
         add_y(2, 1)
         group_z(1)
-        park_z(2)
+        move_z(2)
         quantize_z(0, parts=2)
         row_product(4, 1)
         row_product(5, 0)
         add_y(3, 0)
         add_y(3, 1)
-        park_z(3)
+        move_z(3)
         quantize_z(1)
         add_y(4, 0)
         add_y(4, 1)
-        park_z(4)
-        early = {}
+        move_z(4)
+
         for n in range(2):
-            gate_product(0, n * HALF, HALF)
-            chan_product(0, n * HALF, HALF)
-            early[n] = store_product_pool(0, n * HALF)
+            half_products(0, n)
+            pool_product(0, n * HALF)
         row_product(5, 1)
         add_y(5, 0)
         add_y(5, 1)
-        park_z(5)
+        move_z(5)
         for n in range(2):
             turn_z_blocks(2 + n)
             for h in range(2):
                 row_product(6 + n, h)
                 add_y(6 + n, h)
-            park_z(6 + n)
-            store(0, n * HALF, early[n])
+            move_z(6 + n)
+            store_pool_result(0, n * HALF)
             group_z_blocks(2 + n)
-            gate_product(1, n * HALF, HALF)
-            chan_product(1, n * HALF, HALF)
-            early[2 + n] = store_product_pool(1, n * HALF)
+            half_products(1, n)
+            pool_product(1, n * HALF)
             quantize_z(2 + n)
         turn_z_blocks(4)
-        store(1, 0, early[2])
-        for m in range(2, TILES - 1):
-            gate_product(m, 0, HALF)
-            chan_product(m, 0, HALF)
-            if m == 2:
-                group_z_blocks(4)
-                turn_z_blocks(5)
-                store(1, HALF, early[3])
-            else:
-                store_product(m - 1, HALF, HALF)
+        store_pool_result(1, 0)
+
+        half_products(2, 0)
+        group_z_blocks(4)
+        turn_z_blocks(5)
+        store_pool_result(1, HALF)
+        quantize_z(4)
+        store_product(2, 0, HALF)
+        half_products(2, 1)
+        group_z_blocks(5)
+        for m in range(3, TILES - 1):
+            half_products(m, 0)
+            store_product(m - 1, HALF, HALF)
             if m + 2 < TILES:
                 quantize_z(m + 2)
-            if m > 2 and m + 3 < TILES:
+            if m + 3 < TILES:
                 turn_z_blocks(m + 3)
             store_product(m, 0, HALF)
-            gate_product(m, HALF, HALF)
-            chan_product(m, HALF, HALF)
+            half_products(m, 1)
             if m + 3 < TILES:
                 group_z_blocks(m + 3)
         store_product(TILES - 2, HALF, HALF)

@@ -21,11 +21,8 @@ P = 128
 TILES = 8
 HALF = 512
 SHARE = 256
-PART = 256
 UNSORTED_TILE = 2
-SORTED_PASSES = 3
-ON_TENSOR = 2
-EARLY_ROWS = 5
+BY_HALVES = 1
 
 
 def tile_codebook_patch_mixer_t2_kernel(
@@ -40,6 +37,9 @@ def tile_codebook_patch_mixer_t2_kernel(
 
         def kept(name, shape, dtype, tag=None):
             return keep.tile(shape, dtype, name=name, tag=tag or name, align_bytes=64)
+
+        def ringed(name, shape, dtype, tag, bufs):
+            return ring.tile(shape, dtype, name=name, tag=tag, bufs=bufs, align_bytes=64)
 
         free_banks = list(range(8))
         bank_of = {}
@@ -131,7 +131,7 @@ def tile_codebook_patch_mixer_t2_kernel(
         sorted_words, turned, grouped, sums = {}, {}, {}, {}
 
         def sort_codes(m, parts=1):
-            sorted_words[m] = ring.tile([P, 4, 2, P], F32, name="sorted%d" % m, tag="sorted", bufs=2, align_bytes=64)
+            sorted_words[m] = ringed("sorted%d" % m, [P, 4, 2, P], F32, "sorted", 3)
             width = 4 // parts
             for i in range(parts):
                 raw = codes_raw[m][:, i * width * 512 : (i + 1) * width * 512].bitcast(F32)
@@ -140,38 +140,27 @@ def tile_codebook_patch_mixer_t2_kernel(
                     in_=raw.rearrange("p (g w u) -> p g u w", g=width, u=2),
                 )
 
-        def sort_first_passes(m):
-            sorted_words[m] = ring.tile([P, 4, 2, P], F32, name="sorted%d" % m, tag="sorted", bufs=2, align_bytes=64)
-            raw = codes_raw[m][:, 0 : SORTED_PASSES * 512].bitcast(F32)
-            nc.vector.tensor_copy(
-                out=sorted_words[m][:, 0:SORTED_PASSES].rearrange("p g u w -> p u g w"),
-                in_=raw.rearrange("p (g w u) -> p u g w", g=SORTED_PASSES, u=2),
-            )
-
         def turn_codes(m):
             words = codes_raw[m][:].bitcast(F32)
             for b in range(2):
-                turned[b] = take_bank("turn%d%d" % (m, b), [P, 2, 2, P])
+                turned[m, b] = take_bank("turn%d%d" % (m, b), [P, 2, 2, P])
                 for i in range(2):
                     g = 2 * b + i
                     for u in range(2):
-                        if m == UNSORTED_TILE or (UNSORTED_TILE < m < TILES - 1 and g >= SORTED_PASSES):
+                        if m == UNSORTED_TILE:
                             source = words[:, 256 * g + u : 256 * (g + 1) : 2]
                         else:
                             source = sorted_words[m][:, g, u, :]
-                        nc.tensor.transpose(turned[b][:, i, u, :], source, ident[:])
+                        nc.tensor.transpose(turned[m, b][:, i, u, :], source, ident[:])
+
+        def group_codes(m):
             for b in range(2):
-                if (m, b) == (TILES - 1, 1):
-                    grouped[m, b] = kept("grouped_last", [P, 2, P, 4], BF16, tag="pool_out")
-                else:
-                    grouped[m, b] = ring.tile(
-                        [P, 2, P, 4], BF16, name="grouped%d%d" % (m, b), tag="grouped", bufs=5, align_bytes=64
-                    )
-                nc.scalar.copy(out=grouped[m, b][:].bitcast(F32), in_=turned[b][:].rearrange("p i u n -> p i n u"))
+                grouped[m, b] = ringed("grouped%d%d" % (m, b), [P, 2, P, 4], BF16, "grouped", 5)
+                nc.scalar.copy(out=grouped[m, b][:].bitcast(F32), in_=turned[m, b][:].rearrange("p i u n -> p i n u"))
                 give_bank("turn%d%d" % (m, b))
 
-        def quantize_codes(m):
-            for b in range(2):
+        def quantize_codes(m, banks=(0, 1)):
+            for b in banks:
                 cols = slice(b * 2 * P, (b + 1) * 2 * P)
                 nc.vector.quantize_mx(
                     out=codes_q[m][:, cols].bitcast(FP8X4),
@@ -179,10 +168,11 @@ def tile_codebook_patch_mixer_t2_kernel(
                     in_=grouped[m, b][:].rearrange("p g n t -> p (g n t)"),
                 )
 
-        def book_passes(acc, m, h, c0, width):
+        def book_product(m, h, c0=0, width=HALF):
+            sums[m, h, c0] = take_bank("book%d%d%d" % (m, h, c0), [P, width])
             for g in range(4):
                 nc.tensor.matmul_mx(
-                    out=acc,
+                    out=sums[m, h, c0][:],
                     lhsT=codes_q[m][:, g * P : (g + 1) * P].bitcast(FP8X4),
                     lhsT_scale=codes_s[m][:, g * P : (g + 1) * P],
                     rhs=book_w[h][:, g, 2 * c0 : 2 * (c0 + width)].bitcast(FP4X4),
@@ -191,34 +181,29 @@ def tile_codebook_patch_mixer_t2_kernel(
                     stop=(g == 3),
                 )
 
-        def book_product(m, h):
-            sums[m, h, 0] = take_bank("book%d%d0" % (m, h), [P, HALF])
-            book_passes(sums[m, h, 0][:], m, h, 0, HALF)
-
-        def book_product_share(m, h, c0):
-            sums[m, h, c0] = take_bank("book%d%d%d" % (m, h, c0), [P, SHARE])
-            for i in range(0, SHARE, P):
-                book_passes(sums[m, h, c0][:, i : i + P], m, h, c0 + i, P)
-
-        def add_x(m, h, c0=0, c1=HALF):
-            nc.vector.tensor_tensor(out=y_sb[m, h][:, c0:c1], in0=sums[m, h, c0][:], in1=x_sb[m, h][:, c0:c1], op=ADD)
+        def add_x(m, h, c0=0, width=HALF):
+            acc, cols = sums[m, h, c0][:], slice(c0, c0 + width)
+            if h == 0:
+                nc.vector.tensor_tensor(
+                    out=y_sb[m, h][:].rearrange("p (u w s) -> p u w s", u=2, s=2),
+                    in0=acc.rearrange("p (w u s) -> p u w s", u=2, s=2),
+                    in1=x_sb[m, h][:].rearrange("p (w u s) -> p u w s", u=2, s=2),
+                    op=ADD,
+                )
+            else:
+                nc.vector.tensor_tensor(out=y_sb[m, h][:, cols], in0=acc, in1=x_sb[m, h][:, cols], op=ADD)
             give_bank("book%d%d%d" % (m, h, c0))
 
         e_rows, e_words = {}, {}
 
-        def scale_y(m, h, c0=0, c1=HALF):
+        def scale_y(m, h, c0=0, width=HALF):
             g, t = m // 4, m % 4
-            if t == 0:
-                e_rows[g, h] = ring.tile(
-                    [P, 4, HALF], BF16, name="e_rows%d%d" % (g, h), tag="e_rows", bufs=3, align_bytes=64
-                )
+            if (g, h) not in e_rows:
+                e_rows[g, h] = ringed("e_rows%d%d" % (g, h), [P, 4, HALF], BF16, "e_rows", 3)
+            cols = slice(c0, c0 + width)
             nc.scalar.activation(
-                out=e_rows[g, h][:, t, c0:c1], in_=y_sb[m, h][:, c0:c1], func=ACT.Copy, scale=gain[:, m : m + 1]
+                out=e_rows[g, h][:, t, cols], in_=y_sb[m, h][:, cols], func=ACT.Copy, scale=gain[:, m : m + 1]
             )
-
-        def finish_y(m, h):
-            add_x(m, h)
-            scale_y(m, h)
 
         def new_e_words(g, h, share, tag):
             e_words[g, h, share] = kept("e_words%d%d%d" % (g, h, share), [P, SHARE, 4], BF16, tag=tag)
@@ -230,18 +215,15 @@ def tile_codebook_patch_mixer_t2_kernel(
                 in_=e_rows[g, h][:, :, c0:c1].rearrange("p t (c i) -> p c t i", i=4),
             )
 
-        def interleave_shared(g, h):
-            new_e_words(g, h, 0, "pool_out")
+        def interleave_on_pool(g, h, share):
             nc.gpsimd.tensor_scalar(
-                out=e_words[g, h, 0][:],
-                in0=e_rows[g, h][:, :, 0:SHARE].rearrange("p t c -> p c t"),
+                out=e_words[g, h, share][:],
+                in0=e_rows[g, h][:, :, share * SHARE : (share + 1) * SHARE].rearrange("p t c -> p c t"),
                 scalar1=1.0,
                 scalar2=1.0,
                 op0=MULT,
                 op1=MULT,
             )
-            new_e_words(g, h, 1, "e_words%d1" % g)
-            interleave(nc.scalar.copy, g, h, SHARE, HALF)
 
         def quantize_e(g, h, shares):
             for share in shares:
@@ -275,136 +257,146 @@ def tile_codebook_patch_mixer_t2_kernel(
             for r in range(4):
                 nc.sync.dma_start(out=row_s[:].bitcast(I32)[r:P:32], in_=dealt[8 * r : 8 * (r + 1)])
 
-        mixed, z_sb, z_turned, z_grouped = {}, {}, {}, {}
-
-        def row_pass(m, h, g):
-            if g == 0:
-                mixed[m, h] = take_bank("row%d%d" % (m, h), [P, HALF])
-            first = (4 * g + m % 4) * P
-            nc.tensor.matmul_mx(
-                out=mixed[m, h][:],
-                lhsT=row_w[m // 4][:, 2 * first : 2 * (first + P)].bitcast(FP4X4),
-                lhsT_scale=row_s[:, g, m * P : (m + 1) * P],
-                rhs=e_q[g, h][:].bitcast(FP8X4),
-                rhs_scale=e_s[g, h][:],
-                start=(g == 0),
-                stop=(g == 1),
-            )
+        mixed, z_sb, z_moved, z_blocks, z_grouped = {}, {}, {}, {}, {}
 
         def row_product(m, h):
+            mixed[m, h] = take_bank("row%d%d" % (m, h), [P, HALF])
             for g in range(2):
-                row_pass(m, h, g)
+                first = (4 * g + m % 4) * P
+                nc.tensor.matmul_mx(
+                    out=mixed[m, h][:],
+                    lhsT=row_w[m // 4][:, 2 * first : 2 * (first + P)].bitcast(FP4X4),
+                    lhsT_scale=row_s[:, g, m * P : (m + 1) * P],
+                    rhs=e_q[g, h][:].bitcast(FP8X4),
+                    rhs_scale=e_s[g, h][:],
+                    start=(g == 0),
+                    stop=(g == 1),
+                )
+
+        def z_target(m, h):
+            if m not in z_sb:
+                z_sb[m] = kept("z%d" % m, [P, 2 * HALF], BF16, tag="codes_raw%d" % m)
+            if m < BY_HALVES:
+                return z_sb[m][:].rearrange("p (h d u k) -> p h u d k", d=4, h=2, u=2)[:, h]
+            return z_sb[m][:].rearrange("p (d h u k) -> p h u d k", d=4, h=2, u=2)[:, h]
 
         def add_y(m, h):
+            target = z_target(m, h)
             if h == 0:
-                z_sb[m] = kept("z%d" % m, [P, 2 * HALF], BF16, tag="codes_raw%d" % m)
-            if m < ON_TENSOR:
-                target = z_sb[m][:, h * HALF : (h + 1) * HALF].rearrange("p (u d j s) -> p u d j s", u=2, d=4, s=2)
+                order = dict(u=2, d=4)
+                nc.vector.tensor_tensor(
+                    out=target,
+                    in0=mixed[m, h][:].rearrange("p (u d k) -> p u d k", **order),
+                    in1=y_sb[m, h][:].rearrange("p (u d k) -> p u d k", **order),
+                    op=ADD,
+                )
             else:
-                target = z_sb[m][:].rearrange("p (d h u j s) -> p h u d j s", d=4, h=2, u=2, s=2)[:, h]
-            nc.vector.tensor_tensor(
-                out=target,
-                in0=mixed[m, h][:].rearrange("p (d j u s) -> p u d j s", d=4, u=2, s=2),
-                in1=y_sb[m, h][:].rearrange("p (d j u s) -> p u d j s", d=4, u=2, s=2),
-                op=ADD,
-            )
+                order = dict(u=2, d=4, s=2)
+                nc.vector.tensor_tensor(
+                    out=target.rearrange("p u d (j s) -> p u d j s", s=2),
+                    in0=mixed[m, h][:].rearrange("p (d j u s) -> p u d j s", **order),
+                    in1=y_sb[m, h][:].rearrange("p (d j u s) -> p u d j s", **order),
+                    op=ADD,
+                )
             give_bank("row%d%d" % (m, h))
 
-        z_moved, z_blocks = {}, {}
+        spilled = {}
 
-        def move_z(m):
-            z_moved[m] = kept("z_moved%d" % m, [P, 2 * HALF], BF16, tag="codes_q%d" % m)
+        def spill_row(m):
+            spilled[m] = ringed("spilled%d" % m, [P, HALF], F32, "values", 4)
+            nc.scalar.copy(out=spilled[m][:], in_=mixed[m, 0][:])
+            give_bank("row%d0" % m)
+
+        def add_y_on_pool(m):
+            nc.gpsimd.tensor_tensor(
+                out=z_target(m, 0),
+                in0=spilled[m][:].rearrange("p (u d k) -> p u d k", u=2, d=4),
+                in1=y_sb[m, 0][:].rearrange("p (u d k) -> p u d k", u=2, d=4),
+                op=ADD,
+            )
+
+        def span(h):
+            return (0, 2) if h is None else (h, 1)
+
+        def move_z(m, h=None):
+            first, count = span(h)
+            if m not in z_moved:
+                z_moved[m] = kept("z_moved%d" % m, [P, 2 * HALF], BF16, tag="codes_q%d" % m)
+            part = count * P
             for d in range(4):
-                nc.sync.dma_start(
-                    out=z_moved[m][32 * d : 32 * (d + 1), :].rearrange("i (a w) -> i a w", a=4),
-                    in_=z_sb[m][:, d * PART : (d + 1) * PART],
-                )
+                room = z_moved[m][32 * d : 32 * (d + 1), first * HALF : (first + count) * HALF]
+                start = first * HALF + d * part
+                nc.sync.dma_start(out=room.rearrange("i (a w) -> i a w", a=4), in_=z_sb[m][:, start : start + part])
 
-        def turn_z_blocks(m):
-            z_blocks[m] = ring.tile([P, HALF], F32, name="z_blocks%d" % m, tag="sorted", bufs=2, align_bytes=64)
-            nc.vector.transpose(out=z_blocks[m][:], in_=z_moved[m][:].bitcast(F32))
+        def turn_z(m, h=None):
+            first, count = span(h)
+            z_blocks[m, h] = ringed("z_blocks%d_%d" % (m, first), [P, count * SHARE], F32, "sorted", 3)
+            words = z_moved[m][:].bitcast(F32)[:, first * SHARE : (first + count) * SHARE]
+            nc.vector.transpose(out=z_blocks[m, h][:], in_=words)
 
-        def group_z_blocks(m):
-            z_grouped[m] = ring.tile([P, 2, P, 4], BF16, name="z_grouped%d" % m, tag="grouped", bufs=5, align_bytes=64)
-            blocks = z_blocks[m][:].rearrange("p (a b h u i) -> p h a i b u", a=2, b=2, h=2, u=2)
-            for h in range(2):
-                words = z_grouped[m][:, h].bitcast(F32).rearrange("p (i a b) u -> p a i b u", a=2, b=2)
-                nc.scalar.copy(out=words, in_=blocks[:, h])
+        def group_z(m, h=None):
+            first, count = span(h)
+            z_grouped[m, h] = kept("z_grouped%d_%d" % (m, first), [P, count, P, 4], BF16, tag="y%d%d" % (m, first))
+            blocks = z_blocks[m, h][:].rearrange("p (a b h u i) -> p h a i b u", a=2, b=2, h=count, u=2)
+            for k in range(count):
+                words = z_grouped[m, h][:, k].bitcast(F32).rearrange("p (i a b) u -> p a i b u", a=2, b=2)
+                nc.scalar.copy(out=words, in_=blocks[:, k])
 
-        def turn_z(m):
-            z_turned[m] = take_bank("turn_z%d" % m, [P, 2, 2, P])
-            words = z_sb[m][:].bitcast(F32)
-            for h in range(2):
-                for u in range(2):
-                    run = slice((2 * h + u) * P, (2 * h + u + 1) * P)
-                    nc.tensor.transpose(z_turned[m][:, h, u, :], words[:, run], ident[:])
-
-        def group_z(m, parts=1):
-            z_grouped[m] = ring.tile([P, 2, P, 4], BF16, name="z_grouped%d" % m, tag="grouped", bufs=5, align_bytes=64)
-            for i in range(parts):
-                passes = slice(2 * i // parts, 2 * (i + 1) // parts)
-                nc.scalar.copy(
-                    out=z_grouped[m][:, passes].bitcast(F32), in_=z_turned[m][:, passes].rearrange("p h u n -> p h n u")
-                )
-            give_bank("turn_z%d" % m)
-
-        def quantize_z(m, parts=1):
-            for i in range(parts):
-                passes = slice(2 * i // parts, 2 * (i + 1) // parts)
-                cols = slice(passes.start * P, passes.stop * P)
-                nc.vector.quantize_mx(
-                    out=z_q[m][:, cols].bitcast(FP8X4),
-                    scales=z_s[m][:, cols],
-                    in_=z_grouped[m][:, passes].rearrange("p h n t -> p (h n t)"),
-                )
+        def quantize_z(m, h=None):
+            first, count = span(h)
+            cols = slice(first * P, (first + count) * P)
+            nc.vector.quantize_mx(
+                out=z_q[m][:, cols].bitcast(FP8X4),
+                scales=z_s[m][:, cols],
+                in_=z_grouped[m, h][:].rearrange("p h n t -> p (h n t)"),
+            )
 
         h_sums, gates = {}, {}
 
         def chan_product(m, c0, width):
             h_sums[m, c0] = take_bank("chan%d_%d" % (m, c0), [P, width])
-            group = HALF if width == HALF else P
-            for i in range(0, width, group):
-                for h in range(2):
-                    nc.tensor.matmul_mx(
-                        out=h_sums[m, c0][:, i : i + group],
-                        lhsT=z_q[m][:, h * P : (h + 1) * P].bitcast(FP8X4),
-                        lhsT_scale=z_s[m][:, h * P : (h + 1) * P],
-                        rhs=chan_w[h][:, 2 * (c0 + i) : 2 * (c0 + i + group)].bitcast(FP4X4),
-                        rhs_scale=chan_s[:, h, c0 + i : c0 + i + group],
-                        start=(h == 0),
-                        stop=(h == 1),
-                    )
+            for h in range(2):
+                nc.tensor.matmul_mx(
+                    out=h_sums[m, c0][:],
+                    lhsT=z_q[m][:, h * P : (h + 1) * P].bitcast(FP8X4),
+                    lhsT_scale=z_s[m][:, h * P : (h + 1) * P],
+                    rhs=chan_w[h][:, 2 * c0 : 2 * (c0 + width)].bitcast(FP4X4),
+                    rhs_scale=chan_s[:, h, c0 : c0 + width],
+                    start=(h == 0),
+                    stop=(h == 1),
+                )
 
         def gate_product(m, c0, width):
             chan_product(m, 2 * HALF + c0, width)
-            gates[m, c0] = ring.tile(
-                [P, width], F32, name="gate%d_%d" % (m, c0), tag="gate%d" % width, bufs=5 if width == HALF else 4
-            )
+            gates[m, c0] = ringed("gate%d_%d" % (m, c0), [P, width], F32, "gate%d" % width, 6 if width == HALF else 4)
             nc.scalar.activation(out=gates[m, c0][:], in_=h_sums[m, 2 * HALF + c0][:], func=ACT.Tanh)
             give_bank("chan%d_%d" % (m, 2 * HALF + c0))
 
         def new_result(m, c0, width):
-            return ring.tile(
-                [P, width], F32, name="result%d_%d" % (m, c0), tag="result%d" % width, bufs=7 if width == HALF else 4
-            )
+            return ringed("result%d_%d" % (m, c0), [P, width], F32, "result%d" % width, 5 if width == HALF else 4)
 
         def store(m, c0, width, result):
             nc.sync.dma_start(out=out_v[m // 4, m % 4][:, c0 : c0 + width], in_=result[:])
 
-        def store_product(m, c0, width):
+        def store_product(m, c0, width=HALF):
             result = new_result(m, c0, width)
             nc.vector.tensor_tensor(out=result[:], in0=h_sums[m, c0][:], in1=gates[m, c0][:], op=MULT)
             give_bank("chan%d_%d" % (m, c0))
             store(m, c0, width, result)
 
-        pool_results = {}
+        pool_values, pool_results = {}, {}
 
-        def pool_product(m, c0):
-            values = ring.tile([P, HALF], F32, name="values%d_%d" % (m, c0), tag="values", bufs=2)
+        def spill_values(m, c0):
+            values = ringed("values%d_%d" % (m, c0), [P, HALF], F32, "values", 4)
             nc.scalar.copy(out=values[:], in_=h_sums[m, c0][:])
             give_bank("chan%d_%d" % (m, c0))
-            pool_results[m, c0] = new_result(m, c0, HALF)
-            nc.gpsimd.tensor_tensor(out=pool_results[m, c0][:], in0=values[:], in1=gates[m, c0][:], op=MULT)
+            pool_values[m, c0] = values
+
+        def pool_product(m, c0, room):
+            pool_results[m, c0] = kept("result%d_%d" % (m, c0), [P, HALF], F32, tag=room)
+            nc.gpsimd.tensor_tensor(
+                out=pool_results[m, c0][:], in0=pool_values[m, c0][:], in1=gates[m, c0][:], op=MULT
+            )
 
         def store_pool_result(m, c0):
             store(m, c0, HALF, pool_results[m, c0])
@@ -417,172 +409,254 @@ def tile_codebook_patch_mixer_t2_kernel(
         load_codes(1)
         load_scales(book_s[0], book_scales[:, :, scale_cols(0)])
         load_words(book_w[0], book_words[:, :, word_cols(0)])
-        for m in range(2, TILES):
+        for m in (2, 3, 4):
             load_codes(m)
-            load_x(m - 2, 0)
-            if m == 2:
-                nc.sync.dma_start(out=gain_raw[:], in_=patch_gain.rearrange("(g p t) -> p g t", p=P, t=4))
+        load_x(0, 0)
+        nc.sync.dma_start(out=gain_raw[:], in_=patch_gain.rearrange("(g p t) -> p g t", p=P, t=4))
+        load_x(1, 0)
+        load_x(2, 0)
 
         warm_up("warm0", 3)
         sort_codes(0, parts=2)
         turn_codes(0)
+        group_codes(0)
         warm_up("warm1", 2)
         sort_codes(1)
         quantize_codes(0)
         clear(row_s)
-        clear(chan_s)
         turn_codes(1)
+        group_codes(1)
         warm_up("warm2", 1)
 
-        load_row_scales()
+        load_codes(5)
+        load_x(3, 0)
         load_words(book_w[1], book_words[:, :, word_cols(1)])
         load_scales(book_s[1], book_scales[:, :, scale_cols(1)])
-        load_x(6, 0)
+        load_codes(6)
+        load_x(4, 0)
         load_x(0, 1)
-        load_words(row_w_raw[0], row_words[:, :, word_cols(0)])
-        load_x(7, 0)
+        load_codes(7)
         load_x(1, 1)
+        load_x(2, 1)
+        load_row_scales()
+        load_x(3, 1)
+        load_words(row_w_raw[0], row_words[:, :, word_cols(0)])
+        for m in (5, 6, 7):
+            load_x(m, 0)
         load_words(row_w_raw[1], row_words[:, :, word_cols(1)])
-        for m in range(2, TILES):
+        for m in range(4, TILES):
             load_x(m, 1)
 
         quantize_codes(1)
-
+        clear(chan_s)
         book_product(0, 0)
         turn_codes(2)
+        group_codes(2)
+        book_product(1, 0)
+        sort_codes(3)
+        quantize_codes(2, (0,))
+        turn_codes(3)
+        sort_codes(4)
+        quantize_codes(2, (1,))
+        turn_codes(4)
+        group_codes(3)
         add_x(0, 0)
         nc.vector.tensor_copy(out=gain[:], in_=gain_raw[:].rearrange("p g t -> p (g t)"))
+        book_product(2, 0)
+        add_x(1, 0)
+        quantize_codes(3)
+        group_codes(4)
         scale_y(0, 0)
-        book_product(1, 0)
-        sort_first_passes(3)
-        quantize_codes(2)
-        for m in range(2, TILES - 1):
-            turn_codes(m + 1)
-            finish_y(m - 1, 0)
-            book_product(m, 0)
-            if m + 2 < TILES - 1:
-                sort_first_passes(m + 2)
-            elif m + 2 == TILES - 1:
-                sort_codes(m + 2)
-            else:
-                deal_row_scales()
-            quantize_codes(m + 1)
+        scale_y(1, 0)
+        book_product(3, 0)
+        sort_codes(5)
+        quantize_codes(4)
+        add_x(2, 0)
+        scale_y(2, 0)
+        book_product(4, 0)
+        add_x(3, 0)
+        scale_y(3, 0)
+        new_e_words(0, 0, 1, "e_words_b")
+        interleave(nc.scalar.copy, 0, 0, SHARE, HALF)
+        book_product(0, 1)
+        sort_codes(6)
+        turn_codes(5)
+        turn_codes(6)
+        group_codes(5)
+        add_x(4, 0)
+        add_x(0, 1)
+        book_product(1, 1)
+        sort_codes(7)
+        group_codes(6)
+        quantize_codes(5)
+        new_e_words(0, 0, 0, "e_words_a")
+        interleave(nc.vector.tensor_copy, 0, 0, 0, SHARE)
+        book_product(2, 1)
+        add_x(1, 1)
+        turn_codes(7)
+        scale_y(4, 0)
+        scale_y(0, 1)
+        quantize_codes(6)
+        add_x(2, 1)
+        group_codes(7)
+        book_product(3, 1)
+        deal_row_scales()
         place_row_scales()
         for h in range(2):
             nc.sync.dma_start(out=chan_w[h][:].bitcast(I32), in_=chan_words[h].bitcast(I32))
         load_scales(chan_s, chan_scales)
-
-        book_product(0, 1)
-        add_x(6, 0)
-        interleave_shared(0, 0)
-        scale_y(6, 0)
-        book_product(7, 0)
-        finish_y(0, 1)
-        book_product(1, 1)
-        finish_y(7, 0)
+        quantize_e(0, 0, (0, 1))
+        book_product(5, 0)
+        add_x(3, 1)
+        for m in range(1, 4):
+            scale_y(m, 1)
+        quantize_codes(7)
         deal_row_words(0)
-        quantize_e(0, 0, (1, 0))
-        book_product(2, 1)
-        add_x(1, 1)
-        interleave_shared(1, 0)
-        scale_y(1, 1)
-        for m in (3, 4):
-            book_product(m, 1)
-            finish_y(m - 1, 1)
+        book_product(6, 0)
+        add_x(5, 0)
+        new_e_words(0, 1, 0, "e_words_a")
+        interleave_on_pool(0, 1, 0)
+        new_e_words(0, 1, 1, "e_words_b")
+        interleave(nc.scalar.copy, 0, 1, SHARE, HALF)
+        book_product(7, 0)
+        add_x(6, 0)
+        book_product(4, 1)
+        add_x(7, 0)
+        for m in range(5, TILES):
+            scale_y(m, 0)
+        quantize_e(0, 1, (0, 1))
         deal_row_words(1)
-        quantize_e(1, 0, (1, 0))
+        new_e_words(1, 0, 0, "e_words_a")
+        interleave_on_pool(1, 0, 0)
         book_product(5, 1)
         add_x(4, 1)
-        interleave_shared(0, 1)
+        new_e_words(1, 0, 1, "e_words_b")
+        interleave(nc.scalar.copy, 1, 0, SHARE, HALF)
+        book_product(6, 1, 0, SHARE)
+        add_x(5, 1)
         scale_y(4, 1)
-        book_product(6, 1)
-        finish_y(5, 1)
-
-        for c0 in (0, SHARE):
-            book_product_share(7, 1, c0)
-        finish_y(6, 1)
-        for c0 in (0, SHARE):
-            add_x(7, 1, c0, c0 + SHARE)
-        quantize_e(0, 1, (1, 0))
-        for c0 in (0, SHARE):
-            scale_y(7, 1, c0, c0 + SHARE)
-
-        for m in range(EARLY_ROWS):
+        scale_y(5, 1)
+        book_product(7, 1, 0, SHARE)
+        add_x(6, 1, 0, SHARE)
+        quantize_e(1, 0, (0, 1))
+        book_product(6, 1, SHARE, SHARE)
+        book_product(7, 1, SHARE, SHARE)
+        add_x(7, 1, 0, SHARE)
+        for m in (6, 7):
+            scale_y(m, 1, 0, SHARE)
+        for m in (6, 7):
+            add_x(m, 1, SHARE, SHARE)
+            scale_y(m, 1, SHARE, SHARE)
+        for m in range(4):
             row_product(m, 0)
-        for share in range(2):
-            new_e_words(1, 1, share, "e_words1%d" % share)
+        new_e_words(1, 1, 0, "e_words_a")
+        new_e_words(1, 1, 1, "e_words_b")
         interleave(nc.vector.tensor_copy, 1, 1, 0, SHARE)
+        row_product(4, 0)
         interleave(nc.vector.tensor_copy, 1, 1, SHARE, SHARE + P)
         interleave(nc.scalar.copy, 1, 1, SHARE + P, HALF)
         quantize_e(1, 1, (0, 1))
-        for g in range(2):
-            for m in range(2):
-                row_pass(m, 1, g)
-        for h in range(2):
-            for m in range(2):
-                add_y(m, h)
-        for m in range(2, 4):
-            row_product(m, 1)
 
-        turn_z(0)
-        turn_z(1)
-        add_y(2, 0)
-        group_z(0, parts=2)
-        add_y(2, 1)
-        group_z(1)
-        move_z(2)
-        quantize_z(0, parts=2)
-        row_product(4, 1)
+        spill_row(4)
+        add_y_on_pool(4)
+        add_y(0, 0)
+        move_z(0, 0)
+        row_product(0, 1)
+        row_product(1, 1)
+        add_y(0, 1)
+        move_z(0, 1)
         row_product(5, 0)
+        spill_row(5)
+        add_y_on_pool(5)
+        add_y(1, 0)
+        add_y(1, 1)
+        move_z(1)
+        row_product(2, 1)
+        row_product(6, 0)
+        turn_z(0, 0)
+        group_z(0, 0)
+        add_y(2, 0)
+        row_product(3, 1)
+        turn_z(0, 1)
+        group_z(0, 1)
+        add_y(2, 1)
+        move_z(2)
+        row_product(7, 0)
+        row_product(4, 1)
+        quantize_z(0, 0)
         add_y(3, 0)
+        quantize_z(0, 1)
+        spill_row(6)
+        add_y_on_pool(6)
+        row_product(5, 1)
+        turn_z(1)
+        group_z(1)
         add_y(3, 1)
         move_z(3)
-        quantize_z(1)
-        add_y(4, 0)
+        row_product(6, 1)
+        half_products(0, 0)
         add_y(4, 1)
         move_z(4)
-
-        for n in range(2):
-            half_products(0, n)
-            pool_product(0, n * HALF)
-        row_product(5, 1)
-        add_y(5, 0)
+        spill_row(7)
+        quantize_z(1)
+        add_y_on_pool(7)
+        turn_z(2)
+        half_products(0, 1)
+        spill_values(0, 0)
+        group_z(2)
         add_y(5, 1)
         move_z(5)
-        for n in range(2):
-            turn_z_blocks(2 + n)
-            for h in range(2):
-                row_product(6 + n, h)
-                add_y(6 + n, h)
-            move_z(6 + n)
-            store_pool_result(0, n * HALF)
-            group_z_blocks(2 + n)
-            half_products(1, n)
-            pool_product(1, n * HALF)
-            quantize_z(2 + n)
-        turn_z_blocks(4)
-        store_pool_result(1, 0)
-
+        row_product(7, 1)
+        add_y(6, 1)
+        move_z(6)
+        turn_z(3)
+        half_products(1, 0)
+        spill_values(0, HALF)
+        quantize_z(2)
+        pool_product(0, 0, "y20")
+        group_z(3)
+        add_y(7, 1)
+        move_z(7)
+        half_products(1, 1)
+        turn_z(4)
+        spill_values(1, 0)
+        quantize_z(3)
+        pool_product(0, HALF, "y30")
+        store_pool_result(0, 0)
         half_products(2, 0)
-        group_z_blocks(4)
-        turn_z_blocks(5)
-        store_pool_result(1, HALF)
-        quantize_z(4)
-        store_product(2, 0, HALF)
+        group_z(4)
+        store_product(1, HALF)
+        turn_z(5)
         half_products(2, 1)
-        group_z_blocks(5)
-        for m in range(3, TILES - 1):
-            half_products(m, 0)
-            store_product(m - 1, HALF, HALF)
-            if m + 2 < TILES:
-                quantize_z(m + 2)
-            if m + 3 < TILES:
-                turn_z_blocks(m + 3)
-            store_product(m, 0, HALF)
-            half_products(m, 1)
-            if m + 3 < TILES:
-                group_z_blocks(m + 3)
-        store_product(TILES - 2, HALF, HALF)
+        quantize_z(4)
+        pool_product(1, 0, "y40")
+        store_pool_result(0, HALF)
+        group_z(5)
+        store_product(2, 0)
+        half_products(3, 0)
+        turn_z(6)
+        spill_values(3, 0)
+        store_product(2, HALF)
+        quantize_z(5)
+        pool_product(3, 0, "y50")
+        store_pool_result(1, 0)
+        half_products(3, 1)
+        group_z(6)
+        turn_z(7)
+        half_products(4, 0)
+        store_product(3, HALF)
+        quantize_z(6)
+        store_pool_result(3, 0)
+        half_products(4, 1)
+        group_z(7)
+        store_product(4, 0)
+        half_products(5, 0)
+        store_product(4, HALF)
+        quantize_z(7)
+        for k in range(11, 14):
+            half_products(k // 2, k % 2)
+            store_product((k - 1) // 2, (k - 1) % 2 * HALF)
+        store_product(6, HALF)
 
         last = TILES - 1
         gate_product(last, 0, SHARE)

@@ -22,7 +22,8 @@ TILES = 8
 HALF = 512
 SHARE = 256
 UNSORTED_TILE = 2
-BY_HALVES = 1
+BY_HALVES = 0
+ON_TENSOR = 2
 
 
 def tile_codebook_patch_mixer_t2_kernel(
@@ -257,11 +258,12 @@ def tile_codebook_patch_mixer_t2_kernel(
             for r in range(4):
                 nc.sync.dma_start(out=row_s[:].bitcast(I32)[r:P:32], in_=dealt[8 * r : 8 * (r + 1)])
 
-        mixed, z_sb, z_moved, z_blocks, z_grouped = {}, {}, {}, {}, {}
+        mixed, z_sb, z_moved, z_blocks, z_turned, z_grouped = {}, {}, {}, {}, {}, {}
 
-        def row_product(m, h):
-            mixed[m, h] = take_bank("row%d%d" % (m, h), [P, HALF])
-            for g in range(2):
+        def row_product(m, h, passes=(0, 1)):
+            if (m, h) not in mixed:
+                mixed[m, h] = take_bank("row%d%d" % (m, h), [P, HALF])
+            for g in passes:
                 first = (4 * g + m % 4) * P
                 nc.tensor.matmul_mx(
                     out=mixed[m, h][:],
@@ -276,6 +278,8 @@ def tile_codebook_patch_mixer_t2_kernel(
         def z_target(m, h):
             if m not in z_sb:
                 z_sb[m] = kept("z%d" % m, [P, 2 * HALF], BF16, tag="codes_raw%d" % m)
+            if m < ON_TENSOR:
+                return z_sb[m][:].rearrange("p (h u d k) -> p h u d k", d=4, h=2, u=2)[:, h]
             if m < BY_HALVES:
                 return z_sb[m][:].rearrange("p (h d u k) -> p h u d k", d=4, h=2, u=2)[:, h]
             return z_sb[m][:].rearrange("p (d h u k) -> p h u d k", d=4, h=2, u=2)[:, h]
@@ -303,7 +307,7 @@ def tile_codebook_patch_mixer_t2_kernel(
         spilled = {}
 
         def spill_row(m):
-            spilled[m] = ringed("spilled%d" % m, [P, HALF], F32, "values", 4)
+            spilled[m] = ringed("spilled%d" % m, [P, HALF], F32, "values", 2)
             nc.scalar.copy(out=spilled[m][:], in_=mixed[m, 0][:])
             give_bank("row%d0" % m)
 
@@ -342,6 +346,24 @@ def tile_codebook_patch_mixer_t2_kernel(
                 words = z_grouped[m, h][:, k].bitcast(F32).rearrange("p (i a b) u -> p a i b u", a=2, b=2)
                 nc.scalar.copy(out=words, in_=blocks[:, k])
 
+        def turn_z_on_tensor(m):
+            z_turned[m] = take_bank("turn_z%d" % m, [P, 2, 2, P])
+            words = z_sb[m][:].bitcast(F32)
+            for h in range(2):
+                for u in range(2):
+                    run = slice((2 * h + u) * P, (2 * h + u + 1) * P)
+                    nc.tensor.transpose(z_turned[m][:, h, u, :], words[:, run], ident[:])
+
+        def group_turned_z(m, h=None):
+            first, count = span(h)
+            z_grouped[m, h] = kept("z_grouped%d_%d" % (m, first), [P, count, P, 4], BF16, tag="y%d%d" % (m, first))
+            nc.scalar.copy(
+                out=z_grouped[m, h][:].bitcast(F32),
+                in_=z_turned[m][:, first : first + count].rearrange("p h u n -> p h n u"),
+            )
+            if first + count == 2:
+                give_bank("turn_z%d" % m)
+
         def quantize_z(m, h=None):
             first, count = span(h)
             cols = slice(first * P, (first + count) * P)
@@ -368,12 +390,12 @@ def tile_codebook_patch_mixer_t2_kernel(
 
         def gate_product(m, c0, width):
             chan_product(m, 2 * HALF + c0, width)
-            gates[m, c0] = ringed("gate%d_%d" % (m, c0), [P, width], F32, "gate%d" % width, 6 if width == HALF else 4)
+            gates[m, c0] = ringed("gate%d_%d" % (m, c0), [P, width], F32, "gate%d" % width, 5 if width == HALF else 4)
             nc.scalar.activation(out=gates[m, c0][:], in_=h_sums[m, 2 * HALF + c0][:], func=ACT.Tanh)
             give_bank("chan%d_%d" % (m, 2 * HALF + c0))
 
         def new_result(m, c0, width):
-            return ringed("result%d_%d" % (m, c0), [P, width], F32, "result%d" % width, 5 if width == HALF else 4)
+            return ringed("result%d_%d" % (m, c0), [P, width], F32, "result%d" % width, 7 if width == HALF else 4)
 
         def store(m, c0, width, result):
             nc.sync.dma_start(out=out_v[m // 4, m % 4][:, c0 : c0 + width], in_=result[:])
@@ -387,13 +409,13 @@ def tile_codebook_patch_mixer_t2_kernel(
         pool_values, pool_results = {}, {}
 
         def spill_values(m, c0):
-            values = ringed("values%d_%d" % (m, c0), [P, HALF], F32, "values", 4)
+            values = ringed("values%d_%d" % (m, c0), [P, HALF], F32, "values", 2)
             nc.scalar.copy(out=values[:], in_=h_sums[m, c0][:])
             give_bank("chan%d_%d" % (m, c0))
             pool_values[m, c0] = values
 
         def pool_product(m, c0, room):
-            pool_results[m, c0] = kept("result%d_%d" % (m, c0), [P, HALF], F32, tag=room)
+            pool_results[m, c0] = kept("result%d_%d" % (m, c0), [P, HALF], F32, tag=room) if room else new_result(m, c0, HALF)
             nc.gpsimd.tensor_tensor(
                 out=pool_results[m, c0][:], in0=pool_values[m, c0][:], in1=gates[m, c0][:], op=MULT
             )
@@ -556,107 +578,75 @@ def tile_codebook_patch_mixer_t2_kernel(
         interleave(nc.vector.tensor_copy, 1, 1, SHARE, SHARE + P)
         interleave(nc.scalar.copy, 1, 1, SHARE + P, HALF)
         quantize_e(1, 1, (0, 1))
-
-        spill_row(4)
-        add_y_on_pool(4)
-        add_y(0, 0)
-        move_z(0, 0)
-        row_product(0, 1)
-        row_product(1, 1)
-        add_y(0, 1)
-        move_z(0, 1)
-        row_product(5, 0)
-        spill_row(5)
-        add_y_on_pool(5)
-        add_y(1, 0)
-        add_y(1, 1)
-        move_z(1)
-        row_product(2, 1)
-        row_product(6, 0)
-        turn_z(0, 0)
-        group_z(0, 0)
+        for g in range(2):
+            for m in range(2):
+                row_product(m, 1, (g,))
+        for h in range(2):
+            for m in range(2):
+                add_y(m, h)
+        for m in range(2, 4):
+            row_product(m, 1)
+        turn_z_on_tensor(0)
+        turn_z_on_tensor(1)
         add_y(2, 0)
-        row_product(3, 1)
-        turn_z(0, 1)
-        group_z(0, 1)
+        for h in range(2):
+            group_turned_z(0, h)
         add_y(2, 1)
+        group_turned_z(1)
         move_z(2)
-        row_product(7, 0)
+        for h in range(2):
+            quantize_z(0, h)
         row_product(4, 1)
-        quantize_z(0, 0)
+        row_product(5, 0)
         add_y(3, 0)
-        quantize_z(0, 1)
-        spill_row(6)
-        add_y_on_pool(6)
-        row_product(5, 1)
-        turn_z(1)
-        group_z(1)
         add_y(3, 1)
         move_z(3)
-        row_product(6, 1)
-        half_products(0, 0)
+        quantize_z(1)
+        add_y(4, 0)
         add_y(4, 1)
         move_z(4)
-        spill_row(7)
-        quantize_z(1)
-        add_y_on_pool(7)
-        turn_z(2)
-        half_products(0, 1)
-        spill_values(0, 0)
-        group_z(2)
+        for n in range(2):
+            half_products(0, n)
+            spill_values(0, n * HALF)
+            pool_product(0, n * HALF, None)
+        row_product(5, 1)
+        add_y(5, 0)
         add_y(5, 1)
         move_z(5)
-        row_product(7, 1)
-        add_y(6, 1)
-        move_z(6)
-        turn_z(3)
-        half_products(1, 0)
-        spill_values(0, HALF)
-        quantize_z(2)
-        pool_product(0, 0, "y20")
-        group_z(3)
-        add_y(7, 1)
-        move_z(7)
-        half_products(1, 1)
+        for n in range(2):
+            turn_z(2 + n)
+            for h in range(2):
+                row_product(6 + n, h)
+                add_y(6 + n, h)
+            move_z(6 + n)
+            store_pool_result(0, n * HALF)
+            group_z(2 + n)
+            half_products(1, n)
+            spill_values(1, n * HALF)
+            pool_product(1, n * HALF, None)
+            quantize_z(2 + n)
         turn_z(4)
-        spill_values(1, 0)
-        quantize_z(3)
-        pool_product(0, HALF, "y30")
-        store_pool_result(0, 0)
+        store_pool_result(1, 0)
         half_products(2, 0)
         group_z(4)
-        store_product(1, HALF)
         turn_z(5)
-        half_products(2, 1)
+        store_pool_result(1, HALF)
         quantize_z(4)
-        pool_product(1, 0, "y40")
-        store_pool_result(0, HALF)
-        group_z(5)
         store_product(2, 0)
-        half_products(3, 0)
-        turn_z(6)
-        spill_values(3, 0)
-        store_product(2, HALF)
-        quantize_z(5)
-        pool_product(3, 0, "y50")
-        store_pool_result(1, 0)
-        half_products(3, 1)
-        group_z(6)
-        turn_z(7)
-        half_products(4, 0)
-        store_product(3, HALF)
-        quantize_z(6)
-        store_pool_result(3, 0)
-        half_products(4, 1)
-        group_z(7)
-        store_product(4, 0)
-        half_products(5, 0)
-        store_product(4, HALF)
-        quantize_z(7)
-        for k in range(11, 14):
-            half_products(k // 2, k % 2)
-            store_product((k - 1) // 2, (k - 1) % 2 * HALF)
-        store_product(6, HALF)
+        half_products(2, 1)
+        group_z(5)
+        for m in range(3, TILES - 1):
+            half_products(m, 0)
+            store_product(m - 1, HALF)
+            if m + 2 < TILES:
+                quantize_z(m + 2)
+            if m + 3 < TILES:
+                turn_z(m + 3)
+            store_product(m, 0)
+            half_products(m, 1)
+            if m + 3 < TILES:
+                group_z(m + 3)
+        store_product(TILES - 2, HALF)
 
         last = TILES - 1
         gate_product(last, 0, SHARE)

@@ -24,6 +24,7 @@ SHARE = 256
 UNSORTED_TILE = 2
 BY_HALVES = 0
 ON_TENSOR = 2
+SORTED_PASSES = 3
 
 
 def tile_codebook_patch_mixer_t2_kernel(
@@ -115,8 +116,12 @@ def tile_codebook_patch_mixer_t2_kernel(
         def load_x(m, h):
             nc.sync.dma_start(out=x_sb[m, h][:], in_=x_v[m // 4, m % 4][:, h * HALF : (h + 1) * HALF])
 
-        def load_words(tile, words):
-            nc.sync.dma_start(out=tile[:].bitcast(I32), in_=words.bitcast(I32).rearrange("g p b -> p g b"))
+        def load_words(tile, words, parts=1):
+            source = words.bitcast(I32).rearrange("g p b -> p g b")
+            width = source.shape[1] // parts
+            for i in range(parts):
+                passes = slice(i * width, (i + 1) * width)
+                nc.sync.dma_start(out=tile[:].bitcast(I32)[:, passes], in_=source[:, passes])
 
         def load_scales(plane, scales):
             rows = plane[:].bitcast(I32)
@@ -141,22 +146,41 @@ def tile_codebook_patch_mixer_t2_kernel(
                     in_=raw.rearrange("p (g w u) -> p g u w", g=width, u=2),
                 )
 
-        def turn_codes(m):
+        def sort_half(m, b):
+            if b == 0:
+                sorted_words[m] = ringed("sorted%d" % m, [P, 4, 2, P], F32, "sorted", 3)
+            nc.vector.tensor_copy(
+                out=sorted_words[m][:, 2 * b : 2 * b + 2],
+                in_=codes_raw[m][:, b * 1024 : (b + 1) * 1024].bitcast(F32).rearrange("p (g w u) -> p g u w", g=2, u=2),
+            )
+
+        def sort_first_passes(m):
+            sorted_words[m] = ringed("sorted%d" % m, [P, 4, 2, P], F32, "sorted", 3)
+            raw = codes_raw[m][:, 0 : SORTED_PASSES * 512].bitcast(F32)
+            nc.vector.tensor_copy(
+                out=sorted_words[m][:, 0:SORTED_PASSES].rearrange("p g u w -> p u g w"),
+                in_=raw.rearrange("p (g w u) -> p u g w", g=SORTED_PASSES, u=2),
+            )
+
+        def turn_codes(m, banks=(0, 1)):
             words = codes_raw[m][:].bitcast(F32)
-            for b in range(2):
+            for b in banks:
                 turned[m, b] = take_bank("turn%d%d" % (m, b), [P, 2, 2, P])
                 for i in range(2):
                     g = 2 * b + i
                     for u in range(2):
-                        if m == UNSORTED_TILE:
+                        if m == UNSORTED_TILE or (UNSORTED_TILE < m < TILES - 1 and g >= SORTED_PASSES):
                             source = words[:, 256 * g + u : 256 * (g + 1) : 2]
                         else:
                             source = sorted_words[m][:, g, u, :]
                         nc.tensor.transpose(turned[m, b][:, i, u, :], source, ident[:])
 
-        def group_codes(m):
-            for b in range(2):
-                grouped[m, b] = ringed("grouped%d%d" % (m, b), [P, 2, P, 4], BF16, "grouped", 5)
+        def group_codes(m, banks=(0, 1)):
+            for b in banks:
+                if (m, b) == (TILES - 1, 1):
+                    grouped[m, b] = kept("grouped_last", [P, 2, P, 4], BF16, tag="pool_out")
+                else:
+                    grouped[m, b] = ringed("grouped%d%d" % (m, b), [P, 2, P, 4], BF16, "grouped", 5)
                 nc.scalar.copy(out=grouped[m, b][:].bitcast(F32), in_=turned[m, b][:].rearrange("p i u n -> p i n u"))
                 give_bank("turn%d%d" % (m, b))
 
@@ -169,9 +193,10 @@ def tile_codebook_patch_mixer_t2_kernel(
                     in_=grouped[m, b][:].rearrange("p g n t -> p (g n t)"),
                 )
 
-        def book_product(m, h, c0=0, width=HALF):
-            sums[m, h, c0] = take_bank("book%d%d%d" % (m, h, c0), [P, width])
-            for g in range(4):
+        def book_product(m, h, c0=0, width=HALF, passes=range(4)):
+            if (m, h, c0) not in sums:
+                sums[m, h, c0] = take_bank("book%d%d%d" % (m, h, c0), [P, width])
+            for g in passes:
                 nc.tensor.matmul_mx(
                     out=sums[m, h, c0][:],
                     lhsT=codes_q[m][:, g * P : (g + 1) * P].bitcast(FP8X4),
@@ -426,17 +451,15 @@ def tile_codebook_patch_mixer_t2_kernel(
         def half_products(m, n):
             gate_product(m, n * HALF, HALF)
             chan_product(m, n * HALF, HALF)
-
         load_codes(0, parts=2)
         load_codes(1)
         load_scales(book_s[0], book_scales[:, :, scale_cols(0)])
         load_words(book_w[0], book_words[:, :, word_cols(0)])
-        for m in (2, 3, 4):
+        for m in range(2, TILES):
             load_codes(m)
-        load_x(0, 0)
-        nc.sync.dma_start(out=gain_raw[:], in_=patch_gain.rearrange("(g p t) -> p g t", p=P, t=4))
-        load_x(1, 0)
-        load_x(2, 0)
+            load_x(m - 2, 0)
+            if m == 2:
+                nc.sync.dma_start(out=gain_raw[:], in_=patch_gain.rearrange("(g p t) -> p g t", p=P, t=4))
 
         warm_up("warm0", 3)
         sort_codes(0, parts=2)
@@ -446,138 +469,111 @@ def tile_codebook_patch_mixer_t2_kernel(
         sort_codes(1)
         quantize_codes(0)
         clear(row_s)
+        clear(chan_s)
         turn_codes(1)
         group_codes(1)
         warm_up("warm2", 1)
 
-        load_codes(5)
-        load_x(3, 0)
+        load_row_scales()
         load_words(book_w[1], book_words[:, :, word_cols(1)])
         load_scales(book_s[1], book_scales[:, :, scale_cols(1)])
-        load_codes(6)
-        load_x(4, 0)
+        load_x(6, 0)
         load_x(0, 1)
-        load_codes(7)
-        load_x(1, 1)
-        load_x(2, 1)
-        load_row_scales()
-        load_x(3, 1)
         load_words(row_w_raw[0], row_words[:, :, word_cols(0)])
-        for m in (5, 6, 7):
-            load_x(m, 0)
+        load_x(7, 0)
+        load_x(1, 1)
         load_words(row_w_raw[1], row_words[:, :, word_cols(1)])
-        for m in range(4, TILES):
+        for m in range(2, TILES):
             load_x(m, 1)
 
         quantize_codes(1)
-        clear(chan_s)
+
         book_product(0, 0)
         turn_codes(2)
         group_codes(2)
-        book_product(1, 0)
-        sort_codes(3)
-        quantize_codes(2, (0,))
-        turn_codes(3)
-        sort_codes(4)
-        quantize_codes(2, (1,))
-        turn_codes(4)
-        group_codes(3)
         add_x(0, 0)
         nc.vector.tensor_copy(out=gain[:], in_=gain_raw[:].rearrange("p g t -> p (g t)"))
-        book_product(2, 0)
-        add_x(1, 0)
-        quantize_codes(3)
-        group_codes(4)
         scale_y(0, 0)
-        scale_y(1, 0)
-        book_product(3, 0)
-        sort_codes(5)
-        quantize_codes(4)
-        add_x(2, 0)
-        scale_y(2, 0)
-        book_product(4, 0)
-        add_x(3, 0)
-        scale_y(3, 0)
-        new_e_words(0, 0, 1, "e_words_b")
-        interleave(nc.scalar.copy, 0, 0, SHARE, HALF)
-        book_product(0, 1)
-        sort_codes(6)
-        turn_codes(5)
-        turn_codes(6)
-        group_codes(5)
-        add_x(4, 0)
-        add_x(0, 1)
-        book_product(1, 1)
-        sort_codes(7)
-        group_codes(6)
-        quantize_codes(5)
-        new_e_words(0, 0, 0, "e_words_a")
-        interleave(nc.vector.tensor_copy, 0, 0, 0, SHARE)
-        book_product(2, 1)
-        add_x(1, 1)
-        turn_codes(7)
-        scale_y(4, 0)
-        scale_y(0, 1)
-        quantize_codes(6)
-        add_x(2, 1)
-        group_codes(7)
-        book_product(3, 1)
-        deal_row_scales()
+        book_product(1, 0)
+        sort_first_passes(3)
+        quantize_codes(2)
+        for m in range(2, TILES - 1):
+            turn_codes(m + 1)
+            group_codes(m + 1)
+            add_x(m - 1, 0)
+            scale_y(m - 1, 0)
+            book_product(m, 0)
+            if m + 2 < TILES - 1:
+                sort_first_passes(m + 2)
+            elif m + 2 == TILES - 1:
+                sort_codes(m + 2)
+            else:
+                deal_row_scales()
+            quantize_codes(m + 1)
         place_row_scales()
         for h in range(2):
             nc.sync.dma_start(out=chan_w[h][:].bitcast(I32), in_=chan_words[h].bitcast(I32))
         load_scales(chan_s, chan_scales)
-        quantize_e(0, 0, (0, 1))
-        book_product(5, 0)
-        add_x(3, 1)
-        for m in range(1, 4):
-            scale_y(m, 1)
-        quantize_codes(7)
-        deal_row_words(0)
-        book_product(6, 0)
-        add_x(5, 0)
-        new_e_words(0, 1, 0, "e_words_a")
-        interleave_on_pool(0, 1, 0)
-        new_e_words(0, 1, 1, "e_words_b")
-        interleave(nc.scalar.copy, 0, 1, SHARE, HALF)
-        book_product(7, 0)
+
+        book_product(0, 1)
         add_x(6, 0)
-        book_product(4, 1)
+        new_e_words(0, 0, 0, "pool_out")
+        interleave_on_pool(0, 0, 0)
+        new_e_words(0, 0, 1, "e_words01")
+        interleave(nc.scalar.copy, 0, 0, SHARE, HALF)
+        scale_y(6, 0)
+        book_product(7, 0)
+        add_x(0, 1)
+        scale_y(0, 1)
+        book_product(1, 1)
         add_x(7, 0)
-        for m in range(5, TILES):
-            scale_y(m, 0)
-        quantize_e(0, 1, (0, 1))
-        deal_row_words(1)
-        new_e_words(1, 0, 0, "e_words_a")
+        scale_y(7, 0)
+        deal_row_words(0)
+        quantize_e(0, 0, (1, 0))
+        book_product(2, 1)
+        add_x(1, 1)
+        new_e_words(1, 0, 0, "pool_out")
         interleave_on_pool(1, 0, 0)
+        new_e_words(1, 0, 1, "e_words11")
+        interleave(nc.scalar.copy, 1, 0, SHARE, HALF)
+        scale_y(1, 1)
+        for m in (3, 4):
+            book_product(m, 1)
+            add_x(m - 1, 1)
+            scale_y(m - 1, 1)
+        deal_row_words(1)
+        quantize_e(1, 0, (1, 0))
         book_product(5, 1)
         add_x(4, 1)
-        new_e_words(1, 0, 1, "e_words_b")
-        interleave(nc.scalar.copy, 1, 0, SHARE, HALF)
-        book_product(6, 1, 0, SHARE)
-        add_x(5, 1)
+        new_e_words(0, 1, 0, "pool_out")
+        interleave_on_pool(0, 1, 0)
+        new_e_words(0, 1, 1, "e_words01")
+        interleave(nc.scalar.copy, 0, 1, SHARE, HALF)
         scale_y(4, 1)
+        book_product(6, 1)
+        add_x(5, 1)
         scale_y(5, 1)
-        book_product(7, 1, 0, SHARE)
-        add_x(6, 1, 0, SHARE)
-        quantize_e(1, 0, (0, 1))
-        book_product(6, 1, SHARE, SHARE)
-        book_product(7, 1, SHARE, SHARE)
-        add_x(7, 1, 0, SHARE)
-        for m in (6, 7):
-            scale_y(m, 1, 0, SHARE)
-        for m in (6, 7):
-            add_x(m, 1, SHARE, SHARE)
-            scale_y(m, 1, SHARE, SHARE)
-        for m in range(4):
+
+        for c0 in (0, SHARE):
+            book_product(7, 1, c0, SHARE)
+        add_x(6, 1)
+        scale_y(6, 1)
+        for c0 in (0, SHARE):
+            add_x(7, 1, c0, SHARE)
+        quantize_e(0, 1, (1, 0))
+        for c0 in (0, SHARE):
+            scale_y(7, 1, c0, SHARE)
+
+        for m in range(5):
             row_product(m, 0)
-        new_e_words(1, 1, 0, "e_words_a")
-        new_e_words(1, 1, 1, "e_words_b")
+        for share in range(2):
+            new_e_words(1, 1, share, "e_words1%d" % share)
         interleave(nc.vector.tensor_copy, 1, 1, 0, SHARE)
-        row_product(4, 0)
         interleave(nc.vector.tensor_copy, 1, 1, SHARE, SHARE + P)
         interleave(nc.scalar.copy, 1, 1, SHARE + P, HALF)
         quantize_e(1, 1, (0, 1))
+        spill_row(4)
+        add_y_on_pool(4)
         for g in range(2):
             for m in range(2):
                 row_product(m, 1, (g,))
@@ -602,51 +598,73 @@ def tile_codebook_patch_mixer_t2_kernel(
         add_y(3, 1)
         move_z(3)
         quantize_z(1)
-        add_y(4, 0)
         add_y(4, 1)
         move_z(4)
-        for n in range(2):
-            half_products(0, n)
-            spill_values(0, n * HALF)
-            pool_product(0, n * HALF, None)
+        half_products(0, 0)
+        spill_values(0, 0)
+        pool_product(0, 0, None)
         row_product(5, 1)
         add_y(5, 0)
         add_y(5, 1)
         move_z(5)
-        for n in range(2):
-            turn_z(2 + n)
-            for h in range(2):
-                row_product(6 + n, h)
-                add_y(6 + n, h)
-            move_z(6 + n)
-            store_pool_result(0, n * HALF)
-            group_z(2 + n)
-            half_products(1, n)
-            spill_values(1, n * HALF)
-            pool_product(1, n * HALF, None)
-            quantize_z(2 + n)
+        half_products(0, 1)
+        spill_values(0, HALF)
+        turn_z(2)
+        pool_product(0, HALF, None)
+        row_product(6, 0)
+        row_product(6, 1)
+        group_z(2)
+        add_y(6, 0)
+        add_y(6, 1)
+        move_z(6)
+        store_pool_result(0, 0)
+        half_products(1, 0)
+        turn_z(3)
+        quantize_z(2)
+        spill_values(1, 0)
+        pool_product(1, 0, "y20")
+        row_product(7, 0)
+        row_product(7, 1)
+        group_z(3)
+        add_y(7, 0)
+        add_y(7, 1)
+        move_z(7)
+        store_pool_result(0, HALF)
+        half_products(1, 1)
         turn_z(4)
-        store_pool_result(1, 0)
+        quantize_z(3)
+        spill_values(1, HALF)
+        pool_product(1, HALF, "y30")
         half_products(2, 0)
         group_z(4)
         turn_z(5)
-        store_pool_result(1, HALF)
-        quantize_z(4)
-        store_product(2, 0)
+        store_pool_result(1, 0)
         half_products(2, 1)
+        store_product(2, 0)
+        quantize_z(4)
         group_z(5)
-        for m in range(3, TILES - 1):
-            half_products(m, 0)
-            store_product(m - 1, HALF)
-            if m + 2 < TILES:
-                quantize_z(m + 2)
-            if m + 3 < TILES:
-                turn_z(m + 3)
-            store_product(m, 0)
-            half_products(m, 1)
-            if m + 3 < TILES:
-                group_z(m + 3)
-        store_product(TILES - 2, HALF)
+        turn_z(6)
+        store_pool_result(1, HALF)
+        half_products(3, 0)
+        store_product(2, HALF)
+        quantize_z(5)
+        half_products(3, 1)
+        group_z(6)
+        store_product(3, 0)
+        turn_z(7)
+        half_products(4, 0)
+        store_product(3, HALF)
+        quantize_z(6)
+        half_products(4, 1)
+        group_z(7)
+        store_product(4, 0)
+        half_products(5, 0)
+        store_product(4, HALF)
+        quantize_z(7)
+        for k in range(11, 14):
+            half_products(k // 2, k % 2)
+            store_product((k - 1) // 2, (k - 1) % 2 * HALF)
+        store_product(6, HALF)
 
         last = TILES - 1
         gate_product(last, 0, SHARE)

@@ -142,8 +142,8 @@ def tile_codebook_patch_mixer_t2_kernel(
             for i in range(parts):
                 raw = codes_raw[m][:, i * width * 512 : (i + 1) * width * 512].bitcast(F32)
                 nc.vector.tensor_copy(
-                    out=sorted_words[m][:, i * width : (i + 1) * width],
-                    in_=raw.rearrange("p (g w u) -> p g u w", g=width, u=2),
+                    out=sorted_words[m][:, i * width : (i + 1) * width].rearrange("p g u (c w) -> p g c u w", w=4),
+                    in_=raw.rearrange("p (g c w u) -> p g c u w", g=width, w=4, u=2),
                 )
 
         def sort_half(m, b):
@@ -158,8 +158,8 @@ def tile_codebook_patch_mixer_t2_kernel(
             sorted_words[m] = ringed("sorted%d" % m, [P, 4, 2, P], F32, "sorted", 3)
             raw = codes_raw[m][:, 0 : SORTED_PASSES * 512].bitcast(F32)
             nc.vector.tensor_copy(
-                out=sorted_words[m][:, 0:SORTED_PASSES].rearrange("p g u w -> p u g w"),
-                in_=raw.rearrange("p (g w u) -> p u g w", g=SORTED_PASSES, u=2),
+                out=sorted_words[m][:, 0:SORTED_PASSES].rearrange("p g u (c w) -> p c g u w", w=4),
+                in_=raw.rearrange("p (g c w u) -> p c g u w", g=SORTED_PASSES, w=4, u=2),
             )
 
         def turn_codes(m, banks=(0, 1)):

@@ -231,6 +231,16 @@ def tile_codebook_patch_mixer_t2_kernel(
                 out=e_rows[g, h][:, t, cols], in_=y_sb[m, h][:, cols], func=ACT.Copy, scale=gain[:, m : m + 1]
             )
 
+        def scale_y_on_vector(m, h, c0, width):
+            cols = slice(c0, c0 + width)
+            nc.vector.tensor_scalar(
+                out=e_rows[m // 4, h][:, m % 4, cols],
+                in0=y_sb[m, h][:, cols],
+                scalar1=gain[:, m : m + 1],
+                scalar2=None,
+                op0=MULT,
+            )
+
         def new_e_words(g, h, share, tag):
             e_words[g, h, share] = kept("e_words%d%d%d" % (g, h, share), [P, SHARE, 4], BF16, tag=tag)
 
@@ -241,10 +251,10 @@ def tile_codebook_patch_mixer_t2_kernel(
                 in_=e_rows[g, h][:, :, c0:c1].rearrange("p t (c i) -> p c t i", i=4),
             )
 
-        def interleave_on_pool(g, h, share):
+        def interleave_on_pool(g, h, share, width=SHARE):
             nc.gpsimd.tensor_scalar(
-                out=e_words[g, h, share][:],
-                in0=e_rows[g, h][:, :, share * SHARE : (share + 1) * SHARE].rearrange("p t c -> p c t"),
+                out=e_words[g, h, share][:, 0:width],
+                in0=e_rows[g, h][:, :, share * SHARE : share * SHARE + width].rearrange("p t c -> p c t"),
                 scalar1=1.0,
                 scalar2=1.0,
                 op0=MULT,
@@ -548,7 +558,8 @@ def tile_codebook_patch_mixer_t2_kernel(
         new_e_words(0, 1, 0, "pool_out")
         interleave_on_pool(0, 1, 0)
         new_e_words(0, 1, 1, "e_words01")
-        interleave(nc.scalar.copy, 0, 1, SHARE, HALF)
+        interleave_on_pool(0, 1, 1, P)
+        interleave(nc.scalar.copy, 0, 1, SHARE + P, HALF)
         scale_y(4, 1)
         book_product(6, 1)
         add_x(5, 1)
@@ -560,7 +571,7 @@ def tile_codebook_patch_mixer_t2_kernel(
         scale_y(6, 1)
         for c0 in (0, SHARE):
             add_x(7, 1, c0, SHARE)
-        quantize_e(0, 1, (1, 0))
+        quantize_e(0, 1, (0, 1))
         for c0 in (0, SHARE):
             scale_y(7, 1, c0, SHARE)
 

@@ -284,8 +284,8 @@ def tile_codebook_patch_mixer_t2_kernel(
 
         def deal_row_scales():
             nc.vector.tensor_copy(
-                out=row_s_dealt[:].rearrange("p (a t n) -> p a t n", a=2, t=4),
-                in_=row_s_raw[:].rearrange("p (a n t) -> p a t n", a=2, t=4),
+                out=row_s_dealt[:].rearrange("p (a t c n) -> p a c t n", a=2, t=4, n=16),
+                in_=row_s_raw[:].rearrange("p (a c n t) -> p a c t n", a=2, t=4, n=16),
             )
 
         def place_row_scales():
@@ -410,9 +410,10 @@ def tile_codebook_patch_mixer_t2_kernel(
 
         h_sums, gates = {}, {}
 
-        def chan_product(m, c0, width):
-            h_sums[m, c0] = take_bank("chan%d_%d" % (m, c0), [P, width])
-            for h in range(2):
+        def chan_product(m, c0, width, passes=(0, 1)):
+            if (m, c0) not in h_sums:
+                h_sums[m, c0] = take_bank("chan%d_%d" % (m, c0), [P, width])
+            for h in passes:
                 nc.tensor.matmul_mx(
                     out=h_sums[m, c0][:],
                     lhsT=z_q[m][:, h * P : (h + 1) * P].bitcast(FP8X4),
@@ -423,8 +424,8 @@ def tile_codebook_patch_mixer_t2_kernel(
                     stop=(h == 1),
                 )
 
-        def gate_product(m, c0, width):
-            chan_product(m, 2 * HALF + c0, width)
+        def gate_product(m, c0, width, passes=(0, 1)):
+            chan_product(m, 2 * HALF + c0, width, passes)
             gates[m, c0] = ringed("gate%d_%d" % (m, c0), [P, width], F32, "gate%d" % width, 5 if width == HALF else 4)
             nc.scalar.activation(out=gates[m, c0][:], in_=h_sums[m, 2 * HALF + c0][:], func=ACT.Tanh)
             give_bank("chan%d_%d" % (m, 2 * HALF + c0))
@@ -459,8 +460,10 @@ def tile_codebook_patch_mixer_t2_kernel(
             store(m, c0, HALF, pool_results[m, c0])
 
         def half_products(m, n):
-            gate_product(m, n * HALF, HALF)
-            chan_product(m, n * HALF, HALF)
+            for c0 in (2 * HALF + n * HALF, n * HALF):
+                chan_product(m, c0, HALF, (0,))
+            gate_product(m, n * HALF, HALF, (1,))
+            chan_product(m, n * HALF, HALF, (1,))
         load_codes(0, parts=2)
         load_codes(1)
         load_scales(book_s[0], book_scales[:, :, scale_cols(0)])
@@ -510,8 +513,6 @@ def tile_codebook_patch_mixer_t2_kernel(
         for m in range(2, TILES - 1):
             turn_codes(m + 1)
             group_codes(m + 1)
-            add_x(m - 1, 0)
-            scale_y(m - 1, 0)
             book_product(m, 0)
             if m + 2 < TILES - 1:
                 sort_first_passes(m + 2)
@@ -519,6 +520,8 @@ def tile_codebook_patch_mixer_t2_kernel(
                 sort_codes(m + 2)
             else:
                 deal_row_scales()
+            add_x(m - 1, 0)
+            scale_y(m - 1, 0)
             quantize_codes(m + 1)
         place_row_scales()
         for h in range(2):
@@ -622,8 +625,9 @@ def tile_codebook_patch_mixer_t2_kernel(
         spill_values(0, HALF)
         turn_z(2)
         pool_product(0, HALF, None)
-        row_product(6, 0)
-        row_product(6, 1)
+        for g in range(2):
+            for h in range(2):
+                row_product(6, h, (g,))
         group_z(2)
         add_y(6, 0)
         add_y(6, 1)
@@ -634,8 +638,9 @@ def tile_codebook_patch_mixer_t2_kernel(
         quantize_z(2)
         spill_values(1, 0)
         pool_product(1, 0, "y20")
-        row_product(7, 0)
-        row_product(7, 1)
+        for g in range(2):
+            for h in range(2):
+                row_product(7, h, (g,))
         group_z(3)
         add_y(7, 0)
         add_y(7, 1)
@@ -672,15 +677,15 @@ def tile_codebook_patch_mixer_t2_kernel(
         half_products(5, 0)
         store_product(4, HALF)
         quantize_z(7)
-        for k in range(11, 14):
-            half_products(k // 2, k % 2)
-            store_product((k - 1) // 2, (k - 1) % 2 * HALF)
-        store_product(6, HALF)
-
-        last = TILES - 1
-        gate_product(last, 0, SHARE)
-        for c0 in range(0, 2 * HALF, SHARE):
-            if c0 + SHARE < 2 * HALF:
-                gate_product(last, c0 + SHARE, SHARE)
-            chan_product(last, c0, SHARE)
-            store_product(last, c0, SHARE)
+        half_products(5, 1)
+        store_product(5, 0)
+        pending = (5, HALF, HALF)
+        pieces = [(6, 0, HALF), (6, HALF, HALF)] + [(TILES - 1, c0, SHARE) for c0 in range(0, 2 * HALF, SHARE)]
+        gate_product(*pieces[0])
+        for i, piece in enumerate(pieces):
+            if i + 1 < len(pieces):
+                gate_product(*pieces[i + 1])
+            chan_product(*piece)
+            if i == 0:
+                store_product(*pending)
+            store_product(*piece)

@@ -128,6 +128,10 @@ def tile_codebook_patch_mixer_t2_kernel(
             for r in range(4):
                 nc.sync.dma_start(out=rows[r:P:32], in_=scales.rearrange("g (q r) n -> r q g n", r=4)[r].bitcast(I32))
 
+        def load_book_passes(h, first, count):
+            source = book_words[first : first + count, :, word_cols(h)].bitcast(I32).rearrange("g p b -> p g b")
+            nc.sync.dma_start(out=book_w[h][:, first : first + count].bitcast(I32), in_=source)
+
         def word_cols(h):
             return slice(h * 2 * HALF, (h + 1) * 2 * HALF)
 
@@ -150,8 +154,8 @@ def tile_codebook_patch_mixer_t2_kernel(
             if b == 0:
                 sorted_words[m] = ringed("sorted%d" % m, [P, 4, 2, P], F32, "sorted", 3)
             nc.vector.tensor_copy(
-                out=sorted_words[m][:, 2 * b : 2 * b + 2],
-                in_=codes_raw[m][:, b * 1024 : (b + 1) * 1024].bitcast(F32).rearrange("p (g w u) -> p g u w", g=2, u=2),
+                out=sorted_words[m][:, 2 * b : 2 * b + 2].rearrange("p g u (c w) -> p g c u w", w=4),
+                in_=codes_raw[m][:, b * 1024 : (b + 1) * 1024].bitcast(F32).rearrange("p (g c w u) -> p g c u w", g=2, w=4, u=2),
             )
 
         def sort_first_passes(m):
@@ -467,12 +471,16 @@ def tile_codebook_patch_mixer_t2_kernel(
         load_codes(0, parts=2)
         load_codes(1)
         load_scales(book_s[0], book_scales[:, :, scale_cols(0)])
-        load_words(book_w[0], book_words[:, :, word_cols(0)])
-        for m in range(2, TILES):
+        load_book_passes(0, 0, 2)
+        load_codes(2)
+        load_book_passes(0, 2, 2)
+        load_codes(3)
+        load_x(0, 0)
+        nc.sync.dma_start(out=gain_raw[:], in_=patch_gain.rearrange("(g p t) -> p g t", p=P, t=4))
+        load_x(1, 0)
+        for m in range(4, TILES):
             load_codes(m)
             load_x(m - 2, 0)
-            if m == 2:
-                nc.sync.dma_start(out=gain_raw[:], in_=patch_gain.rearrange("(g p t) -> p g t", p=P, t=4))
 
         warm_up("warm0", 3)
         sort_codes(0, parts=2)
@@ -481,11 +489,12 @@ def tile_codebook_patch_mixer_t2_kernel(
         warm_up("warm1", 2)
         sort_codes(1)
         quantize_codes(0)
-        clear(row_s)
-        clear(chan_s)
         turn_codes(1)
         group_codes(1)
         warm_up("warm2", 1)
+        clear(row_s)
+        clear(chan_s)
+        quantize_codes(1)
 
         load_row_scales()
         load_words(book_w[1], book_words[:, :, word_cols(1)])
@@ -499,20 +508,21 @@ def tile_codebook_patch_mixer_t2_kernel(
         for m in range(2, TILES):
             load_x(m, 1)
 
-        quantize_codes(1)
 
-        book_product(0, 0)
+        book_product(0, 0, passes=(0, 1))
         turn_codes(2)
         group_codes(2)
-        add_x(0, 0)
-        nc.vector.tensor_copy(out=gain[:], in_=gain_raw[:].rearrange("p g t -> p (g t)"))
-        scale_y(0, 0)
+        book_product(0, 0, passes=(2, 3))
         book_product(1, 0)
         sort_first_passes(3)
         quantize_codes(2)
+        add_x(0, 0)
+        nc.vector.tensor_copy(out=gain[:], in_=gain_raw[:].rearrange("p g t -> p (g t)"))
         for m in range(2, TILES - 1):
             turn_codes(m + 1)
             group_codes(m + 1)
+            if m == 2:
+                scale_y(0, 0)
             book_product(m, 0)
             if m + 2 < TILES - 1:
                 sort_first_passes(m + 2)

@@ -21,10 +21,9 @@ P = 128
 TILES = 8
 HALF = 512
 SHARE = 256
-UNSORTED_TILE = 2
-BY_HALVES = 0
 ON_TENSOR = 2
 SORTED_PASSES = 3
+ALL_SORTED = 4
 
 
 def tile_codebook_patch_mixer_t2_kernel(
@@ -61,13 +60,13 @@ def tile_codebook_patch_mixer_t2_kernel(
         codes_s = [kept("codes_s%d" % m, [P, 4 * P], U8) for m in range(TILES)]
         book_w = [kept("book_w%d" % h, [P, 4, 2 * HALF], U8) for h in range(2)]
         book_s = [kept("book_s%d" % h, [P, 4, HALF], U8) for h in range(2)]
-        x_sb = {(m, h): kept("x%d%d" % (m, h), [P, HALF], BF16) for m, h in halves}
+        x_sb = {(k, h): kept("x%d%d" % (k, h), [P, 2, HALF], BF16) for k in range(TILES // 2) for h in range(2)}
         y_sb = {(m, h): kept("y%d%d" % (m, h), [P, HALF], F32) for m, h in halves}
         e_q = {(g, h): kept("e_q%d%d" % (g, h), [P, HALF], U32) for g, h in groups}
         e_s = {(g, h): kept("e_s%d%d" % (g, h), [P, HALF], U8) for g, h in groups}
         row_w_raw = [kept("row_w_raw%d" % g, [P, 2, 2 * HALF], U8) for g in range(2)]
-        row_s_raw = kept("row_s_raw", [P, 2 * HALF], U8)
-        row_s_dealt = kept("row_s_dealt", [P, 2 * HALF], U8)
+        row_s_raw = kept("row_s_raw", [P, HALF], U8)
+        row_s_dealt = kept("row_s_dealt", [P, HALF], U8)
         row_s = kept("row_s", [P, 2, 2 * HALF], U8)
         row_w = [kept("row_w%d" % (4 * g), [P, 4 * HALF], U8) for g in range(2)]
         chan_w = [kept("chan_w%d" % h, [P, 4096], U8) for h in range(2)]
@@ -78,16 +77,8 @@ def tile_codebook_patch_mixer_t2_kernel(
         gain_raw = kept("gain_raw", [P, 2, 4], BF16)
         gain = kept("gain", [P, TILES], F32)
 
-        def clear(plane):
-            nc.vector.memset(plane[:].rearrange("p g n -> p (g n)").bitcast(I32), 0)
-
-        clear(book_s[0])
-        make_identity(nc, ident[:])
-        clear(book_s[1])
-        nc.vector.memset(codes_q[TILES - 1][:, 0:P], 0)
-        nc.vector.memset(codes_s[TILES - 1][:, 0:P].bitcast(I32), 0)
-        nc.vector.memset(book_w[1][:, 0, :].bitcast(I32), 0)
-        nc.vector.memset(row_s_raw[:].bitcast(I32), 0)
+        def clear(room):
+            nc.vector.memset(room.bitcast(I32), 0)
 
         def warm_up(name, passes):
             acc = take_bank(name, [P, HALF])
@@ -104,66 +95,50 @@ def tile_codebook_patch_mixer_t2_kernel(
             give_bank(name)
 
         codes_v = codes.rearrange("(g p t) j -> g t p j", p=P, t=4)
-        x_v = x.rearrange("(g p t) c -> g t p c", p=P, t=4)
+        x_v = x.rearrange("(g p t) c -> g p t c", p=P, t=4)
         out_v = out.rearrange("(g p t) c -> g t p c", p=P, t=4)
 
-        def load_codes(m, parts=1):
-            width = 2048 // parts
-            for i in range(parts):
-                cols = slice(i * width, (i + 1) * width)
-                nc.sync.dma_start(out=codes_raw[m][:, cols], in_=codes_v[m // 4, m % 4][:, cols])
+        def word_cols(h):
+            return slice(h * 2 * HALF, (h + 1) * 2 * HALF)
 
-        def load_x(m, h):
-            nc.sync.dma_start(out=x_sb[m, h][:], in_=x_v[m // 4, m % 4][:, h * HALF : (h + 1) * HALF])
+        def half_cols(h):
+            return slice(h * HALF, (h + 1) * HALF)
 
-        def load_words(tile, words, parts=1):
-            source = words.bitcast(I32).rearrange("g p b -> p g b")
-            width = source.shape[1] // parts
-            for i in range(parts):
-                passes = slice(i * width, (i + 1) * width)
-                nc.sync.dma_start(out=tile[:].bitcast(I32)[:, passes], in_=source[:, passes])
+        def load_codes(m, first=0, count=4):
+            cols = slice(first * 512, (first + count) * 512)
+            nc.sync.dma_start(out=codes_raw[m][:, cols], in_=codes_v[m // 4, m % 4][:, cols])
+
+        def load_x(m, h, count=2):
+            room = x_sb[m // 2, h][:, m % 2 : m % 2 + count]
+            nc.sync.dma_start(out=room, in_=x_v[m // 4][:, m % 4 : m % 4 + count, half_cols(h)])
+
+        def load_gain():
+            nc.sync.dma_start(out=gain_raw[:], in_=patch_gain.rearrange("(g p t) -> p g t", p=P, t=4))
 
         def load_scales(plane, scales):
             rows = plane[:].bitcast(I32)
             for r in range(4):
                 nc.sync.dma_start(out=rows[r:P:32], in_=scales.rearrange("g (q r) n -> r q g n", r=4)[r].bitcast(I32))
 
-        def load_book_passes(h, first, count):
+        def load_book(h, first, count):
             source = book_words[first : first + count, :, word_cols(h)].bitcast(I32).rearrange("g p b -> p g b")
             nc.sync.dma_start(out=book_w[h][:, first : first + count].bitcast(I32), in_=source)
 
-        def word_cols(h):
-            return slice(h * 2 * HALF, (h + 1) * 2 * HALF)
+        def load_row_words(group):
+            source = row_words[:, :, word_cols(group)].bitcast(I32).rearrange("g p b -> p g b")
+            nc.sync.dma_start(out=row_w_raw[group][:].bitcast(I32), in_=source)
 
-        def scale_cols(h):
-            return slice(h * HALF, (h + 1) * HALF)
+        sorted_words, sorted_count, turned, grouped, sums = {}, {}, {}, {}, {}
 
-        sorted_words, turned, grouped, sums = {}, {}, {}, {}
-
-        def sort_codes(m, parts=1):
-            sorted_words[m] = ringed("sorted%d" % m, [P, 4, 2, P], F32, "sorted", 3)
-            width = 4 // parts
-            for i in range(parts):
-                raw = codes_raw[m][:, i * width * 512 : (i + 1) * width * 512].bitcast(F32)
-                nc.vector.tensor_copy(
-                    out=sorted_words[m][:, i * width : (i + 1) * width].rearrange("p g u (c w) -> p g c u w", w=4),
-                    in_=raw.rearrange("p (g c w u) -> p g c u w", g=width, w=4, u=2),
-                )
-
-        def sort_half(m, b):
-            if b == 0:
+        def sort_codes(m, first=0, count=4):
+            if first == 0:
                 sorted_words[m] = ringed("sorted%d" % m, [P, 4, 2, P], F32, "sorted", 3)
+            sorted_count[m] = first + count
+            walk = "p g c u w" if count % 2 == 0 else "p c g u w"
+            raw = codes_raw[m][:, first * 512 : (first + count) * 512].bitcast(F32)
             nc.vector.tensor_copy(
-                out=sorted_words[m][:, 2 * b : 2 * b + 2].rearrange("p g u (c w) -> p g c u w", w=4),
-                in_=codes_raw[m][:, b * 1024 : (b + 1) * 1024].bitcast(F32).rearrange("p (g c w u) -> p g c u w", g=2, w=4, u=2),
-            )
-
-        def sort_first_passes(m):
-            sorted_words[m] = ringed("sorted%d" % m, [P, 4, 2, P], F32, "sorted", 3)
-            raw = codes_raw[m][:, 0 : SORTED_PASSES * 512].bitcast(F32)
-            nc.vector.tensor_copy(
-                out=sorted_words[m][:, 0:SORTED_PASSES].rearrange("p g u (c w) -> p c g u w", w=4),
-                in_=raw.rearrange("p (g c w u) -> p c g u w", g=SORTED_PASSES, w=4, u=2),
+                out=sorted_words[m][:, first : first + count].rearrange("p g u (c w) -> " + walk, w=4),
+                in_=raw.rearrange("p (g c w u) -> " + walk, g=count, w=4, u=2),
             )
 
         def turn_codes(m, banks=(0, 1)):
@@ -173,14 +148,11 @@ def tile_codebook_patch_mixer_t2_kernel(
                 for i in range(2):
                     g = 2 * b + i
                     for u in range(2):
-                        if m == UNSORTED_TILE or (UNSORTED_TILE < m < TILES - 1 and g >= SORTED_PASSES):
-                            source = words[:, 256 * g + u : 256 * (g + 1) : 2]
-                        else:
+                        if g < sorted_count[m]:
                             source = sorted_words[m][:, g, u, :]
+                        else:
+                            source = words[:, 256 * g + u : 256 * (g + 1) : 2]
                         nc.tensor.transpose(turned[m, b][:, i, u, :], source, ident[:])
-
-        def group_codes(m, banks=(0, 1)):
-            for b in banks:
                 if (m, b) == (TILES - 1, 1):
                     grouped[m, b] = kept("grouped_last", [P, 2, P, 4], BF16, tag="pool_out")
                 else:
@@ -213,16 +185,20 @@ def tile_codebook_patch_mixer_t2_kernel(
 
         def add_x(m, h, c0=0, width=HALF):
             acc, cols = sums[m, h, c0][:], slice(c0, c0 + width)
+            x_row = x_sb[m // 2, h][:, m % 2]
             if h == 0:
                 nc.vector.tensor_tensor(
                     out=y_sb[m, h][:].rearrange("p (u w s) -> p u w s", u=2, s=2),
                     in0=acc.rearrange("p (w u s) -> p u w s", u=2, s=2),
-                    in1=x_sb[m, h][:].rearrange("p (w u s) -> p u w s", u=2, s=2),
+                    in1=x_row.rearrange("p (w u s) -> p u w s", u=2, s=2),
                     op=ADD,
                 )
             else:
-                nc.vector.tensor_tensor(out=y_sb[m, h][:, cols], in0=acc, in1=x_sb[m, h][:, cols], op=ADD)
+                nc.vector.tensor_tensor(out=y_sb[m, h][:, cols], in0=acc, in1=x_row[:, cols], op=ADD)
             give_bank("book%d%d%d" % (m, h, c0))
+
+        def widen_gain():
+            nc.vector.tensor_copy(out=gain[:], in_=gain_raw[:].rearrange("p g t -> p (g t)"))
 
         e_rows, e_words = {}, {}
 
@@ -233,16 +209,6 @@ def tile_codebook_patch_mixer_t2_kernel(
             cols = slice(c0, c0 + width)
             nc.scalar.activation(
                 out=e_rows[g, h][:, t, cols], in_=y_sb[m, h][:, cols], func=ACT.Copy, scale=gain[:, m : m + 1]
-            )
-
-        def scale_y_on_vector(m, h, c0, width):
-            cols = slice(c0, c0 + width)
-            nc.vector.tensor_scalar(
-                out=e_rows[m // 4, h][:, m % 4, cols],
-                in0=y_sb[m, h][:, cols],
-                scalar1=gain[:, m : m + 1],
-                scalar2=None,
-                op0=MULT,
             )
 
         def new_e_words(g, h, share, tag):
@@ -283,19 +249,21 @@ def tile_codebook_patch_mixer_t2_kernel(
         def load_row_scales():
             rows = row_s_raw[:].bitcast(I32)
             for r in range(4):
-                source = row_scales.rearrange("g (q r) n -> r q g n", r=4)[r].bitcast(I32)
-                nc.sync.dma_start(out=rows[8 * r : 8 * (r + 1)], in_=source)
+                source = row_scales.rearrange("g (q r) (a n) -> r (g q) a n", r=4, a=2)[r].bitcast(I32)
+                nc.sync.dma_start(out=rows[16 * r : 16 * (r + 1)], in_=source)
 
         def deal_row_scales():
             nc.vector.tensor_copy(
-                out=row_s_dealt[:].rearrange("p (a t c n) -> p a c t n", a=2, t=4, n=16),
-                in_=row_s_raw[:].rearrange("p (a c n t) -> p a c t n", a=2, t=4, n=16),
+                out=row_s_dealt[:].rearrange("p (t c n) -> p c t n", t=4, n=16),
+                in_=row_s_raw[:].rearrange("p (c n t) -> p c t n", t=4, n=16),
             )
 
         def place_row_scales():
             dealt = row_s_dealt[:].bitcast(I32)
             for r in range(4):
-                nc.sync.dma_start(out=row_s[:].bitcast(I32)[r:P:32], in_=dealt[8 * r : 8 * (r + 1)])
+                for g in range(2):
+                    first = 16 * r + 8 * g
+                    nc.sync.dma_start(out=row_s[:].bitcast(I32)[r:P:32, g], in_=dealt[first : first + 8])
 
         mixed, z_sb, z_moved, z_blocks, z_turned, z_grouped = {}, {}, {}, {}, {}, {}
 
@@ -319,8 +287,6 @@ def tile_codebook_patch_mixer_t2_kernel(
                 z_sb[m] = kept("z%d" % m, [P, 2 * HALF], BF16, tag="codes_raw%d" % m)
             if m < ON_TENSOR:
                 return z_sb[m][:].rearrange("p (h u d k) -> p h u d k", d=4, h=2, u=2)[:, h]
-            if m < BY_HALVES:
-                return z_sb[m][:].rearrange("p (h d u k) -> p h u d k", d=4, h=2, u=2)[:, h]
             return z_sb[m][:].rearrange("p (d h u k) -> p h u d k", d=4, h=2, u=2)[:, h]
 
         def add_y(m, h):
@@ -468,71 +434,97 @@ def tile_codebook_patch_mixer_t2_kernel(
                 chan_product(m, c0, HALF, (0,))
             gate_product(m, n * HALF, HALF, (1,))
             chan_product(m, n * HALF, HALF, (1,))
-        load_codes(0, parts=2)
-        load_codes(1)
-        load_scales(book_s[0], book_scales[:, :, scale_cols(0)])
-        load_book_passes(0, 0, 2)
-        load_codes(2)
-        load_book_passes(0, 2, 2)
-        load_codes(3)
-        load_x(0, 0)
-        nc.sync.dma_start(out=gain_raw[:], in_=patch_gain.rearrange("(g p t) -> p g t", p=P, t=4))
-        load_x(1, 0)
-        for m in range(4, TILES):
-            load_codes(m)
-            load_x(m - 2, 0)
 
-        warm_up("warm0", 3)
-        sort_codes(0, parts=2)
-        turn_codes(0)
-        group_codes(0)
-        warm_up("warm1", 2)
-        sort_codes(1)
-        quantize_codes(0)
-        turn_codes(1)
-        group_codes(1)
-        warm_up("warm2", 1)
-        clear(row_s)
-        clear(chan_s)
-        quantize_codes(1)
+        make_identity(nc, ident[:])
+        nc.vector.memset(codes_q[TILES - 1][:, 0:P], 0)
+        clear(codes_s[TILES - 1][:, 0:P])
+        clear(book_w[1][:, 0, :])
+        clear(book_s[1][:, 0, :])
+        clear(book_s[0][:].rearrange("p g n -> p (g n)"))
+        clear(book_s[1][:, 1:4, :].rearrange("p g n -> p (g n)"))
+        clear(row_s_raw[:])
+
+        for first in (0, 2):
+            for m in range(2):
+                load_codes(m, first, 2)
+        load_scales(book_s[0], book_scales[:, :, half_cols(0)])
+        load_book(0, 0, 2)
+        load_codes(2, 0, 2)
+        load_codes(2, 2, 2)
+        load_book(0, 2, 2)
+        load_codes(3, 0, 2)
+        load_codes(3, 2, 2)
+        load_x(0, 0, 1)
+        load_codes(4)
+        load_x(1, 0, 1)
+        load_gain()
+        load_codes(5)
+        load_x(2, 0)
+        load_codes(6)
+        load_codes(7)
+        load_x(4, 0)
+
+        warm_up("warm0", 4)
+        sort_codes(0, 0, 2)
+        turn_codes(0, (0,))
+        sort_codes(1, 0, 2)
+        clear(row_s[:, 0])
+        turn_codes(1, (0,))
+        warm_up("warm2", 2)
+        sort_codes(0, 2, 2)
+        clear(row_s[:, 1])
+        turn_codes(0, (1,))
+        sort_codes(1, 2, 2)
+        quantize_codes(0, (0,))
+        quantize_codes(1, (0,))
+        clear(chan_s[:, 0])
+        clear(chan_s[:, 1])
+        turn_codes(1, (1,))
 
         load_row_scales()
-        load_words(book_w[1], book_words[:, :, word_cols(1)])
-        load_scales(book_s[1], book_scales[:, :, scale_cols(1)])
+        load_book(1, 0, 4)
+        load_scales(book_s[1], book_scales[:, :, half_cols(1)])
         load_x(6, 0)
         load_x(0, 1)
-        load_words(row_w_raw[0], row_words[:, :, word_cols(0)])
-        load_x(7, 0)
-        load_x(1, 1)
-        load_words(row_w_raw[1], row_words[:, :, word_cols(1)])
-        for m in range(2, TILES):
-            load_x(m, 1)
+        load_row_words(0)
+        load_x(2, 1)
+        load_row_words(1)
+        load_x(4, 1)
+        load_x(6, 1)
 
-
-        book_product(0, 0, passes=(0, 1))
+        for m in range(2):
+            book_product(m, 0, passes=(0, 1))
+        quantize_codes(0, (1,))
+        for b in range(2):
+            sort_codes(2, 2 * b, 2)
+        quantize_codes(1, (1,))
         turn_codes(2)
-        group_codes(2)
-        book_product(0, 0, passes=(2, 3))
-        book_product(1, 0)
-        sort_first_passes(3)
-        quantize_codes(2)
+        for m in range(2):
+            book_product(m, 0, passes=(2, 3))
+        for b in range(2):
+            sort_codes(3, 2 * b, 2)
+            quantize_codes(2, (b,))
+        turn_codes(3)
         add_x(0, 0)
-        nc.vector.tensor_copy(out=gain[:], in_=gain_raw[:].rearrange("p g t -> p (g t)"))
         for m in range(2, TILES - 1):
-            turn_codes(m + 1)
-            group_codes(m + 1)
-            if m == 2:
+            if m > 2:
+                turn_codes(m + 1)
+            if m == 3:
+                widen_gain()
                 scale_y(0, 0)
             book_product(m, 0)
-            if m + 2 < TILES - 1:
-                sort_first_passes(m + 2)
-            elif m + 2 == TILES - 1:
-                sort_codes(m + 2)
+            if m + 2 < TILES:
+                sort_codes(m + 2, 0, SORTED_PASSES if m + 2 < TILES - 1 else ALL_SORTED)
             else:
                 deal_row_scales()
+            if m == 2:
+                quantize_codes(m + 1)
             add_x(m - 1, 0)
-            scale_y(m - 1, 0)
-            quantize_codes(m + 1)
+            if m > 2:
+                if m == 4:
+                    scale_y(1, 0)
+                scale_y(m - 1, 0)
+                quantize_codes(m + 1)
         place_row_scales()
         for h in range(2):
             nc.sync.dma_start(out=chan_w[h][:].bitcast(I32), in_=chan_words[h].bitcast(I32))

@@ -60,7 +60,7 @@ def tile_codebook_patch_mixer_t2_kernel(
         codes_s = [kept("codes_s%d" % m, [P, 4 * P], U8) for m in range(TILES)]
         book_w = [kept("book_w%d" % h, [P, 4, 2 * HALF], U8) for h in range(2)]
         book_s = [kept("book_s%d" % h, [P, 4, HALF], U8) for h in range(2)]
-        x_sb = {(k, h): kept("x%d%d" % (k, h), [P, 2, HALF], BF16) for k in range(TILES // 2) for h in range(2)}
+        x_sb = {(m, h): kept("x%d%d" % (m, h), [P, HALF], BF16) for m, h in halves}
         y_sb = {(m, h): kept("y%d%d" % (m, h), [P, HALF], F32) for m, h in halves}
         e_q = {(g, h): kept("e_q%d%d" % (g, h), [P, HALF], U32) for g, h in groups}
         e_s = {(g, h): kept("e_s%d%d" % (g, h), [P, HALF], U8) for g, h in groups}
@@ -109,8 +109,8 @@ def tile_codebook_patch_mixer_t2_kernel(
             nc.sync.dma_start(out=codes_raw[m][:, cols], in_=codes_v[m // 4, m % 4][:, cols])
 
         def load_x(m, h, count=2):
-            room = x_sb[m // 2, h][:, m % 2 : m % 2 + count]
-            nc.sync.dma_start(out=room, in_=x_v[m // 4][:, m % 4 : m % 4 + count, half_cols(h)])
+            for k in range(m, m + count):
+                nc.sync.dma_start(out=x_sb[k, h][:], in_=x_v[k // 4][:, k % 4, half_cols(h)])
 
         def load_gain():
             nc.sync.dma_start(out=gain_raw[:], in_=patch_gain.rearrange("(g p t) -> p g t", p=P, t=4))
@@ -148,7 +148,7 @@ def tile_codebook_patch_mixer_t2_kernel(
                 for i in range(2):
                     g = 2 * b + i
                     for u in range(2):
-                        if g < sorted_count[m]:
+                        if g < sorted_count.get(m, 0):
                             source = sorted_words[m][:, g, u, :]
                         else:
                             source = words[:, 256 * g + u : 256 * (g + 1) : 2]
@@ -185,7 +185,7 @@ def tile_codebook_patch_mixer_t2_kernel(
 
         def add_x(m, h, c0=0, width=HALF):
             acc, cols = sums[m, h, c0][:], slice(c0, c0 + width)
-            x_row = x_sb[m // 2, h][:, m % 2]
+            x_row = x_sb[m, h][:]
             if h == 0:
                 nc.vector.tensor_tensor(
                     out=y_sb[m, h][:].rearrange("p (u w s) -> p u w s", u=2, s=2),
@@ -449,15 +449,14 @@ def tile_codebook_patch_mixer_t2_kernel(
                 load_codes(m, first, 2)
         load_scales(book_s[0], book_scales[:, :, half_cols(0)])
         load_book(0, 0, 2)
-        load_codes(2, 0, 2)
-        load_codes(2, 2, 2)
+        load_codes(2)
         load_book(0, 2, 2)
         load_codes(3, 0, 2)
         load_codes(3, 2, 2)
         load_x(0, 0, 1)
+        load_gain()
         load_codes(4)
         load_x(1, 0, 1)
-        load_gain()
         load_codes(5)
         load_x(2, 0)
         load_codes(6)
@@ -477,8 +476,6 @@ def tile_codebook_patch_mixer_t2_kernel(
         sort_codes(1, 2, 2)
         quantize_codes(0, (0,))
         quantize_codes(1, (0,))
-        clear(chan_s[:, 0])
-        clear(chan_s[:, 1])
         turn_codes(1, (1,))
 
         load_row_scales()
@@ -494,37 +491,36 @@ def tile_codebook_patch_mixer_t2_kernel(
 
         for m in range(2):
             book_product(m, 0, passes=(0, 1))
+        clear(chan_s[:, 0])
         quantize_codes(0, (1,))
-        for b in range(2):
-            sort_codes(2, 2 * b, 2)
+        clear(chan_s[:, 1])
         quantize_codes(1, (1,))
         turn_codes(2)
         for m in range(2):
             book_product(m, 0, passes=(2, 3))
         for b in range(2):
             sort_codes(3, 2 * b, 2)
-            quantize_codes(2, (b,))
+        quantize_codes(2)
+        widen_gain()
         turn_codes(3)
         add_x(0, 0)
         for m in range(2, TILES - 1):
             if m > 2:
                 turn_codes(m + 1)
-            if m == 3:
-                widen_gain()
-                scale_y(0, 0)
+            scale_y(m - 2, 0)
             book_product(m, 0)
             if m + 2 < TILES:
                 sort_codes(m + 2, 0, SORTED_PASSES if m + 2 < TILES - 1 else ALL_SORTED)
             else:
                 deal_row_scales()
             if m == 2:
+                quantize_codes(m + 1, (0,))
+                add_x(m - 1, 0)
+                quantize_codes(m + 1, (1,))
+            else:
+                add_x(m - 1, 0)
                 quantize_codes(m + 1)
-            add_x(m - 1, 0)
-            if m > 2:
-                if m == 4:
-                    scale_y(1, 0)
-                scale_y(m - 1, 0)
-                quantize_codes(m + 1)
+        scale_y(5, 0)
         place_row_scales()
         for h in range(2):
             nc.sync.dma_start(out=chan_w[h][:].bitcast(I32), in_=chan_words[h].bitcast(I32))
@@ -588,19 +584,21 @@ def tile_codebook_patch_mixer_t2_kernel(
         interleave(nc.vector.tensor_copy, 1, 1, SHARE, SHARE + P)
         interleave(nc.scalar.copy, 1, 1, SHARE + P, HALF)
         quantize_e(1, 1, (0, 1))
-        spill_row(4)
-        add_y_on_pool(4)
+        for m in (1, 4):
+            spill_row(m)
+            add_y_on_pool(m)
         for g in range(2):
-            for m in range(2):
+            for m in range(3):
                 row_product(m, 1, (g,))
         for h in range(2):
             for m in range(2):
-                add_y(m, h)
-        for m in range(2, 4):
-            row_product(m, 1)
+                if h == 1 or m not in (1, 4):
+                    add_y(m, h)
+        row_product(3, 1)
         turn_z_on_tensor(0)
         turn_z_on_tensor(1)
-        add_y(2, 0)
+        if 2 not in (1, 4):
+            add_y(2, 0)
         for h in range(2):
             group_turned_z(0, h)
         add_y(2, 1)
@@ -610,10 +608,13 @@ def tile_codebook_patch_mixer_t2_kernel(
             quantize_z(0, h)
         row_product(4, 1)
         row_product(5, 0)
-        add_y(3, 0)
+        if 3 not in (1, 4):
+            add_y(3, 0)
         add_y(3, 1)
         move_z(3)
         quantize_z(1)
+        if 4 not in (1, 4):
+            add_y(4, 0)
         add_y(4, 1)
         move_z(4)
         half_products(0, 0)

@@ -246,6 +246,13 @@ def tile_codebook_patch_mixer_t2_kernel(
                 in_=row_w_raw[group][:].bitcast(U16).rearrange("p g (c n t) -> p g c t n", n=8, t=4),
             )
 
+        def deal_row_words_on_scalar(group):
+            for g in range(2):
+                nc.scalar.copy(
+                    out=row_w[group][:].bitcast(U16).rearrange("p (g t c n) -> p g c t n", g=2, t=4, n=8)[:, g],
+                    in_=row_w_raw[group][:].bitcast(U16).rearrange("p g (c n t) -> p g c t n", n=8, t=4)[:, g],
+                )
+
         def load_row_scales():
             rows = row_s_raw[:].bitcast(I32)
             for r in range(4):
@@ -311,8 +318,11 @@ def tile_codebook_patch_mixer_t2_kernel(
 
         spilled = {}
 
-        def spill_row(m):
-            spilled[m] = ringed("spilled%d" % m, [P, HALF], F32, "values", 2)
+        def spill_row(m, room=None):
+            if room:
+                spilled[m] = kept("spilled%d" % m, [P, HALF], F32, tag=room)
+            else:
+                spilled[m] = ringed("spilled%d" % m, [P, HALF], F32, "values", 3)
             nc.scalar.copy(out=spilled[m][:], in_=mixed[m, 0][:])
             give_bank("row%d0" % m)
 
@@ -415,7 +425,7 @@ def tile_codebook_patch_mixer_t2_kernel(
         pool_values, pool_results = {}, {}
 
         def spill_values(m, c0):
-            values = ringed("values%d_%d" % (m, c0), [P, HALF], F32, "values", 2)
+            values = ringed("values%d_%d" % (m, c0), [P, HALF], F32, "values", 3)
             nc.scalar.copy(out=values[:], in_=h_sums[m, c0][:])
             give_bank("chan%d_%d" % (m, c0))
             pool_values[m, c0] = values
@@ -454,8 +464,8 @@ def tile_codebook_patch_mixer_t2_kernel(
         load_codes(3, 0, 2)
         load_codes(3, 2, 2)
         load_x(0, 0, 1)
-        load_gain()
         load_codes(4)
+        load_gain()
         load_x(1, 0, 1)
         load_codes(5)
         load_x(2, 0)
@@ -501,16 +511,22 @@ def tile_codebook_patch_mixer_t2_kernel(
         for b in range(2):
             sort_codes(3, 2 * b, 2)
         quantize_codes(2)
-        widen_gain()
         turn_codes(3)
         add_x(0, 0)
         for m in range(2, TILES - 1):
             if m > 2:
                 turn_codes(m + 1)
-            scale_y(m - 2, 0)
+            if m > 2:
+                scale_y(m - 2, 0)
             book_product(m, 0)
             if m + 2 < TILES:
-                sort_codes(m + 2, 0, SORTED_PASSES if m + 2 < TILES - 1 else ALL_SORTED)
+                if m == 2:
+                    sort_codes(4, 0, 2)
+                    sort_codes(4, 2, 1)
+                    widen_gain()
+                    scale_y(0, 0)
+                else:
+                    sort_codes(m + 2, 0, SORTED_PASSES if m + 2 < TILES - 1 else ALL_SORTED)
             else:
                 deal_row_scales()
             if m == 2:
@@ -546,37 +562,34 @@ def tile_codebook_patch_mixer_t2_kernel(
         new_e_words(1, 0, 0, "pool_out")
         interleave_on_pool(1, 0, 0)
         new_e_words(1, 0, 1, "e_words11")
-        interleave(nc.scalar.copy, 1, 0, SHARE, HALF)
+        interleave_on_pool(1, 0, 1, P)
+        interleave(nc.scalar.copy, 1, 0, SHARE + P, HALF)
         scale_y(1, 1)
         for m in (3, 4):
             book_product(m, 1)
             add_x(m - 1, 1)
             scale_y(m - 1, 1)
-        deal_row_words(1)
-        quantize_e(1, 0, (1, 0))
         book_product(5, 1)
         add_x(4, 1)
+        quantize_e(1, 0, (0, 1))
         new_e_words(0, 1, 0, "pool_out")
         interleave_on_pool(0, 1, 0)
         new_e_words(0, 1, 1, "e_words01")
-        interleave_on_pool(0, 1, 1, P)
-        interleave(nc.scalar.copy, 0, 1, SHARE + P, HALF)
+        interleave(nc.scalar.copy, 0, 1, SHARE, HALF)
         scale_y(4, 1)
         book_product(6, 1)
         add_x(5, 1)
         scale_y(5, 1)
-
         for c0 in (0, SHARE):
             book_product(7, 1, c0, SHARE)
         add_x(6, 1)
         scale_y(6, 1)
         for c0 in (0, SHARE):
             add_x(7, 1, c0, SHARE)
-        quantize_e(0, 1, (0, 1))
+        quantize_e(0, 1, (1, 0))
         for c0 in (0, SHARE):
             scale_y(7, 1, c0, SHARE)
-
-        for m in range(5):
+        for m in range(4):
             row_product(m, 0)
         for share in range(2):
             new_e_words(1, 1, share, "e_words1%d" % share)
@@ -584,21 +597,20 @@ def tile_codebook_patch_mixer_t2_kernel(
         interleave(nc.vector.tensor_copy, 1, 1, SHARE, SHARE + P)
         interleave(nc.scalar.copy, 1, 1, SHARE + P, HALF)
         quantize_e(1, 1, (0, 1))
-        for m in (1, 4):
-            spill_row(m)
-            add_y_on_pool(m)
+        spill_row(3)
+        add_y_on_pool(3)
+        deal_row_words_on_scalar(1)
         for g in range(2):
-            for m in range(3):
+            for m in range(4):
                 row_product(m, 1, (g,))
-        for h in range(2):
-            for m in range(2):
-                if h == 1 or m not in (1, 4):
-                    add_y(m, h)
-        row_product(3, 1)
+        add_y(0, 0)
+        add_y(1, 0)
+        add_y(0, 1)
+        add_y(1, 1)
+        row_product(4, 0)
         turn_z_on_tensor(0)
         turn_z_on_tensor(1)
-        if 2 not in (1, 4):
-            add_y(2, 0)
+        add_y(2, 0)
         for h in range(2):
             group_turned_z(0, h)
         add_y(2, 1)
@@ -608,26 +620,23 @@ def tile_codebook_patch_mixer_t2_kernel(
             quantize_z(0, h)
         row_product(4, 1)
         row_product(5, 0)
-        if 3 not in (1, 4):
-            add_y(3, 0)
+        row_product(5, 1)
         add_y(3, 1)
         move_z(3)
         quantize_z(1)
-        if 4 not in (1, 4):
-            add_y(4, 0)
+        spill_row(4, "y01")
+        add_y_on_pool(4)
         add_y(4, 1)
         move_z(4)
         half_products(0, 0)
         spill_values(0, 0)
         pool_product(0, 0, None)
-        row_product(5, 1)
         add_y(5, 0)
         add_y(5, 1)
         move_z(5)
         half_products(0, 1)
         spill_values(0, HALF)
         turn_z(2)
-        pool_product(0, HALF, None)
         for g in range(2):
             for h in range(2):
                 row_product(6, h, (g,))
@@ -639,8 +648,8 @@ def tile_codebook_patch_mixer_t2_kernel(
         half_products(1, 0)
         turn_z(3)
         quantize_z(2)
+        pool_product(0, HALF, "y20")
         spill_values(1, 0)
-        pool_product(1, 0, "y20")
         for g in range(2):
             for h in range(2):
                 row_product(7, h, (g,))
@@ -648,22 +657,21 @@ def tile_codebook_patch_mixer_t2_kernel(
         add_y(7, 0)
         add_y(7, 1)
         move_z(7)
-        store_pool_result(0, HALF)
         half_products(1, 1)
         turn_z(4)
         quantize_z(3)
-        spill_values(1, HALF)
-        pool_product(1, HALF, "y30")
+        pool_product(1, 0, "y30")
+        store_pool_result(0, HALF)
+        store_product(1, HALF)
         half_products(2, 0)
         group_z(4)
         turn_z(5)
-        store_pool_result(1, 0)
         half_products(2, 1)
         store_product(2, 0)
         quantize_z(4)
+        store_pool_result(1, 0)
         group_z(5)
         turn_z(6)
-        store_pool_result(1, HALF)
         half_products(3, 0)
         store_product(2, HALF)
         quantize_z(5)

@@ -85,9 +85,9 @@ def tile_codebook_patch_mixer_t2_kernel(
             for i in range(passes):
                 nc.tensor.matmul_mx(
                     out=acc[:],
-                    lhsT=codes_q[TILES - 1][:, 0:P].bitcast(FP8X4),
-                    lhsT_scale=codes_s[TILES - 1][:, 0:P],
-                    rhs=book_w[1][:, 0, :].bitcast(FP4X4),
+                    lhsT=book_s[1][:, 0, :].bitcast(FP8X4),
+                    lhsT_scale=book_s[1][:, 0, 0:P],
+                    rhs=book_s[1][:, 0:2, :].rearrange("p g n -> p (g n)").bitcast(FP4X4),
                     rhs_scale=book_s[1][:, 0, :],
                     start=True,
                     stop=True,
@@ -445,13 +445,10 @@ def tile_codebook_patch_mixer_t2_kernel(
             gate_product(m, n * HALF, HALF, (1,))
             chan_product(m, n * HALF, HALF, (1,))
 
+        nc.gpsimd.memset(book_s[1][:, 0:2, :].rearrange("p g n -> p (g n)").bitcast(I32), 0)
         make_identity(nc, ident[:])
-        nc.vector.memset(codes_q[TILES - 1][:, 0:P], 0)
-        clear(codes_s[TILES - 1][:, 0:P])
-        clear(book_w[1][:, 0, :])
-        clear(book_s[1][:, 0, :])
         clear(book_s[0][:].rearrange("p g n -> p (g n)"))
-        clear(book_s[1][:, 1:4, :].rearrange("p g n -> p (g n)"))
+        clear(book_s[1][:, 2:4, :].rearrange("p g n -> p (g n)"))
         clear(row_s_raw[:])
 
         for first in (0, 2):
@@ -473,7 +470,7 @@ def tile_codebook_patch_mixer_t2_kernel(
         load_codes(7)
         load_x(4, 0)
 
-        warm_up("warm0", 4)
+        warm_up("warm0", 3)
         sort_codes(0, 0, 2)
         turn_codes(0, (0,))
         sort_codes(1, 0, 2)

@@ -465,8 +465,9 @@ def tile_codebook_patch_mixer_t2_kernel(
         load_gain()
         load_x(1, 0, 1)
         load_codes(5)
-        load_x(2, 0)
+        load_x(2, 0, 1)
         load_codes(6)
+        load_x(3, 0, 1)
         load_codes(7)
         load_x(4, 0)
 
@@ -486,8 +487,9 @@ def tile_codebook_patch_mixer_t2_kernel(
         turn_codes(1, (1,))
 
         load_row_scales()
-        load_book(1, 0, 4)
+        load_book(1, 0, 2)
         load_scales(book_s[1], book_scales[:, :, half_cols(1)])
+        load_book(1, 2, 2)
         load_x(6, 0)
         load_x(0, 1)
         load_row_words(0)

@@ -22,7 +22,7 @@ TILES = 8
 HALF = 512
 SHARE = 256
 ON_TENSOR = 2
-SORTED_PASSES = 3
+SORTED_PASSES = 4
 ALL_SORTED = 4
 
 
@@ -80,7 +80,7 @@ def tile_codebook_patch_mixer_t2_kernel(
         def clear(room):
             nc.vector.memset(room.bitcast(I32), 0)
 
-        def warm_up(name, passes):
+        def warm_up(name, passes, scales):
             acc = take_bank(name, [P, HALF])
             for i in range(passes):
                 nc.tensor.matmul_mx(
@@ -88,7 +88,7 @@ def tile_codebook_patch_mixer_t2_kernel(
                     lhsT=book_s[1][:, 0, :].bitcast(FP8X4),
                     lhsT_scale=book_s[1][:, 0, 0:P],
                     rhs=book_s[1][:, 0:2, :].rearrange("p g n -> p (g n)").bitcast(FP4X4),
-                    rhs_scale=book_s[1][:, 0, :],
+                    rhs_scale=scales[:, 0, :],
                     start=True,
                     stop=True,
                 )
@@ -456,7 +456,8 @@ def tile_codebook_patch_mixer_t2_kernel(
                 load_codes(m, first, 2)
         load_scales(book_s[0], book_scales[:, :, half_cols(0)])
         load_book(0, 0, 2)
-        load_codes(2)
+        load_codes(2, 0, 2)
+        load_codes(2, 2, 2)
         load_book(0, 2, 2)
         load_codes(3, 0, 2)
         load_codes(3, 2, 2)
@@ -471,13 +472,13 @@ def tile_codebook_patch_mixer_t2_kernel(
         load_codes(7)
         load_x(4, 0)
 
-        warm_up("warm0", 3)
+        warm_up("warm0", 3, book_s[1])
         sort_codes(0, 0, 2)
         turn_codes(0, (0,))
         sort_codes(1, 0, 2)
         clear(row_s[:, 0])
         turn_codes(1, (0,))
-        warm_up("warm2", 2)
+        warm_up("warm2", 2, book_s[1])
         sort_codes(0, 2, 2)
         clear(row_s[:, 1])
         turn_codes(0, (1,))
@@ -485,6 +486,7 @@ def tile_codebook_patch_mixer_t2_kernel(
         quantize_codes(0, (0,))
         quantize_codes(1, (0,))
         turn_codes(1, (1,))
+        warm_up("warm4", 1, book_s[0])
 
         load_row_scales()
         load_book(1, 0, 2)
@@ -501,9 +503,11 @@ def tile_codebook_patch_mixer_t2_kernel(
         for m in range(2):
             book_product(m, 0, passes=(0, 1))
         clear(chan_s[:, 0])
-        quantize_codes(0, (1,))
+        for b in range(2):
+            sort_codes(2, 2 * b, 2)
+        for m in range(2):
+            quantize_codes(m, (1,))
         clear(chan_s[:, 1])
-        quantize_codes(1, (1,))
         turn_codes(2)
         for m in range(2):
             book_product(m, 0, passes=(2, 3))
@@ -521,7 +525,7 @@ def tile_codebook_patch_mixer_t2_kernel(
             if m + 2 < TILES:
                 if m == 2:
                     sort_codes(4, 0, 2)
-                    sort_codes(4, 2, 1)
+                    sort_codes(4, 2, 2)
                     widen_gain()
                     scale_y(0, 0)
                 else:
@@ -529,9 +533,8 @@ def tile_codebook_patch_mixer_t2_kernel(
             else:
                 deal_row_scales()
             if m == 2:
-                quantize_codes(m + 1, (0,))
+                quantize_codes(m + 1)
                 add_x(m - 1, 0)
-                quantize_codes(m + 1, (1,))
             else:
                 add_x(m - 1, 0)
                 quantize_codes(m + 1)

from contextlib import ExitStack

import concourse.mybir as mybir
from concourse.masks import make_identity

FLOPS = 2 * 1024 * 1024 * (2048 + 1024 + 2048)

F32 = mybir.dt.float32
BF16 = mybir.dt.bfloat16
U32 = mybir.dt.uint32
I32 = mybir.dt.int32
U16 = mybir.dt.uint16
U8 = mybir.dt.uint8
FP8X4 = mybir.dt.float8_e4m3fn_x4
FP4X4 = mybir.dt.float4_e2m1fn_x4
ADD = mybir.AluOpType.add
MULT = mybir.AluOpType.mult
ACT = mybir.ActivationFunctionType

P = 128
TILES = 8
HALF = 512
SHARE = 256
ON_TENSOR = 2
SORTED_PASSES = 4
ALL_SORTED = 4


def tile_codebook_patch_mixer_t2_kernel(
    tc, x, codes, patch_gain, book_words, book_scales, row_words, row_scales, chan_words, chan_scales, out
):
    nc = tc.nc
    with ExitStack() as ctx:
        keep = ctx.enter_context(tc.tile_pool(name="keep", bufs=1))
        ring = ctx.enter_context(tc.tile_pool(name="ring", bufs=2))
        psum = ctx.enter_context(tc.psum_pool(name="psum", bufs=1))
        ctx.enter_context(tc.manual_schedule())

        def kept(name, shape, dtype, tag=None):
            return keep.tile(shape, dtype, name=name, tag=tag or name, align_bytes=64)

        def ringed(name, shape, dtype, tag, bufs):
            return ring.tile(shape, dtype, name=name, tag=tag, bufs=bufs, align_bytes=64)

        free_banks = list(range(8))
        bank_of = {}

        def take_bank(name, shape):
            bank_of[name] = free_banks[0]
            free_banks.remove(bank_of[name])
            return psum.tile(shape, F32, name=name, tag="bank%d" % bank_of[name])

        def give_bank(name):
            free_banks.append(bank_of[name])

        halves = [(m, h) for m in range(TILES) for h in range(2)]
        groups = [(g, h) for g in range(2) for h in range(2)]
        codes_raw = [kept("codes_raw%d" % m, [P, 2048], BF16) for m in range(TILES)]
        codes_q = [kept("codes_q%d" % m, [P, 4 * P], U32) for m in range(TILES)]
        codes_s = [kept("codes_s%d" % m, [P, 4 * P], U8) for m in range(TILES)]
        book_w = [kept("book_w%d" % h, [P, 4, 2 * HALF], U8) for h in range(2)]
        book_s = [kept("book_s%d" % h, [P, 4, HALF], U8) for h in range(2)]
        x_sb = {(m, h): kept("x%d%d" % (m, h), [P, HALF], BF16) for m, h in halves}
        y_sb = {(m, h): kept("y%d%d" % (m, h), [P, HALF], F32) for m, h in halves}
        e_q = {(g, h): kept("e_q%d%d" % (g, h), [P, HALF], U32) for g, h in groups}
        e_s = {(g, h): kept("e_s%d%d" % (g, h), [P, HALF], U8) for g, h in groups}
        row_w_raw = [kept("row_w_raw%d" % g, [P, 2, 2 * HALF], U8) for g in range(2)]
        row_s_raw = kept("row_s_raw", [P, HALF], U8)
        row_s_dealt = kept("row_s_dealt", [P, HALF], U8)
        row_s = kept("row_s", [P, 2, 2 * HALF], U8)
        row_w = [kept("row_w%d" % (4 * g), [P, 4 * HALF], U8) for g in range(2)]
        chan_w = [kept("chan_w%d" % h, [P, 4096], U8) for h in range(2)]
        chan_s = kept("chan_s", [P, 2, 2048], U8)
        z_q = [kept("z_q%d" % m, [P, 2 * P], U32) for m in range(TILES)]
        z_s = [kept("z_s%d" % m, [P, 2 * P], U8) for m in range(TILES)]
        ident = kept("ident", [P, P], F32)
        gain_raw = kept("gain_raw", [P, 2, 4], BF16)
        gain = kept("gain", [P, TILES], F32)

        def clear(room):
            nc.vector.memset(room.bitcast(I32), 0)

        def warm_up(name, passes, scales):
            acc = take_bank(name, [P, HALF])
            for i in range(passes):
                nc.tensor.matmul_mx(
                    out=acc[:],
                    lhsT=book_s[1][:, 0, :].bitcast(FP8X4),
                    lhsT_scale=book_s[1][:, 0, 0:P],
                    rhs=book_s[1][:, 0:2, :].rearrange("p g n -> p (g n)").bitcast(FP4X4),
                    rhs_scale=scales[:, 0, :],
                    start=True,
                    stop=True,
                )
            give_bank(name)

        codes_v = codes.rearrange("(g p t) j -> g t p j", p=P, t=4)
        x_v = x.rearrange("(g p t) c -> g p t c", p=P, t=4)
        out_v = out.rearrange("(g p t) c -> g t p c", p=P, t=4)

        def word_cols(h):
            return slice(h * 2 * HALF, (h + 1) * 2 * HALF)

        def half_cols(h):
            return slice(h * HALF, (h + 1) * HALF)

        def load_codes(m, first=0, count=4):
            cols = slice(first * 512, (first + count) * 512)
            nc.sync.dma_start(out=codes_raw[m][:, cols], in_=codes_v[m // 4, m % 4][:, cols])

        def load_x(m, h, count=2):
            for k in range(m, m + count):
                nc.sync.dma_start(out=x_sb[k, h][:], in_=x_v[k // 4][:, k % 4, half_cols(h)])

        def load_gain():
            nc.sync.dma_start(out=gain_raw[:], in_=patch_gain.rearrange("(g p t) -> p g t", p=P, t=4))

        def load_scales(plane, scales):
            rows = plane[:].bitcast(I32)
            for r in range(4):
                nc.sync.dma_start(out=rows[r:P:32], in_=scales.rearrange("g (q r) n -> r q g n", r=4)[r].bitcast(I32))

        def load_book(h, first, count):
            source = book_words[first : first + count, :, word_cols(h)].bitcast(I32).rearrange("g p b -> p g b")
            nc.sync.dma_start(out=book_w[h][:, first : first + count].bitcast(I32), in_=source)

        def load_row_words(group):
            source = row_words[:, :, word_cols(group)].bitcast(I32).rearrange("g p b -> p g b")
            nc.sync.dma_start(out=row_w_raw[group][:].bitcast(I32), in_=source)

        sorted_words, sorted_count, turned, grouped, sums = {}, {}, {}, {}, {}

        def sort_codes(m, first=0, count=4):
            if first == 0:
                sorted_words[m] = ringed("sorted%d" % m, [P, 4, 2, P], F32, "sorted", 3)
            sorted_count[m] = first + count
            walk = "p g c u w" if count % 2 == 0 else "p c g u w"
            raw = codes_raw[m][:, first * 512 : (first + count) * 512].bitcast(F32)
            nc.vector.tensor_copy(
                out=sorted_words[m][:, first : first + count].rearrange("p g u (c w) -> " + walk, w=4),
                in_=raw.rearrange("p (g c w u) -> " + walk, g=count, w=4, u=2),
            )

        def turn_codes(m, banks=(0, 1)):
            words = codes_raw[m][:].bitcast(F32)
            for b in banks:
                turned[m, b] = take_bank("turn%d%d" % (m, b), [P, 2, 2, P])
                for i in range(2):
                    g = 2 * b + i
                    for u in range(2):
                        if g < sorted_count.get(m, 0):
                            source = sorted_words[m][:, g, u, :]
                        else:
                            source = words[:, 256 * g + u : 256 * (g + 1) : 2]
                        nc.tensor.transpose(turned[m, b][:, i, u, :], source, ident[:])
                if (m, b) == (TILES - 1, 1):
                    grouped[m, b] = kept("grouped_last", [P, 2, P, 4], BF16, tag="pool_out")
                else:
                    grouped[m, b] = ringed("grouped%d%d" % (m, b), [P, 2, P, 4], BF16, "grouped", 5)
                nc.scalar.copy(out=grouped[m, b][:].bitcast(F32), in_=turned[m, b][:].rearrange("p i u n -> p i n u"))
                give_bank("turn%d%d" % (m, b))

        def quantize_codes(m, banks=(0, 1)):
            for b in banks:
                cols = slice(b * 2 * P, (b + 1) * 2 * P)
                nc.vector.quantize_mx(
                    out=codes_q[m][:, cols].bitcast(FP8X4),
                    scales=codes_s[m][:, cols],
                    in_=grouped[m, b][:].rearrange("p g n t -> p (g n t)"),
                )

        def book_product(m, h, c0=0, width=HALF, passes=range(4)):
            if (m, h, c0) not in sums:
                sums[m, h, c0] = take_bank("book%d%d%d" % (m, h, c0), [P, width])
            for g in passes:
                nc.tensor.matmul_mx(
                    out=sums[m, h, c0][:],
                    lhsT=codes_q[m][:, g * P : (g + 1) * P].bitcast(FP8X4),
                    lhsT_scale=codes_s[m][:, g * P : (g + 1) * P],
                    rhs=book_w[h][:, g, 2 * c0 : 2 * (c0 + width)].bitcast(FP4X4),
                    rhs_scale=book_s[h][:, g, c0 : c0 + width],
                    start=(g == 0),
                    stop=(g == 3),
                )

        def add_x(m, h, c0=0, width=HALF):
            acc, cols = sums[m, h, c0][:], slice(c0, c0 + width)
            x_row = x_sb[m, h][:]
            if h == 0:
                nc.vector.tensor_tensor(
                    out=y_sb[m, h][:].rearrange("p (u w s) -> p u w s", u=2, s=2),
                    in0=acc.rearrange("p (w u s) -> p u w s", u=2, s=2),
                    in1=x_row.rearrange("p (w u s) -> p u w s", u=2, s=2),
                    op=ADD,
                )
            else:
                nc.vector.tensor_tensor(out=y_sb[m, h][:, cols], in0=acc, in1=x_row[:, cols], op=ADD)
            give_bank("book%d%d%d" % (m, h, c0))

        def widen_gain():
            nc.vector.tensor_copy(out=gain[:], in_=gain_raw[:].rearrange("p g t -> p (g t)"))

        e_rows, e_words = {}, {}

        def scale_y(m, h, c0=0, width=HALF):
            g, t = m // 4, m % 4
            if (g, h) not in e_rows:
                e_rows[g, h] = ringed("e_rows%d%d" % (g, h), [P, 4, HALF], BF16, "e_rows", 3)
            cols = slice(c0, c0 + width)
            nc.scalar.activation(
                out=e_rows[g, h][:, t, cols], in_=y_sb[m, h][:, cols], func=ACT.Copy, scale=gain[:, m : m + 1]
            )

        def new_e_words(g, h, share, tag):
            e_words[g, h, share] = kept("e_words%d%d%d" % (g, h, share), [P, SHARE, 4], BF16, tag=tag)

        def interleave(copy, g, h, c0, c1):
            share, first = c0 // SHARE, c0 % SHARE
            copy(
                out=e_words[g, h, share][:, first : first + c1 - c0, :].rearrange("p (c i) t -> p c t i", i=4),
                in_=e_rows[g, h][:, :, c0:c1].rearrange("p t (c i) -> p c t i", i=4),
            )

        def interleave_on_pool(g, h, share, width=SHARE):
            nc.gpsimd.tensor_scalar(
                out=e_words[g, h, share][:, 0:width],
                in0=e_rows[g, h][:, :, share * SHARE : share * SHARE + width].rearrange("p t c -> p c t"),
                scalar1=1.0,
                scalar2=1.0,
                op0=MULT,
                op1=MULT,
            )

        def quantize_e(g, h, shares):
            for share in shares:
                cols = slice(share * SHARE, (share + 1) * SHARE)
                nc.vector.quantize_mx(
                    out=e_q[g, h][:, cols].bitcast(FP8X4),
                    scales=e_s[g, h][:, cols],
                    in_=e_words[g, h, share][:].rearrange("p c t -> p (c t)"),
                )

        def deal_row_words(group):
            nc.vector.tensor_copy(
                out=row_w[group][:].bitcast(U16).rearrange("p (g t c n) -> p g c t n", g=2, t=4, n=8),
                in_=row_w_raw[group][:].bitcast(U16).rearrange("p g (c n t) -> p g c t n", n=8, t=4),
            )

        def deal_row_words_on_scalar(group):
            for g in range(2):
                nc.scalar.copy(
                    out=row_w[group][:].bitcast(U16).rearrange("p (g t c n) -> p g c t n", g=2, t=4, n=8)[:, g],
                    in_=row_w_raw[group][:].bitcast(U16).rearrange("p g (c n t) -> p g c t n", n=8, t=4)[:, g],
                )

        def load_row_scales():
            rows = row_s_raw[:].bitcast(I32)
            for r in range(4):
                source = row_scales.rearrange("g (q r) (a n) -> r (g q) a n", r=4, a=2)[r].bitcast(I32)
                nc.sync.dma_start(out=rows[16 * r : 16 * (r + 1)], in_=source)

        def deal_row_scales():
            nc.vector.tensor_copy(
                out=row_s_dealt[:].rearrange("p (t c n) -> p c t n", t=4, n=16),
                in_=row_s_raw[:].rearrange("p (c n t) -> p c t n", t=4, n=16),
            )

        def place_row_scales():
            dealt = row_s_dealt[:].bitcast(I32)
            for r in range(4):
                for g in range(2):
                    first = 16 * r + 8 * g
                    nc.sync.dma_start(out=row_s[:].bitcast(I32)[r:P:32, g], in_=dealt[first : first + 8])

        mixed, z_sb, z_moved, z_blocks, z_turned, z_grouped = {}, {}, {}, {}, {}, {}

        def row_product(m, h, passes=(0, 1)):
            if (m, h) not in mixed:
                mixed[m, h] = take_bank("row%d%d" % (m, h), [P, HALF])
            for g in passes:
                first = (4 * g + m % 4) * P
                nc.tensor.matmul_mx(
                    out=mixed[m, h][:],
                    lhsT=row_w[m // 4][:, 2 * first : 2 * (first + P)].bitcast(FP4X4),
                    lhsT_scale=row_s[:, g, m * P : (m + 1) * P],
                    rhs=e_q[g, h][:].bitcast(FP8X4),
                    rhs_scale=e_s[g, h][:],
                    start=(g == 0),
                    stop=(g == 1),
                )

        def z_target(m, h):
            if m not in z_sb:
                z_sb[m] = kept("z%d" % m, [P, 2 * HALF], BF16, tag="codes_raw%d" % m)
            if m < ON_TENSOR:
                return z_sb[m][:].rearrange("p (h u d k) -> p h u d k", d=4, h=2, u=2)[:, h]
            return z_sb[m][:].rearrange("p (d h u k) -> p h u d k", d=4, h=2, u=2)[:, h]

        def add_y(m, h):
            target = z_target(m, h)
            if h == 0:
                order = dict(u=2, d=4)
                nc.vector.tensor_tensor(
                    out=target,
                    in0=mixed[m, h][:].rearrange("p (u d k) -> p u d k", **order),
                    in1=y_sb[m, h][:].rearrange("p (u d k) -> p u d k", **order),
                    op=ADD,
                )
            else:
                order = dict(u=2, d=4, s=2)
                nc.vector.tensor_tensor(
                    out=target.rearrange("p u d (j s) -> p u d j s", s=2),
                    in0=mixed[m, h][:].rearrange("p (d j u s) -> p u d j s", **order),
                    in1=y_sb[m, h][:].rearrange("p (d j u s) -> p u d j s", **order),
                    op=ADD,
                )
            give_bank("row%d%d" % (m, h))

        spilled = {}

        def spill_row(m, room=None):
            if room:
                spilled[m] = kept("spilled%d" % m, [P, HALF], F32, tag=room)
            else:
                spilled[m] = ringed("spilled%d" % m, [P, HALF], F32, "values", 3)
            nc.scalar.copy(out=spilled[m][:], in_=mixed[m, 0][:])
            give_bank("row%d0" % m)

        def add_y_on_pool(m):
            nc.gpsimd.tensor_tensor(
                out=z_target(m, 0),
                in0=spilled[m][:].rearrange("p (u d k) -> p u d k", u=2, d=4),
                in1=y_sb[m, 0][:].rearrange("p (u d k) -> p u d k", u=2, d=4),
                op=ADD,
            )

        def span(h):
            return (0, 2) if h is None else (h, 1)

        def move_z(m, h=None):
            first, count = span(h)
            if m not in z_moved:
                z_moved[m] = kept("z_moved%d" % m, [P, 2 * HALF], BF16, tag="codes_q%d" % m)
            part = count * P
            for d in range(4):
                room = z_moved[m][32 * d : 32 * (d + 1), first * HALF : (first + count) * HALF]
                start = first * HALF + d * part
                nc.sync.dma_start(out=room.rearrange("i (a w) -> i a w", a=4), in_=z_sb[m][:, start : start + part])

        def turn_z(m, h=None):
            first, count = span(h)
            z_blocks[m, h] = ringed("z_blocks%d_%d" % (m, first), [P, count * SHARE], F32, "sorted", 3)
            words = z_moved[m][:].bitcast(F32)[:, first * SHARE : (first + count) * SHARE]
            nc.vector.transpose(out=z_blocks[m, h][:], in_=words)

        def group_z(m, h=None):
            first, count = span(h)
            z_grouped[m, h] = kept("z_grouped%d_%d" % (m, first), [P, count, P, 4], BF16, tag="y%d%d" % (m, first))
            blocks = z_blocks[m, h][:].rearrange("p (a b h u i) -> p h a i b u", a=2, b=2, h=count, u=2)
            for k in range(count):
                words = z_grouped[m, h][:, k].bitcast(F32).rearrange("p (i a b) u -> p a i b u", a=2, b=2)
                nc.scalar.copy(out=words, in_=blocks[:, k])

        def turn_z_on_tensor(m):
            z_turned[m] = take_bank("turn_z%d" % m, [P, 2, 2, P])
            words = z_sb[m][:].bitcast(F32)
            for h in range(2):
                for u in range(2):
                    run = slice((2 * h + u) * P, (2 * h + u + 1) * P)
                    nc.tensor.transpose(z_turned[m][:, h, u, :], words[:, run], ident[:])

        def group_turned_z(m, h=None):
            first, count = span(h)
            z_grouped[m, h] = kept("z_grouped%d_%d" % (m, first), [P, count, P, 4], BF16, tag="y%d%d" % (m, first))
            nc.scalar.copy(
                out=z_grouped[m, h][:].bitcast(F32),
                in_=z_turned[m][:, first : first + count].rearrange("p h u n -> p h n u"),
            )
            if first + count == 2:
                give_bank("turn_z%d" % m)

        def quantize_z(m, h=None):
            first, count = span(h)
            cols = slice(first * P, (first + count) * P)
            nc.vector.quantize_mx(
                out=z_q[m][:, cols].bitcast(FP8X4),
                scales=z_s[m][:, cols],
                in_=z_grouped[m, h][:].rearrange("p h n t -> p (h n t)"),
            )

        h_sums, gates = {}, {}

        def chan_product(m, c0, width, passes=(0, 1)):
            if (m, c0) not in h_sums:
                h_sums[m, c0] = take_bank("chan%d_%d" % (m, c0), [P, width])
            for h in passes:
                nc.tensor.matmul_mx(
                    out=h_sums[m, c0][:],
                    lhsT=z_q[m][:, h * P : (h + 1) * P].bitcast(FP8X4),
                    lhsT_scale=z_s[m][:, h * P : (h + 1) * P],
                    rhs=chan_w[h][:, 2 * c0 : 2 * (c0 + width)].bitcast(FP4X4),
                    rhs_scale=chan_s[:, h, c0 : c0 + width],
                    start=(h == 0),
                    stop=(h == 1),
                )

        def gate_product(m, c0, width, passes=(0, 1)):
            chan_product(m, 2 * HALF + c0, width, passes)
            gates[m, c0] = ringed("gate%d_%d" % (m, c0), [P, width], F32, "gate%d" % width, 5 if width == HALF else 4)
            nc.scalar.activation(out=gates[m, c0][:], in_=h_sums[m, 2 * HALF + c0][:], func=ACT.Tanh)
            give_bank("chan%d_%d" % (m, 2 * HALF + c0))

        def new_result(m, c0, width):
            return ringed("result%d_%d" % (m, c0), [P, width], F32, "result%d" % width, 7 if width == HALF else 4)

        def store(m, c0, width, result):
            nc.sync.dma_start(out=out_v[m // 4, m % 4][:, c0 : c0 + width], in_=result[:])

        def store_product(m, c0, width=HALF):
            result = new_result(m, c0, width)
            nc.vector.tensor_tensor(out=result[:], in0=h_sums[m, c0][:], in1=gates[m, c0][:], op=MULT)
            give_bank("chan%d_%d" % (m, c0))
            store(m, c0, width, result)

        pool_values, pool_results = {}, {}

        def spill_values(m, c0):
            values = ringed("values%d_%d" % (m, c0), [P, HALF], F32, "values", 3)
            nc.scalar.copy(out=values[:], in_=h_sums[m, c0][:])
            give_bank("chan%d_%d" % (m, c0))
            pool_values[m, c0] = values

        def pool_product(m, c0, room):
            pool_results[m, c0] = kept("result%d_%d" % (m, c0), [P, HALF], F32, tag=room) if room else new_result(m, c0, HALF)
            nc.gpsimd.tensor_tensor(
                out=pool_results[m, c0][:], in0=pool_values[m, c0][:], in1=gates[m, c0][:], op=MULT
            )

        def store_pool_result(m, c0):
            store(m, c0, HALF, pool_results[m, c0])

        def half_products(m, n):
            for c0 in (2 * HALF + n * HALF, n * HALF):
                chan_product(m, c0, HALF, (0,))
            gate_product(m, n * HALF, HALF, (1,))
            chan_product(m, n * HALF, HALF, (1,))

        nc.gpsimd.memset(book_s[1][:, 0:2, :].rearrange("p g n -> p (g n)").bitcast(I32), 0)
        make_identity(nc, ident[:])
        clear(book_s[0][:].rearrange("p g n -> p (g n)"))
        clear(book_s[1][:, 2:4, :].rearrange("p g n -> p (g n)"))
        clear(row_s_raw[:])

        for first in (0, 2):
            for m in range(2):
                load_codes(m, first, 2)
        load_scales(book_s[0], book_scales[:, :, half_cols(0)])
        load_book(0, 0, 2)
        load_codes(2, 0, 2)
        load_codes(2, 2, 2)
        load_book(0, 2, 2)
        load_codes(3, 0, 2)
        load_codes(3, 2, 2)
        load_x(0, 0, 1)
        load_codes(4)
        load_gain()
        load_x(1, 0, 1)
        load_codes(5)
        load_x(2, 0, 1)
        load_codes(6)
        load_x(3, 0, 1)
        load_codes(7)
        load_x(4, 0)

        warm_up("warm0", 3, book_s[1])
        sort_codes(0, 0, 2)
        turn_codes(0, (0,))
        sort_codes(1, 0, 2)
        clear(row_s[:, 0])
        turn_codes(1, (0,))
        warm_up("warm2", 2, book_s[1])
        sort_codes(0, 2, 2)
        clear(row_s[:, 1])
        turn_codes(0, (1,))
        sort_codes(1, 2, 2)
        quantize_codes(0, (0,))
        quantize_codes(1, (0,))
        turn_codes(1, (1,))
        warm_up("warm4", 1, book_s[0])

        load_row_scales()
        load_book(1, 0, 2)
        load_scales(book_s[1], book_scales[:, :, half_cols(1)])
        load_book(1, 2, 2)
        load_x(6, 0)
        load_x(0, 1)
        load_row_words(0)
        load_x(2, 1)
        load_row_words(1)
        load_x(4, 1)
        load_x(6, 1)

        for m in range(2):
            book_product(m, 0, passes=(0, 1))
        clear(chan_s[:, 0])
        for b in range(2):
            sort_codes(2, 2 * b, 2)
        for m in range(2):
            quantize_codes(m, (1,))
        clear(chan_s[:, 1])
        turn_codes(2)
        for m in range(2):
            book_product(m, 0, passes=(2, 3))
        for b in range(2):
            sort_codes(3, 2 * b, 2)
        quantize_codes(2)
        turn_codes(3)
        add_x(0, 0)
        for m in range(2, TILES - 1):
            if m > 2:
                turn_codes(m + 1)
            if m > 2:
                scale_y(m - 2, 0)
            book_product(m, 0)
            if m + 2 < TILES:
                if m == 2:
                    sort_codes(4, 0, 2)
                    sort_codes(4, 2, 2)
                    widen_gain()
                    scale_y(0, 0)
                else:
                    sort_codes(m + 2, 0, SORTED_PASSES if m + 2 < TILES - 1 else ALL_SORTED)
            else:
                deal_row_scales()
            if m == 2:
                quantize_codes(m + 1)
                add_x(m - 1, 0)
            else:
                add_x(m - 1, 0)
                quantize_codes(m + 1)
        scale_y(5, 0)
        place_row_scales()
        for h in range(2):
            nc.sync.dma_start(out=chan_w[h][:].bitcast(I32), in_=chan_words[h].bitcast(I32))
        load_scales(chan_s, chan_scales)

        book_product(0, 1)
        add_x(6, 0)
        new_e_words(0, 0, 0, "pool_out")
        interleave_on_pool(0, 0, 0)
        new_e_words(0, 0, 1, "e_words01")
        interleave(nc.scalar.copy, 0, 0, SHARE, HALF)
        scale_y(6, 0)
        book_product(7, 0)
        add_x(0, 1)
        scale_y(0, 1)
        book_product(1, 1)
        add_x(7, 0)
        scale_y(7, 0)
        deal_row_words(0)
        quantize_e(0, 0, (1, 0))
        book_product(2, 1)
        add_x(1, 1)
        new_e_words(1, 0, 0, "pool_out")
        interleave_on_pool(1, 0, 0)
        new_e_words(1, 0, 1, "e_words11")
        interleave_on_pool(1, 0, 1, P)
        interleave(nc.scalar.copy, 1, 0, SHARE + P, HALF)
        scale_y(1, 1)
        for m in (3, 4):
            book_product(m, 1)
            add_x(m - 1, 1)
            scale_y(m - 1, 1)
        book_product(5, 1)
        add_x(4, 1)
        quantize_e(1, 0, (0, 1))
        new_e_words(0, 1, 0, "pool_out")
        interleave_on_pool(0, 1, 0)
        new_e_words(0, 1, 1, "e_words01")
        interleave(nc.scalar.copy, 0, 1, SHARE, HALF)
        scale_y(4, 1)
        book_product(6, 1)
        add_x(5, 1)
        scale_y(5, 1)
        for c0 in (0, SHARE):
            book_product(7, 1, c0, SHARE)
        add_x(6, 1)
        scale_y(6, 1)
        for c0 in (0, SHARE):
            add_x(7, 1, c0, SHARE)
        quantize_e(0, 1, (1, 0))
        for c0 in (0, SHARE):
            scale_y(7, 1, c0, SHARE)
        for m in range(4):
            row_product(m, 0)
        for share in range(2):
            new_e_words(1, 1, share, "e_words1%d" % share)
        interleave(nc.vector.tensor_copy, 1, 1, 0, SHARE)
        interleave(nc.vector.tensor_copy, 1, 1, SHARE, SHARE + P)
        interleave(nc.scalar.copy, 1, 1, SHARE + P, HALF)
        quantize_e(1, 1, (0, 1))
        spill_row(3)
        add_y_on_pool(3)
        deal_row_words_on_scalar(1)
        for g in range(2):
            for m in range(4):
                row_product(m, 1, (g,))
        add_y(0, 0)
        add_y(1, 0)
        add_y(0, 1)
        add_y(1, 1)
        row_product(4, 0)
        turn_z_on_tensor(0)
        turn_z_on_tensor(1)
        add_y(2, 0)
        for h in range(2):
            group_turned_z(0, h)
        add_y(2, 1)
        group_turned_z(1)
        move_z(2)
        for h in range(2):
            quantize_z(0, h)
        row_product(4, 1)
        row_product(5, 0)
        row_product(5, 1)
        add_y(3, 1)
        move_z(3)
        quantize_z(1)
        spill_row(4, "y01")
        add_y_on_pool(4)
        add_y(4, 1)
        move_z(4)
        half_products(0, 0)
        spill_values(0, 0)
        pool_product(0, 0, None)
        add_y(5, 0)
        add_y(5, 1)
        move_z(5)
        half_products(0, 1)
        spill_values(0, HALF)
        turn_z(2)
        for g in range(2):
            for h in range(2):
                row_product(6, h, (g,))
        group_z(2)
        add_y(6, 0)
        add_y(6, 1)
        move_z(6)
        store_pool_result(0, 0)
        half_products(1, 0)
        turn_z(3)
        quantize_z(2)
        pool_product(0, HALF, "y20")
        spill_values(1, 0)
        for g in range(2):
            for h in range(2):
                row_product(7, h, (g,))
        group_z(3)
        add_y(7, 0)
        add_y(7, 1)
        move_z(7)
        half_products(1, 1)
        turn_z(4)
        quantize_z(3)
        pool_product(1, 0, "y30")
        store_pool_result(0, HALF)
        store_product(1, HALF)
        half_products(2, 0)
        group_z(4)
        turn_z(5)
        half_products(2, 1)
        store_product(2, 0)
        quantize_z(4)
        store_pool_result(1, 0)
        group_z(5)
        turn_z(6)
        half_products(3, 0)
        store_product(2, HALF)
        quantize_z(5)
        half_products(3, 1)
        group_z(6)
        store_product(3, 0)
        turn_z(7)
        half_products(4, 0)
        store_product(3, HALF)
        quantize_z(6)
        half_products(4, 1)
        group_z(7)
        store_product(4, 0)
        half_products(5, 0)
        store_product(4, HALF)
        quantize_z(7)
        half_products(5, 1)
        store_product(5, 0)
        pending = (5, HALF, HALF)
        pieces = [(6, 0, HALF), (6, HALF, HALF)] + [(TILES - 1, c0, SHARE) for c0 in range(0, 2 * HALF, SHARE)]
        gate_product(*pieces[0])
        for i, piece in enumerate(pieces):
            if i + 1 < len(pieces):
                gate_product(*pieces[i + 1])
            chan_product(*piece)
            if i == 0:
                store_product(*pending)
            store_product(*piece)
